import numpy as np
import ml_dtypes


def mxq(x, axis, fmt="e4m3"):
    dtype, down = {"e4m3": (ml_dtypes.float8_e4m3fn, 7), "e5m2": (ml_dtypes.float8_e5m2, 14)}[fmt]
    v = np.moveaxis(np.asarray(x, np.float32).astype(ml_dtypes.bfloat16).astype(np.float64), axis, -1)
    blocks = v.reshape(v.shape[:-1] + (-1, 32))
    amax = np.abs(blocks).max(-1, keepdims=True)
    byte = np.maximum(np.where(amax > 0, np.frexp(amax)[1] - 1 + 127, 0) - down, 1)
    scale = np.exp2(byte - 127.0)
    codes = (blocks / scale).astype(np.float32).astype(dtype).astype(np.float64)
    return np.moveaxis((codes * scale).reshape(v.shape), -1, axis)


WIDE = False


def mx_kscale(k):
    if not WIDE:
        return np.ones(k)
    levels = np.array([10, -10, 5, -5, 0])
    if k % 512:
        return np.exp2(np.random.permutation(np.resize(levels, k // 32))).repeat(32)
    a = np.empty((k // 512, 16))
    for p in range(k // 512):
        a[p, :8] = np.random.permutation(np.resize(levels, 8))
        for g in range(8):
            far = levels[np.abs(levels - a[p, g]) >= 10]
            a[p, g + 8] = far[np.random.randint(len(far))]
    return np.exp2(a.ravel()).repeat(32)


BF16 = ml_dtypes.bfloat16


def bf(x):
    return np.asarray(x, np.float32).astype(BF16)


def f64(x):
    return np.asarray(x).astype(np.float64)


E2M1 = np.array([0.0, 0.5, 1.0, 1.5, 2.0, 3.0, 4.0, 6.0, -0.0, -0.5, -1.0, -1.5, -2.0, -3.0, -4.0, -6.0])


def pack_weight(w, fmt):
    k, n = w.shape
    w = f64(bf(w)).reshape(k // 32, 32, n)
    amax = np.abs(w).max(1)
    if fmt == "e4m3":
        byte = np.frexp(amax)[1] - 1 + 127 - 7
    else:
        mant, ex = np.frexp(amax / 6.0)
        byte = np.where(mant > 0.5, ex, ex - 1) + 127
    byte = np.clip(np.where(amax > 0, byte, 1), 1, 254)
    scaled = (w * np.exp2(127.0 - byte)[:, None, :]).reshape(k, n).astype(np.float32)
    by_word = np.ascontiguousarray(scaled.reshape(k // 512, 128, 4, n).transpose(0, 1, 3, 2))
    if fmt == "e4m3":
        words = by_word.astype(ml_dtypes.float8_e4m3fn).view(np.uint8)
    else:
        c = by_word.astype(ml_dtypes.float4_e2m1fn).view(np.uint8) & 0xF
        words = c[..., 0::2] | (c[..., 1::2] << 4)
    return np.ascontiguousarray(words), np.ascontiguousarray(byte.astype(np.uint8).reshape(k // 512, 16, n))


def unpack_weight(words, scales, fmt):
    g, p, n, _ = words.shape
    if fmt == "e4m3":
        vals = np.ascontiguousarray(words).view(ml_dtypes.float8_e4m3fn).astype(np.float64)
    else:
        nib = np.empty((g, p, n, 4), np.uint8)
        nib[..., 0::2] = words & 0xF
        nib[..., 1::2] = words >> 4
        vals = E2M1[nib]
    vals = vals * np.repeat(np.exp2(scales.astype(np.float64) - 127.0), 8, axis=1)[..., None]
    return vals.transpose(0, 1, 3, 2).reshape(g * 512, n)
def pack4(w):
    words, scales = pack_weight(w, "e2m1")
    return words.reshape(words.shape[0], 128, -1), scales


def unpack4(words, scales):
    return unpack_weight(words.reshape(words.shape[0], 128, -1, 2), scales, "e2m1")


def planes(Y):
    n, m = Y.shape
    b = f64(bf(Y)).reshape(n // 32, 32, m)
    amax = np.abs(b).max(1)
    byte = np.clip(np.where(amax > 0, np.frexp(amax)[1] - 1 + 127 - 7, 1), 1, 254)
    codes = (b * np.exp2(127.0 - byte)[:, None, :]).reshape(n, m).astype(np.float32).astype(ml_dtypes.float8_e4m3fn).view(np.uint8)
    words = codes.reshape(n // 512, 128, 4, m).transpose(0, 1, 3, 2)
    return np.ascontiguousarray(words), np.ascontiguousarray(byte.astype(np.uint8).reshape(n // 512, 16, m))


N, M, D, V = 512, 512, 1024, 1024

LEARNING_RATE = 1.0 / 256.0


def sigmoid(v):
    return 1.0 / (1.0 + np.exp(-v))


def train_logit_grad(a, y, c):
    return (sigmoid(a) - y) * c[None, :]


def test_logit_grad(b, e):
    return sigmoid(b) * e[None, :]


def setup_inputs():
    s, u = mx_kscale(D), mx_kscale(V)
    h = bf(np.random.standard_normal((N, D)) * 0.5 * s)
    t = bf(np.random.standard_normal((M, D)) * 0.5 * s)
    words, scales = pack4(np.random.standard_normal((D, V)) * (3.0 / np.sqrt(D)) / s[:, None])
    return {"h": h,
            "t": t,
            "w_words": words,
            "w_scales": scales,
            "y": bf(np.random.uniform(0.0, 1.0, (N, V))),
            "c": bf((1.0 + 0.1 * np.random.standard_normal(V)) * u),
            "e": bf(np.random.standard_normal(V) / u),
            "r": bf(np.random.uniform(0.5, 1.5, D) / (s * s))}


def core(h, t, w_words, w_scales, y, c, e, r):
    wq = unpack4(w_words, w_scales)
    tq = mxq(f64(t), 1, "e4m3")
    a = mxq(f64(h), 1, "e4m3") @ wq
    b = tq @ wq
    ga = train_logit_grad(a, f64(y), f64(c))
    gb = test_logit_grad(b, f64(e))
    logit_gram = mxq(ga, 1, "e4m3") @ mxq(gb, 1, "e4m3").T
    hr = f64(h) * f64(r)[None, :]
    feat_gram = mxq(hr, 1, "e4m3") @ tq.T
    infl = feat_gram * logit_gram * LEARNING_RATE
    return infl


def reference(h, t, w_words, w_scales, y, c, e, r):
    R_out = core(h, t, w_words, w_scales, y, c, e, r)
    words, scales = planes(R_out.T)
    return R_out, words, scales

@@ -1,0 +1,266 @@
+from contextlib import ExitStack
+
+import concourse.mybir as mybir
+from concourse.masks import make_identity
+
+N, M, D, V = 512, 512, 1024, 1024
+FLOPS = 2 * (N * D * V + M * D * V + N * M * V + N * M * D)
+
+F32 = mybir.dt.float32
+BF16 = mybir.dt.bfloat16
+I32 = mybir.dt.int32
+U32 = mybir.dt.uint32
+U8 = mybir.dt.uint8
+FP8X4 = mybir.dt.float8_e4m3fn_x4
+FP4X4 = mybir.dt.float4_e2m1fn_x4
+ALU = mybir.AluOpType
+ACT = mybir.ActivationFunctionType
+
+P = 128
+LEARNING_RATE = 1.0 / 256.0
+LOADS = "h0 s t0 w t1 r c y0 h1 y1 h2 y2 h3 y3".split()
+ORDER = """th0 tt00 eh0 qh0 tt01 wp et00 wsp ma01 et01 hr0 qt0 tce sa01 qr0 th1 tt10 d01 eh1 tt11 et10 th2 hr1 ece et11 ma00 qh1 qr1 eh2 ma11 qt1 sa00 ma10 qh2 sa11 hr2 mb02 sa10 d00 mb00 sb02 qr2 td01 d10 d31 td00 d11 th3 sb00 xc00 td10 d20 td11 xc01 mb01 d30 xc11 eh3 mb03 qa01 xc10 sb01 mb12 hr3 sb03 mb11 qh3 sb12 mb10 qa00 qr3 sb11 mb13 qa10 qa11 xe00 d21 ma21 sb13 ma31 xe01 sb10 ma30 sa21 ma20 xe11 sa30 fg0 sa31 td21 qb0 cf0 fg1 sa20 xe10 fg2 cf1 td20 xc21 cf2 qb1 td31 xc20 td30 qa21 xc31 lg1 qa20 qa31 fg3 xc30 lg2 r1 cf3 lg0 qa30 r2 cr1 lg3 r0 cr2 tr1 cr3 cr0 tr2 er1 tr3 r3 tr0 er2 er3 qo2 er0 qo1 qo3 qo0""".split()
+DIRECT_BF16 = [3]
+Y_ON_PE = [2,3]
+E_ON_ACT = []
+WARM = 0
+
+
+def tile_tracinonevsallheadinfluence_x2_kernel(tc, h, t, w_words, w_scales, y, c, e, r, out_0, out_1, out_2):
+    nc = tc.nc
+    with ExitStack() as ctx:
+        keep = ctx.enter_context(tc.tile_pool(name="keep", bufs=1))
+        psum = ctx.enter_context(tc.psum_pool(name="psum", bufs=1))
+        ctx.enter_context(tc.manual_schedule())
+
+        def sb(name, shape, dtype):
+            return keep.tile(shape, dtype, name=name, align_bytes=64)
+
+        def many(name, count, shape, dtype):
+            return [sb("%s%d" % (name, k), shape, dtype) for k in range(count)]
+
+        banks = {}
+
+        def new_bank(step):
+            banks[step] = psum.tile([P, 512], F32, name="bank_" + step, tag="bank%d" % (len(banks) % 8))
+            return banks[step]
+
+        h_raw = many("h_raw", 4, [P, D], BF16)
+        y_raw = many("y_raw", 4, [P, V], BF16)
+        t_raw = many("t_raw", 2, [P, 4, 512], BF16)
+        w_raw = sb("w_raw", [P, 2, 2 * V], U8)
+        w_perm = sb("w_perm", [P, 2, 2 * V], U8)
+        ws_raw = sb("ws_raw", [P, 2, V], U8)
+        ws_perm = sb("ws_perm", [P, 2, V], U8)
+        ce_rows = sb("ce_rows", [P, 256], BF16)
+        ce = sb("ce", [P, 2, 8], F32)
+        r_sb = sb("r_sb", [P, 2, 4], BF16)
+        ident32 = sb("ident32", [P, P], F32)
+        ident16 = sb("ident16", [P, P], BF16)
+        table_warm = sb("table_warm", [P, 1], F32)
+
+        h_k = many("h_k", 4, [P, 1024], BF16)
+        hr_k = many("hr_k", 4, [P, 1024], BF16)
+        t_k = many("t_k", 2, [P, 2048], BF16)
+        ga_k = many("ga_k", 4, [P, 1024], BF16)
+        gb_k = many("gb_k", 2, [P, 2048], BF16)
+        out_k = many("out_k", 4, [P, 512], BF16)
+        h_q, h_s = many("h_q", 4, [P, 256], U32), many("h_s", 4, [P, 256], U8)
+        hr_q, hr_s = many("hr_q", 4, [P, 256], U32), many("hr_s", 4, [P, 256], U8)
+        ga_q, ga_s = many("ga_q", 4, [P, 256], U32), many("ga_s", 4, [P, 256], U8)
+        t_q, t_s = many("t_q", 2, [P, 512], U32), many("t_s", 2, [P, 512], U8)
+        gb_q, gb_s = many("gb_q", 2, [P, 512], U32), many("gb_s", 2, [P, 512], U8)
+        out_q, out_s = sb("out_q", [P, 512], U32), sb("out_s", [P, 512], U8)
+        sig_a = many("sig_a", 8, [P, 512], F32)
+        diff = many("diff", 8, [P, 512], F32)
+        sig_b = many("sig_b", 2, [P, 4, 512], F32)
+        gb_s16 = many("gb_s16", 2, [P, 4, 512], BF16)
+        feat = many("feat", 4, [P, 512], F32)
+        res = many("res", 4, [P, 512], F32)
+        res16 = many("res16", 4, [P, 512], BF16)
+
+        nc.vector.memset(ws_raw[:].bitcast(I32), 0)
+        make_identity(nc, ident32[:])
+        nc.gpsimd.memset(ce_rows[:], 0.0)
+        make_identity(nc, ident16[:])
+
+        def load(name):
+            k = int(name[1]) if len(name) > 1 else 0
+            if name[0] == "h":
+                nc.sync.dma_start(out=h_raw[k][:], in_=h[k * P : (k + 1) * P, :])
+            elif name[0] == "y":
+                nc.sync.dma_start(out=y_raw[k][:], in_=y[k * P : (k + 1) * P, :])
+            elif name[0] == "t":
+                nc.sync.dma_start(out=t_raw[k][:], in_=t[:, k * 512 : (k + 1) * 512].rearrange("(b p) k -> p b k", p=P))
+            elif name[0] == "w":
+                nc.sync.dma_start(out=w_raw[:].bitcast(I32), in_=w_words.bitcast(I32).rearrange("g p n -> p g n"))
+            elif name[0] == "r":
+                nc.sync.dma_start(out=r_sb[:], in_=r.rearrange("(g p s) -> p g s", g=2, s=4))
+            elif name[0] == "c":
+                for row, vec in ((0, c), (4, e)):
+                    nc.sync.dma_start(out=ce_rows[row : row + 4, :].rearrange("s (a i) -> s a i", i=8),
+                                      in_=vec.rearrange("(a s i) -> s a i", s=4, i=8))
+            else:
+                for quad in range(4):
+                    nc.scalar.dma_start(out=ws_raw[32 * quad : 32 * quad + 4, :, :].bitcast(I32),
+                                        in_=w_scales[:, 4 * quad : 4 * quad + 4, :].bitcast(I32).rearrange("g r n -> r g n"))
+
+        for name in LOADS:
+            load(name)
+        nc.scalar.activation(out=table_warm[:], in_=ident32[:, 0:1], func=ACT.Sigmoid)
+
+        def quantize(codes, scales, values):
+            nc.vector.quantize_mx(out=codes.bitcast(FP8X4), scales=scales, in_=values)
+
+        def two_passes(step, lhs, lhs_scale, rhs, rhs_scale):
+            bank = new_bank(step)
+            for g in range(2):
+                nc.tensor.matmul_mx(out=bank[:], lhsT=lhs(g), lhsT_scale=lhs_scale(g), rhs=rhs(g), rhs_scale=rhs_scale(g),
+                                    start=(g == 0), stop=(g == 1))
+
+        def cols(k, width):
+            return slice(k * width, (k + 1) * width)
+
+        if WARM > 0:
+            warm16 = sb("warm16", [P, 512], BF16)
+            warm_q, warm_s = sb("warm_q", [P, P], U32), sb("warm_s", [P, P], U8)
+            nc.vector.memset(warm16[:], 1.0)
+            quantize(warm_q[:], warm_s[:], warm16[:])
+            bank = new_bank("warm")
+            for k in range(WARM):
+                nc.tensor.matmul_mx(out=bank[:, cols(k % 4, P)], lhsT=warm_q[:].bitcast(FP8X4), lhsT_scale=warm_s[:],
+                                    rhs=warm_q[:].bitcast(FP8X4), rhs_scale=warm_s[:], start=True, stop=True)
+
+        def run(step):
+            kind = "".join([ch for ch in step if ch not in "0123456789"])
+            ix = [int(ch) for ch in step if ch in "0123456789"]
+            a = ix[0] if len(ix) > 0 else 0
+            b = ix[1] if len(ix) > 1 else 0
+            if kind == "wp":
+                for g in range(2):
+                    for v in range(2):
+                        nc.vector.tensor_copy(
+                            out=w_perm[:, g, :].bitcast(I32)[:, cols(v, 256)].rearrange("p (s q i) -> p q s i", s=4, i=4),
+                            in_=w_raw[:, g, :].bitcast(I32)[:, cols(v, 256)].rearrange("p (q s i) -> p q s i", s=4, i=4))
+            elif kind == "wsp":
+                for g in range(2):
+                    for v in range(2):
+                        nc.vector.tensor_copy(
+                            out=ws_perm[:, g, :].bitcast(I32)[:, cols(v, 128)].rearrange("p (s q i) -> p s q i", s=4, i=2),
+                            in_=ws_raw[:, g, :].bitcast(I32)[:, cols(v, 128)].rearrange("p (q s i) -> p s q i", s=4, i=2))
+            elif kind == "tce":
+                bank = new_bank(step)
+                for v in range(2):
+                    nc.tensor.transpose(bank[:].bitcast(BF16)[:, cols(v, P)], ce_rows[:, cols(v, P)], ident16[:])
+            elif kind == "ece":
+                nc.scalar.copy(out=ce[:], in_=banks["tce"][:].bitcast(BF16)[:, 0:256].rearrange("p (v j) -> p v j", v=2)[:, :, 0:8])
+            elif kind == "th":
+                bank = new_bank(step)
+                words = h_raw[a][:].bitcast(F32)
+                for g in range(2):
+                    for u in range(2):
+                        nc.tensor.transpose(bank[:, cols(2 * g + u, P)], words[:, 256 * g + u : 256 * (g + 1) : 2], ident32[:])
+            elif kind == "eh":
+                nc.scalar.copy(out=h_k[a][:].bitcast(F32).rearrange("p (g n u) -> p g n u", g=2, u=2),
+                               in_=banks["th%d" % a][:].rearrange("p (g u n) -> p g n u", g=2, u=2))
+            elif kind == "qh":
+                quantize(h_q[a][:], h_s[a][:], h_k[a][:])
+            elif kind == "hr":
+                nc.vector.tensor_tensor(out=hr_k[a][:].rearrange("p (g n s) -> p g n s", g=2, s=4),
+                                        in0=h_k[a][:].rearrange("p (g n s) -> p g n s", g=2, s=4),
+                                        in1=r_sb[:].unsqueeze(2).to_broadcast([P, 2, P, 4]), op=ALU.mult)
+            elif kind == "qr":
+                quantize(hr_q[a][:], hr_s[a][:], hr_k[a][:])
+            elif kind == "tt":
+                bank = new_bank(step)
+                for blk in range(2):
+                    words = t_raw[a][:, 2 * b + blk, :].bitcast(F32)
+                    for u in range(2):
+                        nc.tensor.transpose(bank[:, cols(2 * blk + u, P)], words[:, u:256:2], ident32[:])
+            elif kind == "et":
+                nc.scalar.copy(out=t_k[a][:, cols(b, 1024)].bitcast(F32).rearrange("p (k m u) -> p k m u", k=2, u=2),
+                               in_=banks["tt%d%d" % (a, b)][:].rearrange("p (k u m) -> p k m u", k=2, u=2))
+            elif kind == "qt":
+                quantize(t_q[a][:], t_s[a][:], t_k[a][:])
+            elif kind == "ma":
+                two_passes(step, lambda g: h_q[a][:, cols(g, P)].bitcast(FP8X4), lambda g: h_s[a][:, cols(g, P)],
+                           lambda g: w_raw[:, g, cols(b, 1024)].bitcast(FP4X4), lambda g: ws_raw[:, g, cols(b, 512)])
+            elif kind == "sa":
+                nc.scalar.activation(out=sig_a[2 * a + b][:].rearrange("p (s q i) -> p s q i", s=4, i=8),
+                                     in_=banks["ma%d%d" % (a, b)][:].rearrange("p (q s i) -> p s q i", s=4, i=8), func=ACT.Sigmoid)
+            elif kind == "d" and a in Y_ON_PE:
+                nc.scalar.activation(out=diff[2 * a + b][:].rearrange("p (s q i) -> p s q i", s=4, i=8),
+                                     in_=y_raw[a][:, cols(b, 512)].rearrange("p (q s i) -> p s q i", s=4, i=8), func=ACT.Copy, scale=-1.0)
+            elif kind == "td" and a in Y_ON_PE:
+                bank = new_bank(step)
+                for k, src in enumerate((diff[2 * a + b], sig_a[2 * a + b])):
+                    for s in range(4):
+                        nc.tensor.matmul(bank[:, cols(s, P)], lhsT=src[:, cols(s, P)], rhs=ident32[:], is_transpose=True,
+                                         start=(k == 0 and s == 0), stop=(k == 1 and s == 3))
+            elif kind == "se":
+                nc.scalar.activation(out=gb_s16[a][:, b, :], in_=sig_b[a][:, b, :], func=ACT.Copy, scale=ce[:, a, 4 + b : 5 + b])
+            elif kind == "xe" and a in E_ON_ACT:
+                nc.vector.tensor_copy(out=gb_k[a][:, cols(b, 1024)].rearrange("p (m i s) -> p m s i", s=4, i=4),
+                                      in_=gb_s16[a][:, :, cols(b, 256)].rearrange("p s (m i) -> p m s i", i=4))
+            elif kind == "d":
+                nc.vector.tensor_tensor(out=diff[2 * a + b][:].rearrange("p (s q i) -> p s q i", s=4, i=8),
+                                        in0=sig_a[2 * a + b][:].rearrange("p (s q i) -> p s q i", s=4, i=8),
+                                        in1=y_raw[a][:, cols(b, 512)].rearrange("p (q s i) -> p s q i", s=4, i=8), op=ALU.subtract)
+            elif kind == "td":
+                bank = new_bank(step)
+                for s in range(4):
+                    nc.tensor.transpose(bank[:, cols(s, P)], diff[2 * a + b][:, cols(s, P)], ident32[:])
+            elif kind == "xc":
+                nc.vector.tensor_tensor(out=ga_k[a][:, cols(b, 512)].rearrange("p (n s) -> p n s", s=4),
+                                        in0=banks["td%d%d" % (a, b)][:].rearrange("p (s n) -> p n s", s=4),
+                                        in1=ce[:, b, 0:4].unsqueeze(1).to_broadcast([P, P, 4]), op=ALU.mult)
+            elif kind == "qa":
+                quantize(ga_q[a][:, cols(b, P)], ga_s[a][:, cols(b, P)], ga_k[a][:, cols(b, 512)])
+            elif kind == "mb":
+                two_passes(step, lambda g: w_perm[:, g, cols(4 * a + b, 256)].bitcast(FP4X4), lambda g: ws_perm[:, g, cols(4 * a + b, P)],
+                           lambda g: t_q[g][:].bitcast(FP8X4), lambda g: t_s[g][:])
+            elif kind == "sb":
+                nc.scalar.activation(out=sig_b[a][:, b, :], in_=banks["mb%d%d" % (a, b)][:], func=ACT.Sigmoid)
+            elif kind == "xe":
+                nc.vector.tensor_tensor(out=gb_k[a][:, cols(b, 1024)].rearrange("p (m i s) -> p m s i", s=4, i=4),
+                                        in0=sig_b[a][:, :, cols(b, 256)].rearrange("p s (m i) -> p m s i", i=4),
+                                        in1=ce[:, a, 4:8].unsqueeze(1).unsqueeze(3).to_broadcast([P, 64, 4, 4]), op=ALU.mult)
+            elif kind == "qb":
+                quantize(gb_q[a][:], gb_s[a][:], gb_k[a][:])
+            elif kind == "fg":
+                two_passes(step, lambda g: hr_q[a][:, cols(g, P)].bitcast(FP8X4), lambda g: hr_s[a][:, cols(g, P)],
+                           lambda g: t_q[g][:].bitcast(FP8X4), lambda g: t_s[g][:])
+            elif kind == "cf":
+                nc.scalar.activation(out=feat[a][:], in_=banks["fg%d" % a][:], func=ACT.Copy, scale=LEARNING_RATE)
+            elif kind == "lg":
+                two_passes(step, lambda g: ga_q[a][:, cols(g, P)].bitcast(FP8X4), lambda g: ga_s[a][:, cols(g, P)],
+                           lambda g: gb_q[g][:].bitcast(FP8X4), lambda g: gb_s[g][:])
+            elif kind == "r":
+                nc.vector.tensor_tensor(out=res[a][:], in0=banks["lg%d" % a][:], in1=feat[a][:], op=ALU.mult)
+                nc.sync.dma_start(out=out_0[cols(a, P), :], in_=res[a][:])
+            elif kind == "cr":
+                pairs_out = res16[a][:].rearrange("p (u k j) -> p u k j", u=2, j=2)
+                if a in DIRECT_BF16:
+                    nc.vector.tensor_tensor(out=pairs_out, in0=banks["lg%d" % a][:].rearrange("p (k u j) -> p u k j", u=2, j=2),
+                                            in1=feat[a][:].rearrange("p (k u j) -> p u k j", u=2, j=2), op=ALU.mult)
+                else:
+                    nc.scalar.copy(out=pairs_out, in_=res[a][:].rearrange("p (k u j) -> p u k j", u=2, j=2))
+            elif kind == "tr":
+                bank = new_bank(step)
+                for u in range(2):
+                    nc.tensor.transpose(bank[:, cols(u, P)], res16[a][:].bitcast(F32)[:, cols(u, P)], ident32[:])
+            elif kind == "er":
+                nc.scalar.copy(out=out_k[a][:].bitcast(F32).rearrange("p (n u) -> p n u", u=2),
+                               in_=banks["tr%d" % a][:, 0:256].rearrange("p (u n) -> p n u", u=2))
+            elif kind == "qo":
+                quantize(out_q[:, cols(a, P)], out_s[:, cols(a, P)], out_k[a][:])
+                nc.sync.dma_start(out=out_1[0].rearrange("p n s -> p (n s)").bitcast(I32)[:, cols(a, P)],
+                                  in_=out_q[:, cols(a, P)].bitcast(I32))
+            else:
+                raise ValueError(step)
+
+        for step in ORDER:
+            run(step)
+        for quad in range(4):
+            queue = nc.sync if quad < 2 else nc.scalar
+            queue.dma_start(out=out_2[0, 4 * quad : 4 * quad + 4, :].bitcast(I32), in_=out_s[32 * quad : 32 * quad + 4, :].bitcast(I32))

@@ -18,12 +18,12 @@ ACT = mybir.ActivationFunctionType
 
 P = 128
 LEARNING_RATE = 1.0 / 256.0
-LOADS = "h0 s t0 w t1 r c y0 h1 y1 h2 y2 h3 y3".split()
-ORDER = """th0 tt00 eh0 qh0 tt01 wp et00 wsp ma01 et01 hr0 qt0 tce sa01 qr0 th1 tt10 d01 eh1 tt11 et10 th2 hr1 ece et11 ma00 qh1 qr1 eh2 ma11 qt1 sa00 ma10 qh2 sa11 hr2 mb02 sa10 d00 mb00 sb02 qr2 td01 d10 d31 td00 d11 th3 sb00 xc00 td10 d20 td11 xc01 mb01 d30 xc11 eh3 mb03 qa01 xc10 sb01 mb12 hr3 sb03 mb11 qh3 sb12 mb10 qa00 qr3 sb11 mb13 qa10 qa11 xe00 d21 ma21 sb13 ma31 xe01 sb10 ma30 sa21 ma20 xe11 sa30 fg0 sa31 td21 qb0 cf0 fg1 sa20 xe10 fg2 cf1 td20 xc21 cf2 qb1 td31 xc20 td30 qa21 xc31 lg1 qa20 qa31 fg3 xc30 lg2 r1 cf3 lg0 qa30 r2 cr1 lg3 r0 cr2 tr1 cr3 cr0 tr2 er1 tr3 r3 tr0 er2 er3 qo2 er0 qo1 qo3 qo0""".split()
+LOADS = "h0 s t0 w h1 t1 r c y0 h2 y1 h3 y2 y3".split()
+ORDER = """th0 wm0 eh0 tt01 qh0 wsp tt00 wp et01 ma01 et00 th1 sa01 qt0 tce ma00 eh1 hr0 tt10 ece d01 sa00 tt11 qh1 et10 qr0 th2 d00 et11 ma11 hr1 eh2 th3 qt1 sa11 td01 qr1 d30 ma10 qh2 hr2 eh3 ma20 xc01 sa10 mb13 qh3 sa20 hr3 mb10 sb13 qa01 mb12 d11 sb10 mb11 qr3 sb12 qr2 mb00 d10 sb11 mb01 d20 sb00 td11 xe10 sb01 td10 td00 se00 td20 xc11 ma21 d21 xc20 se01 ma30 xc10 sa21 mb03 qa20 xe11 sa30 mb02 sb03 ma31 xc00 sb02 td30 qa10 se03 qb1 td21 se02 qa11 xc30 fg0 d31 xe01 sa31 fg3 xe00 cf0 fg1 xc21 td31 cf1 qb0 fg2 cf3 qa21 xc31 lg1 cf2 qa00 lg2 qa30 qa31 r1 lg0 r2 lg30 so1 cr1 lg31 r0 cr2 so2 tr1 cr31 cr0 cr30 so0 tr2 er1 tr30 r3 tr31 tr0 er2 er3 qo1 qo2 so3 er0 qo3 qo0 sw2 sw1 ss3 sw3 ss2 ss1 sw0 ss0""".split()
 DIRECT_BF16 = [3]
-Y_ON_PE = [2,3]
-E_ON_ACT = []
-WARM = 0
+Y_ON_PE = [5,6,7]
+E_ON_ACT = [0]
+WARM = 10
 
 
 def tile_tracinonevsallheadinfluence_x2_kernel(tc, h, t, w_words, w_scales, y, c, e, r, out_0, out_1, out_2):
@@ -64,7 +64,7 @@ def tile_tracinonevsallheadinfluence_x2_kernel(tc, h, t, w_words, w_scales, y, c
         t_k = many("t_k", 2, [P, 2048], BF16)
         ga_k = many("ga_k", 4, [P, 1024], BF16)
         gb_k = many("gb_k", 2, [P, 2048], BF16)
-        out_k = many("out_k", 4, [P, 512], BF16)
+        out_k = sb("out_k", [P, 2048], BF16)
         h_q, h_s = many("h_q", 4, [P, 256], U32), many("h_s", 4, [P, 256], U8)
         hr_q, hr_s = many("hr_q", 4, [P, 256], U32), many("hr_s", 4, [P, 256], U8)
         ga_q, ga_s = many("ga_q", 4, [P, 256], U32), many("ga_s", 4, [P, 256], U8)
@@ -79,7 +79,10 @@ def tile_tracinonevsallheadinfluence_x2_kernel(tc, h, t, w_words, w_scales, y, c
         res = many("res", 4, [P, 512], F32)
         res16 = many("res16", 4, [P, 512], BF16)
 
-        nc.vector.memset(ws_raw[:].bitcast(I32), 0)
+        warm16 = sb("warm16", [P, 512], BF16)
+        warm_q, warm_s = sb("warm_q", [P, P], U32), sb("warm_s", [P, P], U8)
+        nc.vector.memset(warm16[:].bitcast(I32), 0x3F803F80)
+        nc.gpsimd.memset(ws_raw[:].bitcast(I32), 0)
         make_identity(nc, ident32[:])
         nc.gpsimd.memset(ce_rows[:], 0.0)
         make_identity(nc, ident16[:])
@@ -121,22 +124,23 @@ def tile_tracinonevsallheadinfluence_x2_kernel(tc, h, t, w_words, w_scales, y, c
         def cols(k, width):
             return slice(k * width, (k + 1) * width)
 
-        if WARM > 0:
-            warm16 = sb("warm16", [P, 512], BF16)
-            warm_q, warm_s = sb("warm_q", [P, P], U32), sb("warm_s", [P, P], U8)
-            nc.vector.memset(warm16[:], 1.0)
-            quantize(warm_q[:], warm_s[:], warm16[:])
-            bank = new_bank("warm")
-            for k in range(WARM):
-                nc.tensor.matmul_mx(out=bank[:, cols(k % 4, P)], lhsT=warm_q[:].bitcast(FP8X4), lhsT_scale=warm_s[:],
+        def warm_up(count):
+            for k in range(count):
+                nc.tensor.matmul_mx(out=banks["warm"][:, cols(k % 4, P)], lhsT=warm_q[:].bitcast(FP8X4), lhsT_scale=warm_s[:],
                                     rhs=warm_q[:].bitcast(FP8X4), rhs_scale=warm_s[:], start=True, stop=True)
+
+        quantize(warm_q[:], warm_s[:], warm16[:])
+        new_bank("warm")
+        warm_up(WARM)
 
         def run(step):
             kind = "".join([ch for ch in step if ch not in "0123456789"])
             ix = [int(ch) for ch in step if ch in "0123456789"]
             a = ix[0] if len(ix) > 0 else 0
             b = ix[1] if len(ix) > 1 else 0
-            if kind == "wp":
+            if kind == "wm":
+                warm_up(8)
+            elif kind == "wp":
                 for g in range(2):
                     for v in range(2):
                         nc.vector.tensor_copy(
@@ -188,10 +192,10 @@ def tile_tracinonevsallheadinfluence_x2_kernel(tc, h, t, w_words, w_scales, y, c
             elif kind == "sa":
                 nc.scalar.activation(out=sig_a[2 * a + b][:].rearrange("p (s q i) -> p s q i", s=4, i=8),
                                      in_=banks["ma%d%d" % (a, b)][:].rearrange("p (q s i) -> p s q i", s=4, i=8), func=ACT.Sigmoid)
-            elif kind == "d" and a in Y_ON_PE:
+            elif kind == "d" and 2 * a + b in Y_ON_PE:
                 nc.scalar.activation(out=diff[2 * a + b][:].rearrange("p (s q i) -> p s q i", s=4, i=8),
                                      in_=y_raw[a][:, cols(b, 512)].rearrange("p (q s i) -> p s q i", s=4, i=8), func=ACT.Copy, scale=-1.0)
-            elif kind == "td" and a in Y_ON_PE:
+            elif kind == "td" and 2 * a + b in Y_ON_PE:
                 bank = new_bank(step)
                 for k, src in enumerate((diff[2 * a + b], sig_a[2 * a + b])):
                     for s in range(4):
@@ -222,9 +226,9 @@ def tile_tracinonevsallheadinfluence_x2_kernel(tc, h, t, w_words, w_scales, y, c
             elif kind == "sb":
                 nc.scalar.activation(out=sig_b[a][:, b, :], in_=banks["mb%d%d" % (a, b)][:], func=ACT.Sigmoid)
             elif kind == "xe":
-                nc.vector.tensor_tensor(out=gb_k[a][:, cols(b, 1024)].rearrange("p (m i s) -> p m s i", s=4, i=4),
-                                        in0=sig_b[a][:, :, cols(b, 256)].rearrange("p s (m i) -> p m s i", i=4),
-                                        in1=ce[:, a, 4:8].unsqueeze(1).unsqueeze(3).to_broadcast([P, 64, 4, 4]), op=ALU.mult)
+                nc.vector.tensor_tensor(out=gb_k[a][:, cols(b, 1024)].rearrange("p (m i s) -> p m s i", s=4, i=2),
+                                        in0=sig_b[a][:, :, cols(b, 256)].rearrange("p s (m i) -> p m s i", i=2),
+                                        in1=ce[:, a, 4:8].unsqueeze(1).unsqueeze(3).to_broadcast([P, 128, 4, 2]), op=ALU.mult)
             elif kind == "qb":
                 quantize(gb_q[a][:], gb_s[a][:], gb_k[a][:])
             elif kind == "fg":
@@ -233,34 +237,42 @@ def tile_tracinonevsallheadinfluence_x2_kernel(tc, h, t, w_words, w_scales, y, c
             elif kind == "cf":
                 nc.scalar.activation(out=feat[a][:], in_=banks["fg%d" % a][:], func=ACT.Copy, scale=LEARNING_RATE)
             elif kind == "lg":
-                two_passes(step, lambda g: ga_q[a][:, cols(g, P)].bitcast(FP8X4), lambda g: ga_s[a][:, cols(g, P)],
-                           lambda g: gb_q[g][:].bitcast(FP8X4), lambda g: gb_s[g][:])
+                for g in ix[1:] or [0, 1]:
+                    if g == 0:
+                        new_bank("lg%d" % a)
+                    nc.tensor.matmul_mx(out=banks["lg%d" % a][:], lhsT=ga_q[a][:, cols(g, P)].bitcast(FP8X4), lhsT_scale=ga_s[a][:, cols(g, P)],
+                                        rhs=gb_q[g][:].bitcast(FP8X4), rhs_scale=gb_s[g][:], start=(g == 0), stop=(g == 1))
             elif kind == "r":
                 nc.vector.tensor_tensor(out=res[a][:], in0=banks["lg%d" % a][:], in1=feat[a][:], op=ALU.mult)
+            elif kind == "so":
                 nc.sync.dma_start(out=out_0[cols(a, P), :], in_=res[a][:])
             elif kind == "cr":
                 pairs_out = res16[a][:].rearrange("p (u k j) -> p u k j", u=2, j=2)
                 if a in DIRECT_BF16:
-                    nc.vector.tensor_tensor(out=pairs_out, in0=banks["lg%d" % a][:].rearrange("p (k u j) -> p u k j", u=2, j=2),
-                                            in1=feat[a][:].rearrange("p (k u j) -> p u k j", u=2, j=2), op=ALU.mult)
+                    nc.vector.tensor_tensor(out=pairs_out[:, b], in0=banks["lg%d" % a][:].rearrange("p (k u j) -> p u k j", u=2, j=2)[:, b],
+                                            in1=feat[a][:].rearrange("p (k u j) -> p u k j", u=2, j=2)[:, b], op=ALU.mult)
                 else:
                     nc.scalar.copy(out=pairs_out, in_=res[a][:].rearrange("p (k u j) -> p u k j", u=2, j=2))
             elif kind == "tr":
-                bank = new_bank(step)
-                for u in range(2):
-                    nc.tensor.transpose(bank[:, cols(u, P)], res16[a][:].bitcast(F32)[:, cols(u, P)], ident32[:])
+                if ("tr%d" % a) not in banks:
+                    new_bank("tr%d" % a)
+                for u in ix[1:] or [0, 1]:
+                    nc.tensor.transpose(banks["tr%d" % a][:, cols(u, P)], res16[a][:].bitcast(F32)[:, cols(u, P)], ident32[:])
             elif kind == "er":
-                nc.scalar.copy(out=out_k[a][:].bitcast(F32).rearrange("p (n u) -> p n u", u=2),
+                nc.scalar.copy(out=out_k[:, cols(a, 512)].bitcast(F32).rearrange("p (n u) -> p n u", u=2),
                                in_=banks["tr%d" % a][:, 0:256].rearrange("p (u n) -> p n u", u=2))
             elif kind == "qo":
-                quantize(out_q[:, cols(a, P)], out_s[:, cols(a, P)], out_k[a][:])
-                nc.sync.dma_start(out=out_1[0].rearrange("p n s -> p (n s)").bitcast(I32)[:, cols(a, P)],
-                                  in_=out_q[:, cols(a, P)].bitcast(I32))
+                lo, hi = ix[0], ix[-1] + 1
+                quantize(out_q[:, lo * P : hi * P], out_s[:, lo * P : hi * P], out_k[:, lo * 512 : hi * 512])
+            elif kind == "sw":
+                lo, hi = ix[0], ix[-1] + 1
+                nc.sync.dma_start(out=out_1[0].rearrange("p n s -> p (n s)").bitcast(I32)[:, lo * P : hi * P],
+                                  in_=out_q[:, lo * P : hi * P].bitcast(I32))
+            elif kind == "ss":
+                queue = nc.sync if a < 2 else nc.scalar
+                queue.dma_start(out=out_2[0, 4 * a : 4 * a + 4, :].bitcast(I32), in_=out_s[32 * a : 32 * a + 4, :].bitcast(I32))
             else:
                 raise ValueError(step)
 
         for step in ORDER:
             run(step)
-        for quad in range(4):
-            queue = nc.sync if quad < 2 else nc.scalar
-            queue.dma_start(out=out_2[0, 4 * quad : 4 * quad + 4, :].bitcast(I32), in_=out_s[32 * quad : 32 * quad + 4, :].bitcast(I32))

@@ -18,12 +18,14 @@ ACT = mybir.ActivationFunctionType
 
 P = 128
 LEARNING_RATE = 1.0 / 256.0
-LOADS = "h0 s t0 w h1 t1 r c y0 h2 y1 h3 y2 y3".split()
-ORDER = """th0 wm0 eh0 tt01 qh0 wsp tt00 wp et01 ma01 et00 th1 sa01 qt0 tce ma00 eh1 hr0 tt10 ece d01 sa00 tt11 qh1 et10 qr0 th2 d00 et11 ma11 hr1 eh2 th3 qt1 sa11 td01 qr1 d30 ma10 qh2 hr2 eh3 ma20 xc01 sa10 mb13 qh3 sa20 hr3 mb10 sb13 qa01 mb12 d11 sb10 mb11 qr3 sb12 qr2 mb00 d10 sb11 mb01 d20 sb00 td11 xe10 sb01 td10 td00 se00 td20 xc11 ma21 d21 xc20 se01 ma30 xc10 sa21 mb03 qa20 xe11 sa30 mb02 sb03 ma31 xc00 sb02 td30 qa10 se03 qb1 td21 se02 qa11 xc30 fg0 d31 xe01 sa31 fg3 xe00 cf0 fg1 xc21 td31 cf1 qb0 fg2 cf3 qa21 xc31 lg1 cf2 qa00 lg2 qa30 qa31 r1 lg0 r2 lg30 so1 cr1 lg31 r0 cr2 so2 tr1 cr31 cr0 cr30 so0 tr2 er1 tr30 r3 tr31 tr0 er2 er3 qo1 qo2 so3 er0 qo3 qo0 sw2 sw1 ss3 sw3 ss2 ss1 sw0 ss0""".split()
+LOADS = "h0 s t0 w r h1 t1 c y0 h2 y1 h3 y2 y3".split()
+ORDER = """th0 wm0 eh0 tt00 qh0 tt01 et00 wp wsp th1 et01 ma01 eh1 hr0 ma00 qt0 sa01 tt10 sa00 hr1 tt11 qh1 et10 th2 tce qr0 et11 d0 ma11 eh2 ece th3 qt1 d1 td01 td00 qr1 mb13 xc01 eh3 mb11 xc00 sa11 mb10 hr23 sb13 mb12 sb11 mb01 qa0 sb10 qh23 td11 sb12 qr23 mb02 sb01 xc11 mb00 sb02 xe1 mb03 sb00 ma21 sb03 ma30 sa21 ma20 xe0 ma10 sa30 fg0 d2 ma31 fg1 sa10 qb1 td21 sa20 qb0 td10 d3 xc21 td20 xc10 cf0 lg0 xc20 sa31 td30 r0 cf1 td31 qa1 so0 cr0 xc30 fg2 xc31 lg1 cf2 qa2 fg3 qa3 lg2 r1 cf3 lg3 r2 so1 cr1 tr0 cr3 so2 cr2 tr1 r3 er01 tr3 tr2 er3 qo01 so3 er2 qo3 sw01 qo2 sw3 ss2 ss1 sw2 ss3 ss0""".split()
 DIRECT_BF16 = [3]
-Y_ON_PE = [5,6,7]
-E_ON_ACT = [0]
-WARM = 10
+Y_ON_PE = [1,2,3]
+Y_ON_VECTOR = []
+H_GROUPS = ["0","1","23"]
+OUT_GROUPS = ["01","2","3"]
+WARM = 13
 
 
 def tile_tracinonevsallheadinfluence_x2_kernel(tc, h, t, w_words, w_scales, y, c, e, r, out_0, out_1, out_2):
@@ -59,29 +61,32 @@ def tile_tracinonevsallheadinfluence_x2_kernel(tc, h, t, w_words, w_scales, y, c
         ident16 = sb("ident16", [P, P], BF16)
         table_warm = sb("table_warm", [P, 1], F32)
 
-        h_k = many("h_k", 4, [P, 1024], BF16)
-        hr_k = many("hr_k", 4, [P, 1024], BF16)
+        group_of = {int(ch): grp for grp in H_GROUPS for ch in grp}
+        out_group_of = {int(ch): grp for grp in OUT_GROUPS for ch in grp}
+        h_k = {grp: sb("h_k" + grp, [P, 2, 512 * len(grp)], BF16) for grp in H_GROUPS}
+        hr_k = {grp: sb("hr_k" + grp, [P, 2, 512 * len(grp)], BF16) for grp in H_GROUPS}
+        h_q = {grp: sb("h_q" + grp, [P, 2, P * len(grp)], U32) for grp in H_GROUPS}
+        h_s = {grp: sb("h_s" + grp, [P, 2, P * len(grp)], U8) for grp in H_GROUPS}
+        hr_q = {grp: sb("hr_q" + grp, [P, 2, P * len(grp)], U32) for grp in H_GROUPS}
+        hr_s = {grp: sb("hr_s" + grp, [P, 2, P * len(grp)], U8) for grp in H_GROUPS}
         t_k = many("t_k", 2, [P, 2048], BF16)
         ga_k = many("ga_k", 4, [P, 1024], BF16)
         gb_k = many("gb_k", 2, [P, 2048], BF16)
         out_k = sb("out_k", [P, 2048], BF16)
-        h_q, h_s = many("h_q", 4, [P, 256], U32), many("h_s", 4, [P, 256], U8)
-        hr_q, hr_s = many("hr_q", 4, [P, 256], U32), many("hr_s", 4, [P, 256], U8)
         ga_q, ga_s = many("ga_q", 4, [P, 256], U32), many("ga_s", 4, [P, 256], U8)
         t_q, t_s = many("t_q", 2, [P, 512], U32), many("t_s", 2, [P, 512], U8)
         gb_q, gb_s = many("gb_q", 2, [P, 512], U32), many("gb_s", 2, [P, 512], U8)
         out_q, out_s = sb("out_q", [P, 512], U32), sb("out_s", [P, 512], U8)
-        sig_a = many("sig_a", 8, [P, 512], F32)
-        diff = many("diff", 8, [P, 512], F32)
+        sig_a = many("sig_a", 4, [P, 4, 2, P], F32)
+        diff = many("diff", 4, [P, 4, 2, P], F32)
         sig_b = many("sig_b", 2, [P, 4, 512], F32)
-        gb_s16 = many("gb_s16", 2, [P, 4, 512], BF16)
         feat = many("feat", 4, [P, 512], F32)
         res = many("res", 4, [P, 512], F32)
         res16 = many("res16", 4, [P, 512], BF16)
 
         warm16 = sb("warm16", [P, 512], BF16)
         warm_q, warm_s = sb("warm_q", [P, P], U32), sb("warm_s", [P, P], U8)
-        nc.vector.memset(warm16[:].bitcast(I32), 0x3F803F80)
+        nc.gpsimd.memset(warm16[:].bitcast(I32), 0x3F803F80)
         nc.gpsimd.memset(ws_raw[:].bitcast(I32), 0)
         make_identity(nc, ident32[:])
         nc.gpsimd.memset(ce_rows[:], 0.0)
@@ -110,7 +115,7 @@ def tile_tracinonevsallheadinfluence_x2_kernel(tc, h, t, w_words, w_scales, y, c
 
         for name in LOADS:
             load(name)
-        nc.scalar.activation(out=table_warm[:], in_=ident32[:, 0:1], func=ACT.Sigmoid)
+        nc.scalar.activation(out=table_warm[:], in_=warm16[:, 0:1], func=ACT.Sigmoid)
 
         def quantize(codes, scales, values):
             nc.vector.quantize_mx(out=codes.bitcast(FP8X4), scales=scales, in_=values)
@@ -124,6 +129,13 @@ def tile_tracinonevsallheadinfluence_x2_kernel(tc, h, t, w_words, w_scales, y, c
         def cols(k, width):
             return slice(k * width, (k + 1) * width)
 
+        def flat(tile):
+            return tile[:].rearrange("p g n -> p (g n)")
+
+        def rows_of(tiles, n):
+            own = group_of[n]
+            return lambda g: tiles[own][:, g, cols(own.index(str(n)), P)]
+
         def warm_up(count):
             for k in range(count):
                 nc.tensor.matmul_mx(out=banks["warm"][:, cols(k % 4, P)], lhsT=warm_q[:].bitcast(FP8X4), lhsT_scale=warm_s[:],
@@ -136,22 +148,19 @@ def tile_tracinonevsallheadinfluence_x2_kernel(tc, h, t, w_words, w_scales, y, c
         def run(step):
             kind = "".join([ch for ch in step if ch not in "0123456789"])
             ix = [int(ch) for ch in step if ch in "0123456789"]
+            grp = "".join([str(k) for k in ix])
             a = ix[0] if len(ix) > 0 else 0
             b = ix[1] if len(ix) > 1 else 0
             if kind == "wm":
                 warm_up(8)
             elif kind == "wp":
-                for g in range(2):
-                    for v in range(2):
-                        nc.vector.tensor_copy(
-                            out=w_perm[:, g, :].bitcast(I32)[:, cols(v, 256)].rearrange("p (s q i) -> p q s i", s=4, i=4),
-                            in_=w_raw[:, g, :].bitcast(I32)[:, cols(v, 256)].rearrange("p (q s i) -> p q s i", s=4, i=4))
+                nc.vector.tensor_copy(
+                    out=w_perm[:].bitcast(I32).rearrange("p g (v s q i) -> p (g v) q s i", v=2, s=4, i=4),
+                    in_=w_raw[:].bitcast(I32).rearrange("p g (v q s i) -> p (g v) q s i", v=2, s=4, i=4))
             elif kind == "wsp":
-                for g in range(2):
-                    for v in range(2):
-                        nc.vector.tensor_copy(
-                            out=ws_perm[:, g, :].bitcast(I32)[:, cols(v, 128)].rearrange("p (s q i) -> p s q i", s=4, i=2),
-                            in_=ws_raw[:, g, :].bitcast(I32)[:, cols(v, 128)].rearrange("p (q s i) -> p s q i", s=4, i=2))
+                nc.vector.tensor_copy(
+                    out=ws_perm[:].bitcast(I32).rearrange("p g (v s q i) -> p (g v) s q i", v=2, s=4, i=2),
+                    in_=ws_raw[:].bitcast(I32).rearrange("p g (v q s i) -> p (g v) s q i", v=2, s=4, i=2))
             elif kind == "tce":
                 bank = new_bank(step)
                 for v in range(2):
@@ -165,16 +174,17 @@ def tile_tracinonevsallheadinfluence_x2_kernel(tc, h, t, w_words, w_scales, y, c
                     for u in range(2):
                         nc.tensor.transpose(bank[:, cols(2 * g + u, P)], words[:, 256 * g + u : 256 * (g + 1) : 2], ident32[:])
             elif kind == "eh":
-                nc.scalar.copy(out=h_k[a][:].bitcast(F32).rearrange("p (g n u) -> p g n u", g=2, u=2),
+                own = group_of[a]
+                nc.scalar.copy(out=h_k[own][:, :, cols(own.index(str(a)), 512)].bitcast(F32).rearrange("p g (n u) -> p g n u", u=2),
                                in_=banks["th%d" % a][:].rearrange("p (g u n) -> p g n u", g=2, u=2))
             elif kind == "qh":
-                quantize(h_q[a][:], h_s[a][:], h_k[a][:])
+                quantize(flat(h_q[grp]), flat(h_s[grp]), flat(h_k[grp]))
             elif kind == "hr":
-                nc.vector.tensor_tensor(out=hr_k[a][:].rearrange("p (g n s) -> p g n s", g=2, s=4),
-                                        in0=h_k[a][:].rearrange("p (g n s) -> p g n s", g=2, s=4),
-                                        in1=r_sb[:].unsqueeze(2).to_broadcast([P, 2, P, 4]), op=ALU.mult)
+                nc.vector.tensor_tensor(out=hr_k[grp][:].rearrange("p g (n s) -> p g n s", s=4),
+                                        in0=h_k[grp][:].rearrange("p g (n s) -> p g n s", s=4),
+                                        in1=r_sb[:].unsqueeze(2).to_broadcast([P, 2, P * len(grp), 4]), op=ALU.mult)
             elif kind == "qr":
-                quantize(hr_q[a][:], hr_s[a][:], hr_k[a][:])
+                quantize(flat(hr_q[grp]), flat(hr_s[grp]), flat(hr_k[grp]))
             elif kind == "tt":
                 bank = new_bank(step)
                 for blk in range(2):
@@ -187,52 +197,50 @@ def tile_tracinonevsallheadinfluence_x2_kernel(tc, h, t, w_words, w_scales, y, c
             elif kind == "qt":
                 quantize(t_q[a][:], t_s[a][:], t_k[a][:])
             elif kind == "ma":
-                two_passes(step, lambda g: h_q[a][:, cols(g, P)].bitcast(FP8X4), lambda g: h_s[a][:, cols(g, P)],
+                two_passes(step, lambda g: rows_of(h_q, a)(g).bitcast(FP8X4), rows_of(h_s, a),
                            lambda g: w_raw[:, g, cols(b, 1024)].bitcast(FP4X4), lambda g: ws_raw[:, g, cols(b, 512)])
             elif kind == "sa":
-                nc.scalar.activation(out=sig_a[2 * a + b][:].rearrange("p (s q i) -> p s q i", s=4, i=8),
+                nc.scalar.activation(out=sig_a[a][:, :, b, :].rearrange("p s (q i) -> p s q i", i=8),
                                      in_=banks["ma%d%d" % (a, b)][:].rearrange("p (q s i) -> p s q i", s=4, i=8), func=ACT.Sigmoid)
-            elif kind == "d" and 2 * a + b in Y_ON_PE:
-                nc.scalar.activation(out=diff[2 * a + b][:].rearrange("p (s q i) -> p s q i", s=4, i=8),
-                                     in_=y_raw[a][:, cols(b, 512)].rearrange("p (q s i) -> p s q i", s=4, i=8), func=ACT.Copy, scale=-1.0)
-            elif kind == "td" and 2 * a + b in Y_ON_PE:
-                bank = new_bank(step)
-                for k, src in enumerate((diff[2 * a + b], sig_a[2 * a + b])):
-                    for s in range(4):
-                        nc.tensor.matmul(bank[:, cols(s, P)], lhsT=src[:, cols(s, P)], rhs=ident32[:], is_transpose=True,
-                                         start=(k == 0 and s == 0), stop=(k == 1 and s == 3))
-            elif kind == "se":
-                nc.scalar.activation(out=gb_s16[a][:, b, :], in_=sig_b[a][:, b, :], func=ACT.Copy, scale=ce[:, a, 4 + b : 5 + b])
-            elif kind == "xe" and a in E_ON_ACT:
-                nc.vector.tensor_copy(out=gb_k[a][:, cols(b, 1024)].rearrange("p (m i s) -> p m s i", s=4, i=4),
-                                      in_=gb_s16[a][:, :, cols(b, 256)].rearrange("p s (m i) -> p m s i", i=4))
             elif kind == "d":
-                nc.vector.tensor_tensor(out=diff[2 * a + b][:].rearrange("p (s q i) -> p s q i", s=4, i=8),
-                                        in0=sig_a[2 * a + b][:].rearrange("p (s q i) -> p s q i", s=4, i=8),
-                                        in1=y_raw[a][:, cols(b, 512)].rearrange("p (q s i) -> p s q i", s=4, i=8), op=ALU.subtract)
+                lo, hi = (b, b + 1) if len(ix) > 1 else (0, 2)
+                y_view = y_raw[a][:, lo * 512 : hi * 512].rearrange("p (w s i) -> p s w i", s=4, i=8)
+                d_view = diff[a][:, :, lo:hi, :].rearrange("p s v (q i) -> p s (v q) i", i=8)
+                if a not in Y_ON_PE:
+                    nc.vector.tensor_tensor(out=d_view, in0=sig_a[a][:, :, lo:hi, :].rearrange("p s v (q i) -> p s (v q) i", i=8),
+                                            in1=y_view, op=ALU.subtract)
+                elif a in Y_ON_VECTOR:
+                    nc.vector.tensor_scalar(out=d_view, in0=y_view, scalar1=-1.0, scalar2=None, op0=ALU.mult)
+                else:
+                    nc.scalar.activation(out=d_view, in_=y_view, func=ACT.Copy, scale=-1.0)
             elif kind == "td":
                 bank = new_bank(step)
-                for s in range(4):
-                    nc.tensor.transpose(bank[:, cols(s, P)], diff[2 * a + b][:, cols(s, P)], ident32[:])
+                terms = (diff[a], sig_a[a]) if a in Y_ON_PE else (diff[a],)
+                for k, src in enumerate(terms):
+                    for s in range(4):
+                        nc.tensor.matmul(bank[:, cols(s, P)], lhsT=src[:, s, b, :], rhs=ident32[:], is_transpose=True,
+                                         start=(k == 0 and s == 0), stop=(k == len(terms) - 1 and s == 3))
             elif kind == "xc":
                 nc.vector.tensor_tensor(out=ga_k[a][:, cols(b, 512)].rearrange("p (n s) -> p n s", s=4),
                                         in0=banks["td%d%d" % (a, b)][:].rearrange("p (s n) -> p n s", s=4),
                                         in1=ce[:, b, 0:4].unsqueeze(1).to_broadcast([P, P, 4]), op=ALU.mult)
             elif kind == "qa":
-                quantize(ga_q[a][:, cols(b, P)], ga_s[a][:, cols(b, P)], ga_k[a][:, cols(b, 512)])
+                lo, hi = (b, b + 1) if len(ix) > 1 else (0, 2)
+                quantize(ga_q[a][:, lo * P : hi * P], ga_s[a][:, lo * P : hi * P], ga_k[a][:, lo * 512 : hi * 512])
             elif kind == "mb":
                 two_passes(step, lambda g: w_perm[:, g, cols(4 * a + b, 256)].bitcast(FP4X4), lambda g: ws_perm[:, g, cols(4 * a + b, P)],
                            lambda g: t_q[g][:].bitcast(FP8X4), lambda g: t_s[g][:])
             elif kind == "sb":
                 nc.scalar.activation(out=sig_b[a][:, b, :], in_=banks["mb%d%d" % (a, b)][:], func=ACT.Sigmoid)
             elif kind == "xe":
-                nc.vector.tensor_tensor(out=gb_k[a][:, cols(b, 1024)].rearrange("p (m i s) -> p m s i", s=4, i=2),
-                                        in0=sig_b[a][:, :, cols(b, 256)].rearrange("p s (m i) -> p m s i", i=2),
-                                        in1=ce[:, a, 4:8].unsqueeze(1).unsqueeze(3).to_broadcast([P, 128, 4, 2]), op=ALU.mult)
+                lo, hi = (b, b + 1) if len(ix) > 1 else (0, 2)
+                nc.vector.tensor_tensor(out=gb_k[a][:, lo * 1024 : hi * 1024].rearrange("p (m i s) -> p m s i", s=4, i=2),
+                                        in0=sig_b[a][:, :, lo * 256 : hi * 256].rearrange("p s (m i) -> p m s i", i=2),
+                                        in1=ce[:, a, 4:8].unsqueeze(1).unsqueeze(3).to_broadcast([P, 128 * (hi - lo), 4, 2]), op=ALU.mult)
             elif kind == "qb":
                 quantize(gb_q[a][:], gb_s[a][:], gb_k[a][:])
             elif kind == "fg":
-                two_passes(step, lambda g: hr_q[a][:, cols(g, P)].bitcast(FP8X4), lambda g: hr_s[a][:, cols(g, P)],
+                two_passes(step, lambda g: rows_of(hr_q, a)(g).bitcast(FP8X4), rows_of(hr_s, a),
                            lambda g: t_q[g][:].bitcast(FP8X4), lambda g: t_s[g][:])
             elif kind == "cf":
                 nc.scalar.activation(out=feat[a][:], in_=banks["fg%d" % a][:], func=ACT.Copy, scale=LEARNING_RATE)
@@ -249,18 +257,20 @@ def tile_tracinonevsallheadinfluence_x2_kernel(tc, h, t, w_words, w_scales, y, c
             elif kind == "cr":
                 pairs_out = res16[a][:].rearrange("p (u k j) -> p u k j", u=2, j=2)
                 if a in DIRECT_BF16:
-                    nc.vector.tensor_tensor(out=pairs_out[:, b], in0=banks["lg%d" % a][:].rearrange("p (k u j) -> p u k j", u=2, j=2)[:, b],
-                                            in1=feat[a][:].rearrange("p (k u j) -> p u k j", u=2, j=2)[:, b], op=ALU.mult)
+                    nc.vector.tensor_tensor(out=pairs_out, in0=banks["lg%d" % a][:].rearrange("p (k u j) -> p u k j", u=2, j=2),
+                                            in1=feat[a][:].rearrange("p (k u j) -> p u k j", u=2, j=2), op=ALU.mult)
                 else:
                     nc.scalar.copy(out=pairs_out, in_=res[a][:].rearrange("p (k u j) -> p u k j", u=2, j=2))
             elif kind == "tr":
-                if ("tr%d" % a) not in banks:
-                    new_bank("tr%d" % a)
-                for u in ix[1:] or [0, 1]:
-                    nc.tensor.transpose(banks["tr%d" % a][:, cols(u, P)], res16[a][:].bitcast(F32)[:, cols(u, P)], ident32[:])
+                own = out_group_of[a]
+                if ("tr" + own) not in banks:
+                    new_bank("tr" + own)
+                for u in range(2):
+                    nc.tensor.transpose(banks["tr" + own][:, cols(2 * own.index(str(a)) + u, P)], res16[a][:].bitcast(F32)[:, cols(u, P)], ident32[:])
             elif kind == "er":
-                nc.scalar.copy(out=out_k[:, cols(a, 512)].bitcast(F32).rearrange("p (n u) -> p n u", u=2),
-                               in_=banks["tr%d" % a][:, 0:256].rearrange("p (u n) -> p n u", u=2))
+                lo, hi = ix[0], ix[-1] + 1
+                nc.scalar.copy(out=out_k[:, lo * 512 : hi * 512].bitcast(F32).rearrange("p (j n u) -> p j n u", n=P, u=2),
+                               in_=banks["tr" + grp][:, 0 : 256 * (hi - lo)].rearrange("p (j u n) -> p j n u", n=P, u=2))
             elif kind == "qo":
                 lo, hi = ix[0], ix[-1] + 1
                 quantize(out_q[:, lo * P : hi * P], out_s[:, lo * P : hi * P], out_k[:, lo * 512 : hi * 512])

@@ -18,13 +18,16 @@ ACT = mybir.ActivationFunctionType
 
 P = 128
 LEARNING_RATE = 1.0 / 256.0
-LOADS = "h0 s t0 w r h1 t1 c y0 h2 y1 h3 y2 y3".split()
-ORDER = """th0 wm0 eh0 tt00 qh0 tt01 et00 wp wsp th1 et01 ma01 eh1 hr0 ma00 qt0 sa01 tt10 sa00 hr1 tt11 qh1 et10 th2 tce qr0 et11 d0 ma11 eh2 ece th3 qt1 d1 td01 td00 qr1 mb13 xc01 eh3 mb11 xc00 sa11 mb10 hr23 sb13 mb12 sb11 mb01 qa0 sb10 qh23 td11 sb12 qr23 mb02 sb01 xc11 mb00 sb02 xe1 mb03 sb00 ma21 sb03 ma30 sa21 ma20 xe0 ma10 sa30 fg0 d2 ma31 fg1 sa10 qb1 td21 sa20 qb0 td10 d3 xc21 td20 xc10 cf0 lg0 xc20 sa31 td30 r0 cf1 td31 qa1 so0 cr0 xc30 fg2 xc31 lg1 cf2 qa2 fg3 qa3 lg2 r1 cf3 lg3 r2 so1 cr1 tr0 cr3 so2 cr2 tr1 r3 er01 tr3 tr2 er3 qo01 so3 er2 qo3 sw01 qo2 sw3 ss2 ss1 sw2 ss3 ss0""".split()
+LOADS = "h0 s t0 w h1 t1 r y0 h2 h3 c y1 y2 y3".split()
+ORDER = """th0 pt0 wm0 eh0 tt00 qh0 tt01 p1 ma00 et00 wsp wp et01 th1 pt1 sa00 ma01 eh1 qt0 tt11 hr0 sa01 tt10 qh1 th2 et11 d0 th3 et10 tce eh2 ma11 qt1 eh3 hr1 ma10 ece sa11 qr0 mb12 qr1 sa10 qh23 mb13 sb12 mb10 hr23 sb13 mb11 sb10 d1 ma21 sb11 mb01 d2 qr23 mb00 xe1 mb03 sa21 mb02 sb01 td01 sb00 td00 sb03 td11 xc01 td10 se01 qb1 td21 sb02 ma20 se00 xc21 se02 ma31 xc00 se03 ma30 xc10 sa31 fg1 qa0 xc11 sa20 fg0 xe0 d3 fg3 td20 sa30 qa1 qb0 td31 cf1 xc20 cf3 td30 xc31 cf0 lg0 qa2 xc30 fg2 r0 lg1 qa3 cf2 lg2 so0 cr0 r1 lg3 r2 tr0 so1 cr1 cr3 cr2 so2 tr1 r3 tr3 er01 tr2 er3 so3 qo01 er2 qo3 sw01 qo2 sw3 ss3 ss1 ss2 ss0 sw2""".split()
 DIRECT_BF16 = [3]
-Y_ON_PE = [1,2,3]
+Y_ON_PE = [2,3]
 Y_ON_VECTOR = []
 H_GROUPS = ["0","1","23"]
 OUT_GROUPS = ["01","2","3"]
+E_ON_ACT = [0]
+H_PRE = [1]
+T_PRE = [0,1]
 WARM = 13
 
 
@@ -80,6 +83,9 @@ def tile_tracinonevsallheadinfluence_x2_kernel(tc, h, t, w_words, w_scales, y, c
         sig_a = many("sig_a", 4, [P, 4, 2, P], F32)
         diff = many("diff", 4, [P, 4, 2, P], F32)
         sig_b = many("sig_b", 2, [P, 4, 512], F32)
+        gb_s16 = sb("gb_s16", [P, 4, 512], BF16)
+        h_pre = {k: sb("h_pre%d" % k, [P, 2, 2, P], F32) for k in H_PRE}
+        t_pre = {k: sb("t_pre%d" % k, [P, 4, 2, P], F32) for k in T_PRE}
         feat = many("feat", 4, [P, 512], F32)
         res = many("res", 4, [P, 512], F32)
         res16 = many("res16", 4, [P, 512], BF16)
@@ -167,12 +173,16 @@ def tile_tracinonevsallheadinfluence_x2_kernel(tc, h, t, w_words, w_scales, y, c
                     nc.tensor.transpose(bank[:].bitcast(BF16)[:, cols(v, P)], ce_rows[:, cols(v, P)], ident16[:])
             elif kind == "ece":
                 nc.scalar.copy(out=ce[:], in_=banks["tce"][:].bitcast(BF16)[:, 0:256].rearrange("p (v j) -> p v j", v=2)[:, :, 0:8])
+            elif kind == "p":
+                nc.vector.tensor_copy(out=h_pre[a][:], in_=h_raw[a][:].bitcast(F32).rearrange("p (g k u) -> p g u k", g=2, u=2))
+            elif kind == "pt":
+                nc.vector.tensor_copy(out=t_pre[a][:], in_=t_raw[a][:].bitcast(F32).rearrange("p b (k u) -> p b u k", u=2))
             elif kind == "th":
                 bank = new_bank(step)
                 words = h_raw[a][:].bitcast(F32)
                 for g in range(2):
                     for u in range(2):
-                        nc.tensor.transpose(bank[:, cols(2 * g + u, P)], words[:, 256 * g + u : 256 * (g + 1) : 2], ident32[:])
+                        nc.tensor.transpose(bank[:, cols(2 * g + u, P)], h_pre[a][:, g, u, :] if a in H_PRE else words[:, 256 * g + u : 256 * (g + 1) : 2], ident32[:])
             elif kind == "eh":
                 own = group_of[a]
                 nc.scalar.copy(out=h_k[own][:, :, cols(own.index(str(a)), 512)].bitcast(F32).rearrange("p g (n u) -> p g n u", u=2),
@@ -190,7 +200,7 @@ def tile_tracinonevsallheadinfluence_x2_kernel(tc, h, t, w_words, w_scales, y, c
                 for blk in range(2):
                     words = t_raw[a][:, 2 * b + blk, :].bitcast(F32)
                     for u in range(2):
-                        nc.tensor.transpose(bank[:, cols(2 * blk + u, P)], words[:, u:256:2], ident32[:])
+                        nc.tensor.transpose(bank[:, cols(2 * blk + u, P)], t_pre[a][:, 2 * b + blk, u, :] if a in T_PRE else words[:, u:256:2], ident32[:])
             elif kind == "et":
                 nc.scalar.copy(out=t_k[a][:, cols(b, 1024)].bitcast(F32).rearrange("p (k m u) -> p k m u", k=2, u=2),
                                in_=banks["tt%d%d" % (a, b)][:].rearrange("p (k u m) -> p k m u", k=2, u=2))
@@ -232,6 +242,11 @@ def tile_tracinonevsallheadinfluence_x2_kernel(tc, h, t, w_words, w_scales, y, c
                            lambda g: t_q[g][:].bitcast(FP8X4), lambda g: t_s[g][:])
             elif kind == "sb":
                 nc.scalar.activation(out=sig_b[a][:, b, :], in_=banks["mb%d%d" % (a, b)][:], func=ACT.Sigmoid)
+            elif kind == "se":
+                nc.scalar.activation(out=gb_s16[:, b, :], in_=sig_b[a][:, b, :], func=ACT.Copy, scale=ce[:, a, 4 + b : 5 + b])
+            elif kind == "xe" and a in E_ON_ACT:
+                nc.vector.tensor_copy(out=gb_k[a][:].rearrange("p (m i s) -> p m s i", s=4, i=4),
+                                      in_=gb_s16[:].rearrange("p s (m i) -> p m s i", i=4))
             elif kind == "xe":
                 lo, hi = (b, b + 1) if len(ix) > 1 else (0, 2)
                 nc.vector.tensor_tensor(out=gb_k[a][:, lo * 1024 : hi * 1024].rearrange("p (m i s) -> p m s i", s=4, i=2),

@@ -17,18 +17,32 @@ ALU = mybir.AluOpType
 ACT = mybir.ActivationFunctionType
 
 P = 128
+GROUP = 512
+BLOCKS = N // P
+BANKS = 8
 LEARNING_RATE = 1.0 / 256.0
-LOADS = "h0 s t0 w h1 t1 r y0 h2 h3 c y1 y2 y3".split()
-ORDER = """th0 pt0 wm0 eh0 tt00 qh0 tt01 p1 ma00 et00 wsp wp et01 th1 pt1 sa00 ma01 eh1 qt0 tt11 hr0 sa01 tt10 qh1 th2 et11 d0 th3 et10 tce eh2 ma11 qt1 eh3 hr1 ma10 ece sa11 qr0 mb12 qr1 sa10 qh23 mb13 sb12 mb10 hr23 sb13 mb11 sb10 d1 ma21 sb11 mb01 d2 qr23 mb00 xe1 mb03 sa21 mb02 sb01 td01 sb00 td00 sb03 td11 xc01 td10 se01 qb1 td21 sb02 ma20 se00 xc21 se02 ma31 xc00 se03 ma30 xc10 sa31 fg1 qa0 xc11 sa20 fg0 xe0 d3 fg3 td20 sa30 qa1 qb0 td31 cf1 xc20 cf3 td30 xc31 cf0 lg0 qa2 xc30 fg2 r0 lg1 qa3 cf2 lg2 so0 cr0 r1 lg3 r2 tr0 so1 cr1 cr3 cr2 so2 tr1 r3 tr3 er01 tr2 er3 so3 qo01 er2 qo3 sw01 qo2 sw3 ss3 ss1 ss2 ss0 sw2""".split()
-DIRECT_BF16 = [3]
-Y_ON_PE = [2,3]
-Y_ON_VECTOR = []
-H_GROUPS = ["0","1","23"]
-OUT_GROUPS = ["01","2","3"]
-E_ON_ACT = [0]
-H_PRE = [1]
-T_PRE = [0,1]
-WARM = 13
+BF16_ONE_PAIR = 0x3F803F80
+WARM_UP_PASSES = 12
+
+H_SETS = ("0", "1", "23")
+Y_ADDED_IN_PSUM = ((2, 1), (3, 0), (3, 1))
+E_ON_SCALAR = 0
+ROUNDED_FROM_PSUM = 3
+
+LOADS = "h0 s t0 h1 w t1 r h2 c y0 h3 y1 y2 y3".split()
+
+ORDER = """
+th0 eh0 tt01 tt00 qh0 et01 th1 et00 wp wsp ma00 eh1 qt0 ma01 sa00 qh1 tt11 sa01 hr1 tt10 et11 hr0 th2 et10 d01
+tce eh2 th3 d00 td01 ece qr0 eh3 ma11 qt1 d21 qr1 ma10 qh23 sa11 mb13 xc01 sa10 mb11 d11 sb13 mb12 hr23 sb11
+mb10 mb02 sb12 d10 ma20 sb10 qr23 mb03 sb02 xe1 mb00 sa20 mb01 se02 td11 sb03 td00 sb00 td10 d20 ma31 se03
+xc11 ma21 sb01 xc00 ma30 se00 xc10 fg0 se01 qa0 fg3 qb1 sa31 fg1 qa1 sa21 xe0 td20 d31 td21 d30 xc20 td31 sa30
+qb0 cf0 td30 xc21 cf3 xc31 lg0 cf1 xc30 fg2 qa2 lg1 qa3 cf2 r0 lg2 r1 lg3 so0 cr0 r2 so1 cr1 cr3 tr0 so2 cr2
+tr1 tr3 r3 er0 tr2 er1 qo0 er3 so3 qo1 er2 qo3 sw0 sw1 qo2 sw3 ss3 ss0 sw2 ss2 ss1
+""".split()
+
+
+def cols(k, width):
+    return slice(k * width, (k + 1) * width)
 
 
 def tile_tracinonevsallheadinfluence_x2_kernel(tc, h, t, w_words, w_scales, y, c, e, r, out_0, out_1, out_2):
@@ -38,266 +52,281 @@ def tile_tracinonevsallheadinfluence_x2_kernel(tc, h, t, w_words, w_scales, y, c
         psum = ctx.enter_context(tc.psum_pool(name="psum", bufs=1))
         ctx.enter_context(tc.manual_schedule())
 
-        def sb(name, shape, dtype):
+        def sbuf(name, shape, dtype):
             return keep.tile(shape, dtype, name=name, align_bytes=64)
 
-        def many(name, count, shape, dtype):
-            return [sb("%s%d" % (name, k), shape, dtype) for k in range(count)]
+        def sbuf_list(name, count, shape, dtype):
+            return [sbuf("%s%d" % (name, k), shape, dtype) for k in range(count)]
+
+        def sbuf_per_set(name, width, dtype):
+            return {key: sbuf(name + key, [P, 2, width * len(key)], dtype) for key in H_SETS}
 
         banks = {}
 
-        def new_bank(step):
-            banks[step] = psum.tile([P, 512], F32, name="bank_" + step, tag="bank%d" % (len(banks) % 8))
-            return banks[step]
+        def new_bank(name):
+            banks[name] = psum.tile([P, GROUP], F32, name="bank_" + name, tag="bank%d" % (len(banks) % BANKS))
+            return banks[name]
 
-        h_raw = many("h_raw", 4, [P, D], BF16)
-        y_raw = many("y_raw", 4, [P, V], BF16)
-        t_raw = many("t_raw", 2, [P, 4, 512], BF16)
-        w_raw = sb("w_raw", [P, 2, 2 * V], U8)
-        w_perm = sb("w_perm", [P, 2, 2 * V], U8)
-        ws_raw = sb("ws_raw", [P, 2, V], U8)
-        ws_perm = sb("ws_perm", [P, 2, V], U8)
-        ce_rows = sb("ce_rows", [P, 256], BF16)
-        ce = sb("ce", [P, 2, 8], F32)
-        r_sb = sb("r_sb", [P, 2, 4], BF16)
-        ident32 = sb("ident32", [P, P], F32)
-        ident16 = sb("ident16", [P, P], BF16)
-        table_warm = sb("table_warm", [P, 1], F32)
+        h_raw = sbuf_list("h_raw", BLOCKS, [P, D], BF16)
+        y_raw = sbuf_list("y_raw", BLOCKS, [P, V], BF16)
+        t_raw = sbuf_list("t_raw", 2, [P, BLOCKS, GROUP], BF16)
+        w_raw = sbuf("w_raw", [P, 2, 2 * V], U8)
+        w_perm = sbuf("w_perm", [P, 2, 2 * V], U8)
+        ws_raw = sbuf("ws_raw", [P, 2, V], U8)
+        ws_perm = sbuf("ws_perm", [P, 2, V], U8)
+        ce_rows = sbuf("ce_rows", [P, 2 * P], BF16)
+        ce = sbuf("ce", [P, 2, 8], F32)
+        r_sb = sbuf("r_sb", [P, 2, 4], BF16)
+        ident32 = sbuf("ident32", [P, P], F32)
+        ident16 = sbuf("ident16", [P, P], BF16)
+        table_warm = sbuf("table_warm", [P, 1], F32)
 
-        group_of = {int(ch): grp for grp in H_GROUPS for ch in grp}
-        out_group_of = {int(ch): grp for grp in OUT_GROUPS for ch in grp}
-        h_k = {grp: sb("h_k" + grp, [P, 2, 512 * len(grp)], BF16) for grp in H_GROUPS}
-        hr_k = {grp: sb("hr_k" + grp, [P, 2, 512 * len(grp)], BF16) for grp in H_GROUPS}
-        h_q = {grp: sb("h_q" + grp, [P, 2, P * len(grp)], U32) for grp in H_GROUPS}
-        h_s = {grp: sb("h_s" + grp, [P, 2, P * len(grp)], U8) for grp in H_GROUPS}
-        hr_q = {grp: sb("hr_q" + grp, [P, 2, P * len(grp)], U32) for grp in H_GROUPS}
-        hr_s = {grp: sb("hr_s" + grp, [P, 2, P * len(grp)], U8) for grp in H_GROUPS}
-        t_k = many("t_k", 2, [P, 2048], BF16)
-        ga_k = many("ga_k", 4, [P, 1024], BF16)
-        gb_k = many("gb_k", 2, [P, 2048], BF16)
-        out_k = sb("out_k", [P, 2048], BF16)
-        ga_q, ga_s = many("ga_q", 4, [P, 256], U32), many("ga_s", 4, [P, 256], U8)
-        t_q, t_s = many("t_q", 2, [P, 512], U32), many("t_s", 2, [P, 512], U8)
-        gb_q, gb_s = many("gb_q", 2, [P, 512], U32), many("gb_s", 2, [P, 512], U8)
-        out_q, out_s = sb("out_q", [P, 512], U32), sb("out_s", [P, 512], U8)
-        sig_a = many("sig_a", 4, [P, 4, 2, P], F32)
-        diff = many("diff", 4, [P, 4, 2, P], F32)
-        sig_b = many("sig_b", 2, [P, 4, 512], F32)
-        gb_s16 = sb("gb_s16", [P, 4, 512], BF16)
-        h_pre = {k: sb("h_pre%d" % k, [P, 2, 2, P], F32) for k in H_PRE}
-        t_pre = {k: sb("t_pre%d" % k, [P, 4, 2, P], F32) for k in T_PRE}
-        feat = many("feat", 4, [P, 512], F32)
-        res = many("res", 4, [P, 512], F32)
-        res16 = many("res16", 4, [P, 512], BF16)
+        h_k, hr_k = sbuf_per_set("h_k", GROUP, BF16), sbuf_per_set("hr_k", GROUP, BF16)
+        h_q, h_s = sbuf_per_set("h_q", P, U32), sbuf_per_set("h_s", P, U8)
+        hr_q, hr_s = sbuf_per_set("hr_q", P, U32), sbuf_per_set("hr_s", P, U8)
+        t_k, gb_k = sbuf_list("t_k", 2, [P, 4 * M], BF16), sbuf_list("gb_k", 2, [P, 4 * M], BF16)
+        t_q, t_s = sbuf_list("t_q", 2, [P, M], U32), sbuf_list("t_s", 2, [P, M], U8)
+        gb_q, gb_s = sbuf_list("gb_q", 2, [P, M], U32), sbuf_list("gb_s", 2, [P, M], U8)
+        ga_k = sbuf_list("ga_k", BLOCKS, [P, 2 * GROUP], BF16)
+        ga_q, ga_s = sbuf_list("ga_q", BLOCKS, [P, 2 * P], U32), sbuf_list("ga_s", BLOCKS, [P, 2 * P], U8)
+        out_k, out_q, out_s = sbuf("out_k", [P, 4 * N], BF16), sbuf("out_q", [P, N], U32), sbuf("out_s", [P, N], U8)
+        sig_a = sbuf_list("sig_a", BLOCKS, [P, 4, 2, P], F32)
+        diff = sbuf_list("diff", BLOCKS, [P, 4, 2, P], F32)
+        sig_b = sbuf_list("sig_b", 2, [P, 4, M], F32)
+        gb_rows = sbuf("gb_rows", [P, 4, M], BF16)
+        feat = sbuf_list("feat", BLOCKS, [P, M], F32)
+        res = sbuf_list("res", BLOCKS, [P, M], F32)
+        res16 = sbuf_list("res16", BLOCKS, [P, M], BF16)
+        warm16, warm_q, warm_s = sbuf("warm16", [P, GROUP], BF16), sbuf("warm_q", [P, P], U32), sbuf("warm_s", [P, P], U8)
 
-        warm16 = sb("warm16", [P, 512], BF16)
-        warm_q, warm_s = sb("warm_q", [P, P], U32), sb("warm_s", [P, P], U8)
-        nc.gpsimd.memset(warm16[:].bitcast(I32), 0x3F803F80)
+        nc.gpsimd.memset(warm16[:].bitcast(I32), BF16_ONE_PAIR)
         nc.gpsimd.memset(ws_raw[:].bitcast(I32), 0)
         make_identity(nc, ident32[:])
         nc.gpsimd.memset(ce_rows[:], 0.0)
         make_identity(nc, ident16[:])
 
-        def load(name):
-            k = int(name[1]) if len(name) > 1 else 0
+        for name in LOADS:
             if name[0] == "h":
-                nc.sync.dma_start(out=h_raw[k][:], in_=h[k * P : (k + 1) * P, :])
+                nc.sync.dma_start(out=h_raw[int(name[1])][:], in_=h[cols(int(name[1]), P), :])
             elif name[0] == "y":
-                nc.sync.dma_start(out=y_raw[k][:], in_=y[k * P : (k + 1) * P, :])
+                nc.sync.dma_start(out=y_raw[int(name[1])][:], in_=y[cols(int(name[1]), P), :])
             elif name[0] == "t":
-                nc.sync.dma_start(out=t_raw[k][:], in_=t[:, k * 512 : (k + 1) * 512].rearrange("(b p) k -> p b k", p=P))
-            elif name[0] == "w":
+                nc.sync.dma_start(out=t_raw[int(name[1])][:],
+                                  in_=t[:, cols(int(name[1]), GROUP)].rearrange("(b p) k -> p b k", p=P))
+            elif name == "w":
                 nc.sync.dma_start(out=w_raw[:].bitcast(I32), in_=w_words.bitcast(I32).rearrange("g p n -> p g n"))
-            elif name[0] == "r":
+            elif name == "r":
                 nc.sync.dma_start(out=r_sb[:], in_=r.rearrange("(g p s) -> p g s", g=2, s=4))
-            elif name[0] == "c":
+            elif name == "c":
                 for row, vec in ((0, c), (4, e)):
-                    nc.sync.dma_start(out=ce_rows[row : row + 4, :].rearrange("s (a i) -> s a i", i=8),
-                                      in_=vec.rearrange("(a s i) -> s a i", s=4, i=8))
+                    nc.sync.dma_start(out=ce_rows[row : row + 4, :].rearrange("s (gq i) -> s gq i", i=8),
+                                      in_=vec.rearrange("(gq s i) -> s gq i", s=4, i=8))
             else:
                 for quad in range(4):
-                    nc.scalar.dma_start(out=ws_raw[32 * quad : 32 * quad + 4, :, :].bitcast(I32),
-                                        in_=w_scales[:, 4 * quad : 4 * quad + 4, :].bitcast(I32).rearrange("g r n -> r g n"))
-
-        for name in LOADS:
-            load(name)
-        nc.scalar.activation(out=table_warm[:], in_=warm16[:, 0:1], func=ACT.Sigmoid)
+                    nc.scalar.dma_start(
+                        out=ws_raw[32 * quad : 32 * quad + 4, :, :].bitcast(I32),
+                        in_=w_scales[:, 4 * quad : 4 * quad + 4, :].bitcast(I32).rearrange("g j n -> j g n"))
 
         def quantize(codes, scales, values):
             nc.vector.quantize_mx(out=codes.bitcast(FP8X4), scales=scales, in_=values)
 
-        def two_passes(step, lhs, lhs_scale, rhs, rhs_scale):
-            bank = new_bank(step)
+        nc.scalar.activation(out=table_warm[:], in_=warm16[:, 0:1], func=ACT.Sigmoid)
+        quantize(warm_q[:], warm_s[:], warm16[:])
+        warm_bank = new_bank("warm")
+        for k in range(WARM_UP_PASSES):
+            nc.tensor.matmul_mx(out=warm_bank[:, cols(k % 4, P)], lhsT=warm_q[:].bitcast(FP8X4), lhsT_scale=warm_s[:],
+                                rhs=warm_q[:].bitcast(FP8X4), rhs_scale=warm_s[:], start=True, stop=True)
+
+        def product(name, lhs, lhs_scale, rhs, rhs_scale):
+            bank = new_bank(name)
             for g in range(2):
                 nc.tensor.matmul_mx(out=bank[:], lhsT=lhs(g), lhsT_scale=lhs_scale(g), rhs=rhs(g), rhs_scale=rhs_scale(g),
                                     start=(g == 0), stop=(g == 1))
 
-        def cols(k, width):
-            return slice(k * width, (k + 1) * width)
+        def set_of(blk):
+            key = [key for key in H_SETS if str(blk) in key][0]
+            return key, key.index(str(blk))
+
+        def block_of(tiles, blk, g):
+            key, place = set_of(blk)
+            return tiles[key][:, g, cols(place, P)]
 
         def flat(tile):
             return tile[:].rearrange("p g n -> p (g n)")
 
-        def rows_of(tiles, n):
-            own = group_of[n]
-            return lambda g: tiles[own][:, g, cols(own.index(str(n)), P)]
+        def permute_w_words():
+            nc.vector.tensor_copy(
+                out=w_perm[:].bitcast(I32).rearrange("p f (g s q j) -> p (f g) q s j", g=2, s=4, j=4),
+                in_=w_raw[:].bitcast(I32).rearrange("p f (g q s j) -> p (f g) q s j", g=2, s=4, j=4))
 
-        def warm_up(count):
-            for k in range(count):
-                nc.tensor.matmul_mx(out=banks["warm"][:, cols(k % 4, P)], lhsT=warm_q[:].bitcast(FP8X4), lhsT_scale=warm_s[:],
-                                    rhs=warm_q[:].bitcast(FP8X4), rhs_scale=warm_s[:], start=True, stop=True)
+        def permute_w_scales():
+            nc.vector.tensor_copy(
+                out=ws_perm[:].bitcast(I32).rearrange("p f (g s q j) -> p (f g) s q j", g=2, s=4, j=2),
+                in_=ws_raw[:].bitcast(I32).rearrange("p f (g q s j) -> p (f g) s q j", g=2, s=4, j=2))
 
-        quantize(warm_q[:], warm_s[:], warm16[:])
-        new_bank("warm")
-        warm_up(WARM)
+        def transpose_ce():
+            bank = new_bank("ce")
+            for g in range(2):
+                nc.tensor.transpose(bank[:].bitcast(BF16)[:, cols(g, P)], ce_rows[:, cols(g, P)], ident16[:])
 
-        def run(step):
-            kind = "".join([ch for ch in step if ch not in "0123456789"])
-            ix = [int(ch) for ch in step if ch in "0123456789"]
-            grp = "".join([str(k) for k in ix])
-            a = ix[0] if len(ix) > 0 else 0
-            b = ix[1] if len(ix) > 1 else 0
-            if kind == "wm":
-                warm_up(8)
-            elif kind == "wp":
-                nc.vector.tensor_copy(
-                    out=w_perm[:].bitcast(I32).rearrange("p g (v s q i) -> p (g v) q s i", v=2, s=4, i=4),
-                    in_=w_raw[:].bitcast(I32).rearrange("p g (v q s i) -> p (g v) q s i", v=2, s=4, i=4))
-            elif kind == "wsp":
-                nc.vector.tensor_copy(
-                    out=ws_perm[:].bitcast(I32).rearrange("p g (v s q i) -> p (g v) s q i", v=2, s=4, i=2),
-                    in_=ws_raw[:].bitcast(I32).rearrange("p g (v q s i) -> p (g v) s q i", v=2, s=4, i=2))
-            elif kind == "tce":
-                bank = new_bank(step)
-                for v in range(2):
-                    nc.tensor.transpose(bank[:].bitcast(BF16)[:, cols(v, P)], ce_rows[:, cols(v, P)], ident16[:])
-            elif kind == "ece":
-                nc.scalar.copy(out=ce[:], in_=banks["tce"][:].bitcast(BF16)[:, 0:256].rearrange("p (v j) -> p v j", v=2)[:, :, 0:8])
-            elif kind == "p":
-                nc.vector.tensor_copy(out=h_pre[a][:], in_=h_raw[a][:].bitcast(F32).rearrange("p (g k u) -> p g u k", g=2, u=2))
-            elif kind == "pt":
-                nc.vector.tensor_copy(out=t_pre[a][:], in_=t_raw[a][:].bitcast(F32).rearrange("p b (k u) -> p b u k", u=2))
-            elif kind == "th":
-                bank = new_bank(step)
-                words = h_raw[a][:].bitcast(F32)
-                for g in range(2):
-                    for u in range(2):
-                        nc.tensor.transpose(bank[:, cols(2 * g + u, P)], h_pre[a][:, g, u, :] if a in H_PRE else words[:, 256 * g + u : 256 * (g + 1) : 2], ident32[:])
-            elif kind == "eh":
-                own = group_of[a]
-                nc.scalar.copy(out=h_k[own][:, :, cols(own.index(str(a)), 512)].bitcast(F32).rearrange("p g (n u) -> p g n u", u=2),
-                               in_=banks["th%d" % a][:].rearrange("p (g u n) -> p g n u", g=2, u=2))
-            elif kind == "qh":
-                quantize(flat(h_q[grp]), flat(h_s[grp]), flat(h_k[grp]))
-            elif kind == "hr":
-                nc.vector.tensor_tensor(out=hr_k[grp][:].rearrange("p g (n s) -> p g n s", s=4),
-                                        in0=h_k[grp][:].rearrange("p g (n s) -> p g n s", s=4),
-                                        in1=r_sb[:].unsqueeze(2).to_broadcast([P, 2, P * len(grp), 4]), op=ALU.mult)
-            elif kind == "qr":
-                quantize(flat(hr_q[grp]), flat(hr_s[grp]), flat(hr_k[grp]))
-            elif kind == "tt":
-                bank = new_bank(step)
-                for blk in range(2):
-                    words = t_raw[a][:, 2 * b + blk, :].bitcast(F32)
-                    for u in range(2):
-                        nc.tensor.transpose(bank[:, cols(2 * blk + u, P)], t_pre[a][:, 2 * b + blk, u, :] if a in T_PRE else words[:, u:256:2], ident32[:])
-            elif kind == "et":
-                nc.scalar.copy(out=t_k[a][:, cols(b, 1024)].bitcast(F32).rearrange("p (k m u) -> p k m u", k=2, u=2),
-                               in_=banks["tt%d%d" % (a, b)][:].rearrange("p (k u m) -> p k m u", k=2, u=2))
-            elif kind == "qt":
-                quantize(t_q[a][:], t_s[a][:], t_k[a][:])
-            elif kind == "ma":
-                two_passes(step, lambda g: rows_of(h_q, a)(g).bitcast(FP8X4), rows_of(h_s, a),
-                           lambda g: w_raw[:, g, cols(b, 1024)].bitcast(FP4X4), lambda g: ws_raw[:, g, cols(b, 512)])
-            elif kind == "sa":
-                nc.scalar.activation(out=sig_a[a][:, :, b, :].rearrange("p s (q i) -> p s q i", i=8),
-                                     in_=banks["ma%d%d" % (a, b)][:].rearrange("p (q s i) -> p s q i", s=4, i=8), func=ACT.Sigmoid)
-            elif kind == "d":
-                lo, hi = (b, b + 1) if len(ix) > 1 else (0, 2)
-                y_view = y_raw[a][:, lo * 512 : hi * 512].rearrange("p (w s i) -> p s w i", s=4, i=8)
-                d_view = diff[a][:, :, lo:hi, :].rearrange("p s v (q i) -> p s (v q) i", i=8)
-                if a not in Y_ON_PE:
-                    nc.vector.tensor_tensor(out=d_view, in0=sig_a[a][:, :, lo:hi, :].rearrange("p s v (q i) -> p s (v q) i", i=8),
-                                            in1=y_view, op=ALU.subtract)
-                elif a in Y_ON_VECTOR:
-                    nc.vector.tensor_scalar(out=d_view, in0=y_view, scalar1=-1.0, scalar2=None, op0=ALU.mult)
-                else:
-                    nc.scalar.activation(out=d_view, in_=y_view, func=ACT.Copy, scale=-1.0)
-            elif kind == "td":
-                bank = new_bank(step)
-                terms = (diff[a], sig_a[a]) if a in Y_ON_PE else (diff[a],)
-                for k, src in enumerate(terms):
-                    for s in range(4):
-                        nc.tensor.matmul(bank[:, cols(s, P)], lhsT=src[:, s, b, :], rhs=ident32[:], is_transpose=True,
-                                         start=(k == 0 and s == 0), stop=(k == len(terms) - 1 and s == 3))
-            elif kind == "xc":
-                nc.vector.tensor_tensor(out=ga_k[a][:, cols(b, 512)].rearrange("p (n s) -> p n s", s=4),
-                                        in0=banks["td%d%d" % (a, b)][:].rearrange("p (s n) -> p n s", s=4),
-                                        in1=ce[:, b, 0:4].unsqueeze(1).to_broadcast([P, P, 4]), op=ALU.mult)
-            elif kind == "qa":
-                lo, hi = (b, b + 1) if len(ix) > 1 else (0, 2)
-                quantize(ga_q[a][:, lo * P : hi * P], ga_s[a][:, lo * P : hi * P], ga_k[a][:, lo * 512 : hi * 512])
-            elif kind == "mb":
-                two_passes(step, lambda g: w_perm[:, g, cols(4 * a + b, 256)].bitcast(FP4X4), lambda g: ws_perm[:, g, cols(4 * a + b, P)],
-                           lambda g: t_q[g][:].bitcast(FP8X4), lambda g: t_s[g][:])
-            elif kind == "sb":
-                nc.scalar.activation(out=sig_b[a][:, b, :], in_=banks["mb%d%d" % (a, b)][:], func=ACT.Sigmoid)
-            elif kind == "se":
-                nc.scalar.activation(out=gb_s16[:, b, :], in_=sig_b[a][:, b, :], func=ACT.Copy, scale=ce[:, a, 4 + b : 5 + b])
-            elif kind == "xe" and a in E_ON_ACT:
-                nc.vector.tensor_copy(out=gb_k[a][:].rearrange("p (m i s) -> p m s i", s=4, i=4),
-                                      in_=gb_s16[:].rearrange("p s (m i) -> p m s i", i=4))
-            elif kind == "xe":
-                lo, hi = (b, b + 1) if len(ix) > 1 else (0, 2)
-                nc.vector.tensor_tensor(out=gb_k[a][:, lo * 1024 : hi * 1024].rearrange("p (m i s) -> p m s i", s=4, i=2),
-                                        in0=sig_b[a][:, :, lo * 256 : hi * 256].rearrange("p s (m i) -> p m s i", i=2),
-                                        in1=ce[:, a, 4:8].unsqueeze(1).unsqueeze(3).to_broadcast([P, 128 * (hi - lo), 4, 2]), op=ALU.mult)
-            elif kind == "qb":
-                quantize(gb_q[a][:], gb_s[a][:], gb_k[a][:])
-            elif kind == "fg":
-                two_passes(step, lambda g: rows_of(hr_q, a)(g).bitcast(FP8X4), rows_of(hr_s, a),
-                           lambda g: t_q[g][:].bitcast(FP8X4), lambda g: t_s[g][:])
-            elif kind == "cf":
-                nc.scalar.activation(out=feat[a][:], in_=banks["fg%d" % a][:], func=ACT.Copy, scale=LEARNING_RATE)
-            elif kind == "lg":
-                for g in ix[1:] or [0, 1]:
-                    if g == 0:
-                        new_bank("lg%d" % a)
-                    nc.tensor.matmul_mx(out=banks["lg%d" % a][:], lhsT=ga_q[a][:, cols(g, P)].bitcast(FP8X4), lhsT_scale=ga_s[a][:, cols(g, P)],
-                                        rhs=gb_q[g][:].bitcast(FP8X4), rhs_scale=gb_s[g][:], start=(g == 0), stop=(g == 1))
-            elif kind == "r":
-                nc.vector.tensor_tensor(out=res[a][:], in0=banks["lg%d" % a][:], in1=feat[a][:], op=ALU.mult)
-            elif kind == "so":
-                nc.sync.dma_start(out=out_0[cols(a, P), :], in_=res[a][:])
-            elif kind == "cr":
-                pairs_out = res16[a][:].rearrange("p (u k j) -> p u k j", u=2, j=2)
-                if a in DIRECT_BF16:
-                    nc.vector.tensor_tensor(out=pairs_out, in0=banks["lg%d" % a][:].rearrange("p (k u j) -> p u k j", u=2, j=2),
-                                            in1=feat[a][:].rearrange("p (k u j) -> p u k j", u=2, j=2), op=ALU.mult)
-                else:
-                    nc.scalar.copy(out=pairs_out, in_=res[a][:].rearrange("p (k u j) -> p u k j", u=2, j=2))
-            elif kind == "tr":
-                own = out_group_of[a]
-                if ("tr" + own) not in banks:
-                    new_bank("tr" + own)
+        def copy_ce():
+            turned = banks["ce"][:].bitcast(BF16)[:, 0 : 2 * P].rearrange("p (g row) -> p g row", g=2)
+            nc.scalar.copy(out=ce[:], in_=turned[:, :, 0:8])
+
+        def transpose_h(blk):
+            bank = new_bank("h%d" % blk)
+            words = h_raw[blk][:].bitcast(F32)
+            for g in range(2):
                 for u in range(2):
-                    nc.tensor.transpose(banks["tr" + own][:, cols(2 * own.index(str(a)) + u, P)], res16[a][:].bitcast(F32)[:, cols(u, P)], ident32[:])
-            elif kind == "er":
-                lo, hi = ix[0], ix[-1] + 1
-                nc.scalar.copy(out=out_k[:, lo * 512 : hi * 512].bitcast(F32).rearrange("p (j n u) -> p j n u", n=P, u=2),
-                               in_=banks["tr" + grp][:, 0 : 256 * (hi - lo)].rearrange("p (j u n) -> p j n u", n=P, u=2))
-            elif kind == "qo":
-                lo, hi = ix[0], ix[-1] + 1
-                quantize(out_q[:, lo * P : hi * P], out_s[:, lo * P : hi * P], out_k[:, lo * 512 : hi * 512])
-            elif kind == "sw":
-                lo, hi = ix[0], ix[-1] + 1
-                nc.sync.dma_start(out=out_1[0].rearrange("p n s -> p (n s)").bitcast(I32)[:, lo * P : hi * P],
-                                  in_=out_q[:, lo * P : hi * P].bitcast(I32))
-            elif kind == "ss":
-                queue = nc.sync if a < 2 else nc.scalar
-                queue.dma_start(out=out_2[0, 4 * a : 4 * a + 4, :].bitcast(I32), in_=out_s[32 * a : 32 * a + 4, :].bitcast(I32))
-            else:
-                raise ValueError(step)
+                    nc.tensor.transpose(bank[:, cols(2 * g + u, P)], words[:, 2 * P * g + u : 2 * P * (g + 1) : 2], ident32[:])
 
+        def copy_h(blk):
+            key, place = set_of(blk)
+            nc.scalar.copy(out=h_k[key][:, :, cols(place, GROUP)].bitcast(F32).rearrange("p g (n u) -> p g n u", u=2),
+                           in_=banks["h%d" % blk][:].rearrange("p (g u n) -> p g n u", g=2, u=2))
+
+        def set_key(blks):
+            return "".join([str(blk) for blk in blks])
+
+        def quantize_h(*blks):
+            key = set_key(blks)
+            quantize(flat(h_q[key]), flat(h_s[key]), flat(h_k[key]))
+
+        def scale_h_by_r(*blks):
+            key = set_key(blks)
+            nc.vector.tensor_tensor(out=hr_k[key][:].rearrange("p g (n s) -> p g n s", s=4),
+                                    in0=h_k[key][:].rearrange("p g (n s) -> p g n s", s=4),
+                                    in1=r_sb[:].unsqueeze(2).to_broadcast([P, 2, P * len(blks), 4]), op=ALU.mult)
+
+        def quantize_hr(*blks):
+            key = set_key(blks)
+            quantize(flat(hr_q[key]), flat(hr_s[key]), flat(hr_k[key]))
+
+        def transpose_t(g, half):
+            bank = new_bank("t%d%d" % (g, half))
+            for k in range(2):
+                words = t_raw[g][:, 2 * half + k, :].bitcast(F32)
+                for u in range(2):
+                    nc.tensor.transpose(bank[:, cols(2 * k + u, P)], words[:, u : 2 * P : 2], ident32[:])
+
+        def copy_t(g, half):
+            nc.scalar.copy(out=t_k[g][:, cols(half, 2 * M)].bitcast(F32).rearrange("p (k m u) -> p k m u", k=2, u=2),
+                           in_=banks["t%d%d" % (g, half)][:].rearrange("p (k u m) -> p k m u", k=2, u=2))
+
+        def quantize_t(g):
+            quantize(t_q[g][:], t_s[g][:], t_k[g][:])
+
+        def matmul_a(blk, g):
+            product("a%d%d" % (blk, g), lambda f: block_of(h_q, blk, f).bitcast(FP8X4), lambda f: block_of(h_s, blk, f),
+                    lambda f: w_raw[:, f, cols(g, 2 * GROUP)].bitcast(FP4X4), lambda f: ws_raw[:, f, cols(g, GROUP)])
+
+        def sigmoid_a(blk, g):
+            nc.scalar.activation(out=sig_a[blk][:, :, g, :].rearrange("p s (q i) -> p s q i", i=8),
+                                 in_=banks["a%d%d" % (blk, g)][:].rearrange("p (q s i) -> p s q i", s=4, i=8), func=ACT.Sigmoid)
+
+        def take_y(blk, g):
+            y_view = y_raw[blk][:, cols(g, GROUP)].rearrange("p (q s i) -> p s q i", s=4, i=8)
+            diff_view = diff[blk][:, :, g, :].rearrange("p s (q i) -> p s q i", i=8)
+            if (blk, g) in Y_ADDED_IN_PSUM:
+                nc.scalar.activation(out=diff_view, in_=y_view, func=ACT.Copy, scale=-1.0)
+            else:
+                nc.vector.tensor_tensor(out=diff_view, in0=sig_a[blk][:, :, g, :].rearrange("p s (q i) -> p s q i", i=8),
+                                        in1=y_view, op=ALU.subtract)
+
+        def transpose_diff(blk, g):
+            bank = new_bank("d%d%d" % (blk, g))
+            terms = (diff[blk], sig_a[blk]) if (blk, g) in Y_ADDED_IN_PSUM else (diff[blk],)
+            for k, term in enumerate(terms):
+                for s in range(4):
+                    nc.tensor.matmul(bank[:, cols(s, P)], lhsT=term[:, s, g, :], rhs=ident32[:], is_transpose=True,
+                                     start=(k == 0 and s == 0), stop=(k == len(terms) - 1 and s == 3))
+
+        def scale_by_c(blk, g):
+            nc.vector.tensor_tensor(out=ga_k[blk][:, cols(g, GROUP)].rearrange("p (n s) -> p n s", s=4),
+                                    in0=banks["d%d%d" % (blk, g)][:].rearrange("p (s n) -> p n s", s=4),
+                                    in1=ce[:, g, 0:4].unsqueeze(1).to_broadcast([P, P, 4]), op=ALU.mult)
+
+        def quantize_ga(blk):
+            quantize(ga_q[blk][:], ga_s[blk][:], ga_k[blk][:])
+
+        def matmul_b(g, s):
+            product("b%d%d" % (g, s), lambda f: w_perm[:, f, cols(4 * g + s, 2 * P)].bitcast(FP4X4),
+                    lambda f: ws_perm[:, f, cols(4 * g + s, P)], lambda f: t_q[f][:].bitcast(FP8X4), lambda f: t_s[f][:])
+
+        def sigmoid_b(g, s):
+            nc.scalar.activation(out=sig_b[g][:, s, :], in_=banks["b%d%d" % (g, s)][:], func=ACT.Sigmoid)
+
+        def scale_by_e(g, s):
+            nc.scalar.activation(out=gb_rows[:, s, :], in_=sig_b[g][:, s, :], func=ACT.Copy, scale=ce[:, g, 4 + s : 5 + s])
+
+        def interleave_gb(g):
+            if g == E_ON_SCALAR:
+                nc.vector.tensor_copy(out=gb_k[g][:].rearrange("p (m j s) -> p m s j", s=4, j=4),
+                                      in_=gb_rows[:].rearrange("p s (m j) -> p m s j", j=4))
+            else:
+                nc.vector.tensor_tensor(out=gb_k[g][:].rearrange("p (m j s) -> p m s j", s=4, j=2),
+                                        in0=sig_b[g][:].rearrange("p s (m j) -> p m s j", j=2),
+                                        in1=ce[:, g, 4:8].unsqueeze(1).unsqueeze(3).to_broadcast([P, M // 2, 4, 2]), op=ALU.mult)
+
+        def quantize_gb(g):
+            quantize(gb_q[g][:], gb_s[g][:], gb_k[g][:])
+
+        def matmul_feat(blk):
+            product("f%d" % blk, lambda f: block_of(hr_q, blk, f).bitcast(FP8X4), lambda f: block_of(hr_s, blk, f),
+                    lambda f: t_q[f][:].bitcast(FP8X4), lambda f: t_s[f][:])
+
+        def copy_feat(blk):
+            nc.scalar.activation(out=feat[blk][:], in_=banks["f%d" % blk][:], func=ACT.Copy, scale=LEARNING_RATE)
+
+        def matmul_logit(blk):
+            product("l%d" % blk, lambda g: ga_q[blk][:, cols(g, P)].bitcast(FP8X4), lambda g: ga_s[blk][:, cols(g, P)],
+                    lambda g: gb_q[g][:].bitcast(FP8X4), lambda g: gb_s[g][:])
+
+        def multiply_grams(blk):
+            nc.vector.tensor_tensor(out=res[blk][:], in0=banks["l%d" % blk][:], in1=feat[blk][:], op=ALU.mult)
+
+        def store_result(blk):
+            nc.sync.dma_start(out=out_0[cols(blk, P), :], in_=res[blk][:])
+
+        def round_result(blk):
+            pairs = res16[blk][:].rearrange("n (u p j) -> n u p j", u=2, j=2)
+            if blk == ROUNDED_FROM_PSUM:
+                nc.vector.tensor_tensor(out=pairs, in0=banks["l%d" % blk][:].rearrange("n (p u j) -> n u p j", u=2, j=2),
+                                        in1=feat[blk][:].rearrange("n (p u j) -> n u p j", u=2, j=2), op=ALU.mult)
+            else:
+                nc.scalar.copy(out=pairs, in_=res[blk][:].rearrange("n (p u j) -> n u p j", u=2, j=2))
+
+        def transpose_result(blk):
+            bank = new_bank("r%d" % blk)
+            for u in range(2):
+                nc.tensor.transpose(bank[:, cols(u, P)], res16[blk][:].bitcast(F32)[:, cols(u, P)], ident32[:])
+
+        def copy_result(blk):
+            nc.scalar.copy(out=out_k[:, cols(blk, GROUP)].bitcast(F32).rearrange("p (n u) -> p n u", u=2),
+                           in_=banks["r%d" % blk][:, 0 : 2 * P].rearrange("p (u n) -> p n u", u=2))
+
+        def quantize_result(blk):
+            quantize(out_q[:, cols(blk, P)], out_s[:, cols(blk, P)], out_k[:, cols(blk, GROUP)])
+
+        def store_words(blk):
+            nc.sync.dma_start(out=out_1[0].rearrange("p n s -> p (n s)").bitcast(I32)[:, cols(blk, P)],
+                              in_=out_q[:, cols(blk, P)].bitcast(I32))
+
+        def store_scales(quad):
+            queue = nc.sync if quad < 2 else nc.scalar
+            queue.dma_start(out=out_2[0, 4 * quad : 4 * quad + 4, :].bitcast(I32),
+                            in_=out_s[32 * quad : 32 * quad + 4, :].bitcast(I32))
+
+        STEPS = {
+            "wp": permute_w_words, "wsp": permute_w_scales, "tce": transpose_ce, "ece": copy_ce,
+            "th": transpose_h, "eh": copy_h, "qh": quantize_h, "hr": scale_h_by_r, "qr": quantize_hr,
+            "tt": transpose_t, "et": copy_t, "qt": quantize_t,
+            "ma": matmul_a, "sa": sigmoid_a, "d": take_y, "td": transpose_diff, "xc": scale_by_c, "qa": quantize_ga,
+            "mb": matmul_b, "sb": sigmoid_b, "se": scale_by_e, "xe": interleave_gb, "qb": quantize_gb,
+            "fg": matmul_feat, "cf": copy_feat, "lg": matmul_logit, "r": multiply_grams, "so": store_result,
+            "cr": round_result, "tr": transpose_result, "er": copy_result, "qo": quantize_result,
+            "sw": store_words, "ss": store_scales,
+        }
         for step in ORDER:
-            run(step)
+            kind = "".join([ch for ch in step if ch not in "0123456789"])
+            STEPS[kind](*[int(ch) for ch in step if ch in "0123456789"])

@@ -4,7 +4,8 @@ import concourse.mybir as mybir
 from concourse.masks import make_identity
 
 N, M, D, V = 512, 512, 1024, 1024
-FLOPS = 2 * (N * D * V + M * D * V + N * M * V + N * M * D)
+LEARNING_RATE = 1.0 / 256.0
+FLOPS = 2 * (N + M) * D * V + 2 * N * M * (V + D)
 
 F32 = mybir.dt.float32
 BF16 = mybir.dt.bfloat16
@@ -13,320 +14,505 @@ U32 = mybir.dt.uint32
 U8 = mybir.dt.uint8
 FP8X4 = mybir.dt.float8_e4m3fn_x4
 FP4X4 = mybir.dt.float4_e2m1fn_x4
-ALU = mybir.AluOpType
 ACT = mybir.ActivationFunctionType
+ALU = mybir.AluOpType
 
 P = 128
-GROUP = 512
-BLOCKS = N // P
-BANKS = 8
-LEARNING_RATE = 1.0 / 256.0
-BF16_ONE_PAIR = 0x3F803F80
-WARM_UP_PASSES = 12
-
-H_SETS = ("0", "1", "23")
-Y_ADDED_IN_PSUM = ((2, 1), (3, 0), (3, 1))
-E_ON_SCALAR = 0
-ROUNDED_FROM_PSUM = 3
-
-LOADS = "h0 s t0 h1 w t1 r h2 c y0 h3 y1 y2 y3".split()
-
-ORDER = """
-th0 eh0 tt01 tt00 qh0 et01 th1 et00 wp wsp ma00 eh1 qt0 ma01 sa00 qh1 tt11 sa01 hr1 tt10 et11 hr0 th2 et10 d01
-tce eh2 th3 d00 td01 ece qr0 eh3 ma11 qt1 d21 qr1 ma10 qh23 sa11 mb13 xc01 sa10 mb11 d11 sb13 mb12 hr23 sb11
-mb10 mb02 sb12 d10 ma20 sb10 qr23 mb03 sb02 xe1 mb00 sa20 mb01 se02 td11 sb03 td00 sb00 td10 d20 ma31 se03
-xc11 ma21 sb01 xc00 ma30 se00 xc10 fg0 se01 qa0 fg3 qb1 sa31 fg1 qa1 sa21 xe0 td20 d31 td21 d30 xc20 td31 sa30
-qb0 cf0 td30 xc21 cf3 xc31 lg0 cf1 xc30 fg2 qa2 lg1 qa3 cf2 r0 lg2 r1 lg3 so0 cr0 r2 so1 cr1 cr3 tr0 so2 cr2
-tr1 tr3 r3 er0 tr2 er1 qo0 er3 so3 qo1 er2 qo3 sw0 sw1 qo2 sw3 ss3 ss0 sw2 ss2 ss1
-""".split()
-
-
-def cols(k, width):
-    return slice(k * width, (k + 1) * width)
+TILES = 4
+PASSES = 2
+BANK = 512
 
 
 def tile_tracinonevsallheadinfluence_x2_kernel(tc, h, t, w_words, w_scales, y, c, e, r, out_0, out_1, out_2):
     nc = tc.nc
     with ExitStack() as ctx:
-        keep = ctx.enter_context(tc.tile_pool(name="keep", bufs=1))
-        psum = ctx.enter_context(tc.psum_pool(name="psum", bufs=1))
+        sb = ctx.enter_context(tc.tile_pool(name="sb", bufs=1))
+        ps = ctx.enter_context(tc.psum_pool(name="ps", bufs=8))
         ctx.enter_context(tc.manual_schedule())
 
-        def sbuf(name, shape, dtype):
-            return keep.tile(shape, dtype, name=name, align_bytes=64)
+        def tiles(name, shape, dtype, count=TILES):
+            return [sb.tile(shape, dtype, name=name + str(i), align_bytes=64) for i in range(count)]
 
-        def sbuf_list(name, count, shape, dtype):
-            return [sbuf("%s%d" % (name, k), shape, dtype) for k in range(count)]
+        def new_bank():
+            return ps.tile([P, BANK], F32, name="bank")
 
-        def sbuf_per_set(name, width, dtype):
-            return {key: sbuf(name + key, [P, 2, width * len(key)], dtype) for key in H_SETS}
-
+        rows = {"h": tiles("h", [P, D], BF16), "t": tiles("t", [P, D], BF16)}
+        src = {"h": h, "t": t}
+        y_rows = tiles("y", [P, V], BF16)
+        y_neg = tiles("yneg", [P, V], F32)
+        w_all = sb.tile([P, PASSES, 2 * V], U8, align_bytes=64)
+        w_nat = [w_all[:, g, :] for g in range(PASSES)]
+        w_run = tiles("wrun", [P, 2 * V], U8, PASSES)
+        ws_nat = sb.tile([P, PASSES * V], U8, align_bytes=64)
+        ws_run = sb.tile([P, PASSES * V], U8, align_bytes=64)
+        r_k = sb.tile([P, PASSES, 4], BF16, align_bytes=64)
+        ce_rows = sb.tile([P, PASSES * P], BF16, align_bytes=64)
+        ce_k = sb.tile([P, PASSES, 8], BF16, align_bytes=64)
+        ident = sb.tile([P, P], F32, align_bytes=64)
+        ident_bf = sb.tile([P, P], BF16, align_bytes=64)
+        packed = {"h": tiles("hpack", [P, D], BF16), "t": tiles("tpack", [P, D], BF16)}
+        hr_pack = tiles("hrpack", [P, D], BF16)
+        h_codes, h_scales = tiles("hc", [P, PASSES * P], U32), tiles("hs", [P, PASSES * P], U8)
+        hr_codes, hr_scales = tiles("hrc", [P, PASSES * P], U32), tiles("hrs", [P, PASSES * P], U8)
+        t_codes, t_scales = tiles("tc", [P, M], U32, PASSES), tiles("ts", [P, M], U8, PASSES)
+        ga_codes, ga_scales = tiles("gac", [P, PASSES * P], U32), tiles("gas", [P, PASSES * P], U8)
+        gb_codes, gb_scales = tiles("gbc", [P, M], U32, PASSES), tiles("gbs", [P, M], U8, PASSES)
+        sig = {"h": tiles("sa", [P, BANK], F32, 2 * TILES), "t": tiles("sb", [P, BANK], F32, 2 * TILES)}
+        diff = tiles("diff", [P, BANK], F32, 2 * TILES)
+        grad = {"h": tiles("ga", [P, BANK], BF16, 2 * TILES), "t": tiles("gb", [P, BANK], BF16, 2 * TILES)}
+        feat = tiles("feat", [P, M], F32)
+        infl = tiles("infl", [P, M], F32)
+        infl_bf = tiles("inflbf", [P, M], BF16)
+        infl_pack = tiles("inflpack", [P, M], BF16)
+        out_codes = sb.tile([P, N], U32, align_bytes=64)
+        out_scales = sb.tile([P, N], U8, align_bytes=64)
         banks = {}
 
-        def new_bank(name):
-            banks[name] = psum.tile([P, GROUP], F32, name="bank_" + name, tag="bank%d" % (len(banks) % BANKS))
-            return banks[name]
+        def load_rows(kind, i):
+            nc.sync.dma_start(out=rows[kind][i][:], in_=src[kind][P * i : P * (i + 1), :])
 
-        h_raw = sbuf_list("h_raw", BLOCKS, [P, D], BF16)
-        y_raw = sbuf_list("y_raw", BLOCKS, [P, V], BF16)
-        t_raw = sbuf_list("t_raw", 2, [P, BLOCKS, GROUP], BF16)
-        w_raw = sbuf("w_raw", [P, 2, 2 * V], U8)
-        w_perm = sbuf("w_perm", [P, 2, 2 * V], U8)
-        ws_raw = sbuf("ws_raw", [P, 2, V], U8)
-        ws_perm = sbuf("ws_perm", [P, 2, V], U8)
-        ce_rows = sbuf("ce_rows", [P, 2 * P], BF16)
-        ce = sbuf("ce", [P, 2, 8], F32)
-        r_sb = sbuf("r_sb", [P, 2, 4], BF16)
-        ident32 = sbuf("ident32", [P, P], F32)
-        ident16 = sbuf("ident16", [P, P], BF16)
-        table_warm = sbuf("table_warm", [P, 1], F32)
+        def load_y(i):
+            nc.sync.dma_start(out=y_rows[i][:], in_=y[P * i : P * (i + 1), :])
 
-        h_k, hr_k = sbuf_per_set("h_k", GROUP, BF16), sbuf_per_set("hr_k", GROUP, BF16)
-        h_q, h_s = sbuf_per_set("h_q", P, U32), sbuf_per_set("h_s", P, U8)
-        hr_q, hr_s = sbuf_per_set("hr_q", P, U32), sbuf_per_set("hr_s", P, U8)
-        t_k, gb_k = sbuf_list("t_k", 2, [P, 4 * M], BF16), sbuf_list("gb_k", 2, [P, 4 * M], BF16)
-        t_q, t_s = sbuf_list("t_q", 2, [P, M], U32), sbuf_list("t_s", 2, [P, M], U8)
-        gb_q, gb_s = sbuf_list("gb_q", 2, [P, M], U32), sbuf_list("gb_s", 2, [P, M], U8)
-        ga_k = sbuf_list("ga_k", BLOCKS, [P, 2 * GROUP], BF16)
-        ga_q, ga_s = sbuf_list("ga_q", BLOCKS, [P, 2 * P], U32), sbuf_list("ga_s", BLOCKS, [P, 2 * P], U8)
-        out_k, out_q, out_s = sbuf("out_k", [P, 4 * N], BF16), sbuf("out_q", [P, N], U32), sbuf("out_s", [P, N], U8)
-        sig_a = sbuf_list("sig_a", BLOCKS, [P, 4, 2, P], F32)
-        diff = sbuf_list("diff", BLOCKS, [P, 4, 2, P], F32)
-        sig_b = sbuf_list("sig_b", 2, [P, 4, M], F32)
-        gb_rows = sbuf("gb_rows", [P, 4, M], BF16)
-        feat = sbuf_list("feat", BLOCKS, [P, M], F32)
-        res = sbuf_list("res", BLOCKS, [P, M], F32)
-        res16 = sbuf_list("res16", BLOCKS, [P, M], BF16)
-        warm16, warm_q, warm_s = sbuf("warm16", [P, GROUP], BF16), sbuf("warm_q", [P, P], U32), sbuf("warm_s", [P, P], U8)
+        def load_w():
+            nc.sync.dma_start(out=w_all[:].bitcast(I32), in_=w_words.bitcast(I32).rearrange("g p n -> p g n"))
 
-        nc.gpsimd.memset(warm16[:].bitcast(I32), BF16_ONE_PAIR)
-        nc.gpsimd.memset(ws_raw[:].bitcast(I32), 0)
-        make_identity(nc, ident32[:])
-        nc.gpsimd.memset(ce_rows[:], 0.0)
-        make_identity(nc, ident16[:])
+        def load_w_scales():
+            for q in range(4):
+                nc.scalar.dma_start(
+                    out=ws_nat[32 * q : 32 * q + 4, :].bitcast(I32).rearrange("r (g n) -> r g n", g=PASSES),
+                    in_=w_scales[:, 4 * q : 4 * q + 4, :].bitcast(I32).rearrange("g r n -> r g n"),
+                )
 
-        for name in LOADS:
-            if name[0] == "h":
-                nc.sync.dma_start(out=h_raw[int(name[1])][:], in_=h[cols(int(name[1]), P), :])
-            elif name[0] == "y":
-                nc.sync.dma_start(out=y_raw[int(name[1])][:], in_=y[cols(int(name[1]), P), :])
-            elif name[0] == "t":
-                nc.sync.dma_start(out=t_raw[int(name[1])][:],
-                                  in_=t[:, cols(int(name[1]), GROUP)].rearrange("(b p) k -> p b k", p=P))
-            elif name == "w":
-                nc.sync.dma_start(out=w_raw[:].bitcast(I32), in_=w_words.bitcast(I32).rearrange("g p n -> p g n"))
-            elif name == "r":
-                nc.sync.dma_start(out=r_sb[:], in_=r.rearrange("(g p s) -> p g s", g=2, s=4))
-            elif name == "c":
-                for row, vec in ((0, c), (4, e)):
-                    nc.sync.dma_start(out=ce_rows[row : row + 4, :].rearrange("s (gq i) -> s gq i", i=8),
-                                      in_=vec.rearrange("(gq s i) -> s gq i", s=4, i=8))
-            else:
-                for quad in range(4):
-                    nc.scalar.dma_start(
-                        out=ws_raw[32 * quad : 32 * quad + 4, :, :].bitcast(I32),
-                        in_=w_scales[:, 4 * quad : 4 * quad + 4, :].bitcast(I32).rearrange("g j n -> j g n"))
+        def load_vectors():
+            nc.sync.dma_start(out=r_k[:], in_=r.rearrange("(g p j) -> p g j", g=PASSES, j=4))
+            for first, vec in ((0, c), (4, e)):
+                nc.sync.dma_start(
+                    out=ce_rows[first : first + 4, :].rearrange("j (q s) -> j q s", s=8),
+                    in_=vec.rearrange("(q j s) -> j q s", j=4, s=8),
+                )
 
-        def quantize(codes, scales, values):
+        def turn_vectors():
+            bank = new_bank()
+            view = bank[:].bitcast(BF16)
+            for g in range(PASSES):
+                nc.tensor.transpose(view[:, P * g : P * (g + 1)], ce_rows[:, P * g : P * (g + 1)], ident_bf[:])
+            nc.vector.tensor_copy(out=ce_k[:], in_=view[:, 0 : PASSES * P].rearrange("p (g j) -> p g j", g=PASSES)[:, :, 0:8])
+
+        def sort_w(g):
+            nc.vector.tensor_copy(
+                out=w_run[g][:].bitcast(I32).rearrange("p (u j q s) -> p u j q s", u=2, j=4, q=16),
+                in_=w_nat[g].bitcast(I32).rearrange("p (u q j s) -> p u j q s", u=2, j=4, q=16),
+            )
+
+        def sort_w_scales():
+            nc.vector.tensor_copy(
+                out=ws_run[:].bitcast(I32).rearrange("p (u j q s) -> p u j q s", u=4, j=4, q=16),
+                in_=ws_nat[:].bitcast(I32).rearrange("p (u q j s) -> p u j q s", u=4, j=4, q=16),
+            )
+
+        def turn_rows(kind, i):
+            bank = new_bank()
+            banks["rows", kind, i] = bank
+            words = rows[kind][i][:].bitcast(F32)
+            for g in range(PASSES):
+                for u in range(2):
+                    at = P * (2 * g + u)
+                    nc.tensor.transpose(bank[:, at : at + P], words[:, 256 * g + u : 256 * (g + 1) : 2], ident[:])
+
+        def pack_rows(kind, i):
+            nc.scalar.copy(
+                out=packed[kind][i][:].bitcast(F32).rearrange("p (g n u) -> p g n u", g=PASSES, u=2),
+                in_=banks["rows", kind, i][:].rearrange("p (g u n) -> p g n u", g=PASSES, u=2),
+            )
+
+        def quantise(codes, scales, values):
             nc.vector.quantize_mx(out=codes.bitcast(FP8X4), scales=scales, in_=values)
 
-        nc.scalar.activation(out=table_warm[:], in_=warm16[:, 0:1], func=ACT.Sigmoid)
-        quantize(warm_q[:], warm_s[:], warm16[:])
-        warm_bank = new_bank("warm")
-        for k in range(WARM_UP_PASSES):
-            nc.tensor.matmul_mx(out=warm_bank[:, cols(k % 4, P)], lhsT=warm_q[:].bitcast(FP8X4), lhsT_scale=warm_s[:],
-                                rhs=warm_q[:].bitcast(FP8X4), rhs_scale=warm_s[:], start=True, stop=True)
-
-        def product(name, lhs, lhs_scale, rhs, rhs_scale):
-            bank = new_bank(name)
-            for g in range(2):
-                nc.tensor.matmul_mx(out=bank[:], lhsT=lhs(g), lhsT_scale=lhs_scale(g), rhs=rhs(g), rhs_scale=rhs_scale(g),
-                                    start=(g == 0), stop=(g == 1))
-
-        def set_of(blk):
-            key = [key for key in H_SETS if str(blk) in key][0]
-            return key, key.index(str(blk))
-
-        def block_of(tiles, blk, g):
-            key, place = set_of(blk)
-            return tiles[key][:, g, cols(place, P)]
-
-        def flat(tile):
-            return tile[:].rearrange("p g n -> p (g n)")
-
-        def permute_w_words():
-            nc.vector.tensor_copy(
-                out=w_perm[:].bitcast(I32).rearrange("p f (g s q j) -> p (f g) q s j", g=2, s=4, j=4),
-                in_=w_raw[:].bitcast(I32).rearrange("p f (g q s j) -> p (f g) q s j", g=2, s=4, j=4))
-
-        def permute_w_scales():
-            nc.vector.tensor_copy(
-                out=ws_perm[:].bitcast(I32).rearrange("p f (g s q j) -> p (f g) s q j", g=2, s=4, j=2),
-                in_=ws_raw[:].bitcast(I32).rearrange("p f (g q s j) -> p (f g) s q j", g=2, s=4, j=2))
-
-        def transpose_ce():
-            bank = new_bank("ce")
-            for g in range(2):
-                nc.tensor.transpose(bank[:].bitcast(BF16)[:, cols(g, P)], ce_rows[:, cols(g, P)], ident16[:])
-
-        def copy_ce():
-            turned = banks["ce"][:].bitcast(BF16)[:, 0 : 2 * P].rearrange("p (g row) -> p g row", g=2)
-            nc.scalar.copy(out=ce[:], in_=turned[:, :, 0:8])
-
-        def transpose_h(blk):
-            bank = new_bank("h%d" % blk)
-            words = h_raw[blk][:].bitcast(F32)
-            for g in range(2):
-                for u in range(2):
-                    nc.tensor.transpose(bank[:, cols(2 * g + u, P)], words[:, 2 * P * g + u : 2 * P * (g + 1) : 2], ident32[:])
-
-        def copy_h(blk):
-            key, place = set_of(blk)
-            nc.scalar.copy(out=h_k[key][:, :, cols(place, GROUP)].bitcast(F32).rearrange("p g (n u) -> p g n u", u=2),
-                           in_=banks["h%d" % blk][:].rearrange("p (g u n) -> p g n u", g=2, u=2))
-
-        def set_key(blks):
-            return "".join([str(blk) for blk in blks])
-
-        def quantize_h(*blks):
-            key = set_key(blks)
-            quantize(flat(h_q[key]), flat(h_s[key]), flat(h_k[key]))
-
-        def scale_h_by_r(*blks):
-            key = set_key(blks)
-            nc.vector.tensor_tensor(out=hr_k[key][:].rearrange("p g (n s) -> p g n s", s=4),
-                                    in0=h_k[key][:].rearrange("p g (n s) -> p g n s", s=4),
-                                    in1=r_sb[:].unsqueeze(2).to_broadcast([P, 2, P * len(blks), 4]), op=ALU.mult)
-
-        def quantize_hr(*blks):
-            key = set_key(blks)
-            quantize(flat(hr_q[key]), flat(hr_s[key]), flat(hr_k[key]))
-
-        def transpose_t(g, half):
-            bank = new_bank("t%d%d" % (g, half))
-            for k in range(2):
-                words = t_raw[g][:, 2 * half + k, :].bitcast(F32)
-                for u in range(2):
-                    nc.tensor.transpose(bank[:, cols(2 * k + u, P)], words[:, u : 2 * P : 2], ident32[:])
-
-        def copy_t(g, half):
-            nc.scalar.copy(out=t_k[g][:, cols(half, 2 * M)].bitcast(F32).rearrange("p (k m u) -> p k m u", k=2, u=2),
-                           in_=banks["t%d%d" % (g, half)][:].rearrange("p (k u m) -> p k m u", k=2, u=2))
-
-        def quantize_t(g):
-            quantize(t_q[g][:], t_s[g][:], t_k[g][:])
-
-        def matmul_a(blk, g):
-            product("a%d%d" % (blk, g), lambda f: block_of(h_q, blk, f).bitcast(FP8X4), lambda f: block_of(h_s, blk, f),
-                    lambda f: w_raw[:, f, cols(g, 2 * GROUP)].bitcast(FP4X4), lambda f: ws_raw[:, f, cols(g, GROUP)])
-
-        def sigmoid_a(blk, g):
-            nc.scalar.activation(out=sig_a[blk][:, :, g, :].rearrange("p s (q i) -> p s q i", i=8),
-                                 in_=banks["a%d%d" % (blk, g)][:].rearrange("p (q s i) -> p s q i", s=4, i=8), func=ACT.Sigmoid)
-
-        def take_y(blk, g):
-            y_view = y_raw[blk][:, cols(g, GROUP)].rearrange("p (q s i) -> p s q i", s=4, i=8)
-            diff_view = diff[blk][:, :, g, :].rearrange("p s (q i) -> p s q i", i=8)
-            if (blk, g) in Y_ADDED_IN_PSUM:
-                nc.scalar.activation(out=diff_view, in_=y_view, func=ACT.Copy, scale=-1.0)
+        def quantise_rows(kind, i):
+            if kind == "h":
+                quantise(h_codes[i][:], h_scales[i][:], packed["h"][i][:])
             else:
-                nc.vector.tensor_tensor(out=diff_view, in0=sig_a[blk][:, :, g, :].rearrange("p s (q i) -> p s q i", i=8),
-                                        in1=y_view, op=ALU.subtract)
+                for g in range(PASSES):
+                    cols = slice(P * i, P * (i + 1))
+                    quantise(t_codes[g][:, cols], t_scales[g][:, cols], packed["t"][i][:, BANK * g : BANK * (g + 1)])
 
-        def transpose_diff(blk, g):
-            bank = new_bank("d%d%d" % (blk, g))
-            terms = (diff[blk], sig_a[blk]) if (blk, g) in Y_ADDED_IN_PSUM else (diff[blk],)
-            for k, term in enumerate(terms):
-                for s in range(4):
-                    nc.tensor.matmul(bank[:, cols(s, P)], lhsT=term[:, s, g, :], rhs=ident32[:], is_transpose=True,
-                                     start=(k == 0 and s == 0), stop=(k == len(terms) - 1 and s == 3))
+        def scale_rows(i):
+            nc.vector.tensor_tensor(
+                out=hr_pack[i][:].rearrange("p (g n j) -> p g n j", g=PASSES, j=4),
+                in0=packed["h"][i][:].rearrange("p (g n j) -> p g n j", g=PASSES, j=4),
+                in1=r_k[:].unsqueeze(2).to_broadcast([P, PASSES, P, 4]),
+                op=ALU.mult,
+            )
 
-        def scale_by_c(blk, g):
-            nc.vector.tensor_tensor(out=ga_k[blk][:, cols(g, GROUP)].rearrange("p (n s) -> p n s", s=4),
-                                    in0=banks["d%d%d" % (blk, g)][:].rearrange("p (s n) -> p n s", s=4),
-                                    in1=ce[:, g, 0:4].unsqueeze(1).to_broadcast([P, P, 4]), op=ALU.mult)
+        def quantise_scaled(i):
+            quantise(hr_codes[i][:], hr_scales[i][:], hr_pack[i][:])
 
-        def quantize_ga(blk):
-            quantize(ga_q[blk][:], ga_s[blk][:], ga_k[blk][:])
-
-        def matmul_b(g, s):
-            product("b%d%d" % (g, s), lambda f: w_perm[:, f, cols(4 * g + s, 2 * P)].bitcast(FP4X4),
-                    lambda f: ws_perm[:, f, cols(4 * g + s, P)], lambda f: t_q[f][:].bitcast(FP8X4), lambda f: t_s[f][:])
-
-        def sigmoid_b(g, s):
-            nc.scalar.activation(out=sig_b[g][:, s, :], in_=banks["b%d%d" % (g, s)][:], func=ACT.Sigmoid)
-
-        def scale_by_e(g, s):
-            nc.scalar.activation(out=gb_rows[:, s, :], in_=sig_b[g][:, s, :], func=ACT.Copy, scale=ce[:, g, 4 + s : 5 + s])
-
-        def interleave_gb(g):
-            if g == E_ON_SCALAR:
-                nc.vector.tensor_copy(out=gb_k[g][:].rearrange("p (m j s) -> p m s j", s=4, j=4),
-                                      in_=gb_rows[:].rearrange("p s (m j) -> p m s j", j=4))
+        def logits(kind, i, u):
+            bank = new_bank()
+            banks["logits", kind, i, u] = bank
+            if kind == "h":
+                for g in range(PASSES):
+                    nc.tensor.matmul_mx(
+                        out=bank[:],
+                        lhsT=h_codes[i][:, P * g : P * (g + 1)].bitcast(FP8X4),
+                        lhsT_scale=h_scales[i][:, P * g : P * (g + 1)],
+                        rhs=w_nat[g][:, 2 * BANK * u : 2 * BANK * (u + 1)].bitcast(FP4X4),
+                        rhs_scale=ws_nat[:, V * g + BANK * u : V * g + BANK * (u + 1)],
+                        start=(g == 0),
+                        stop=(g == PASSES - 1),
+                    )
             else:
-                nc.vector.tensor_tensor(out=gb_k[g][:].rearrange("p (m j s) -> p m s j", s=4, j=2),
-                                        in0=sig_b[g][:].rearrange("p s (m j) -> p m s j", j=2),
-                                        in1=ce[:, g, 4:8].unsqueeze(1).unsqueeze(3).to_broadcast([P, M // 2, 4, 2]), op=ALU.mult)
+                for j in range(4):
+                    at = BANK * u + P * j
+                    for g in range(PASSES):
+                        nc.tensor.matmul_mx(
+                            out=bank[:, P * j : P * (j + 1)],
+                            lhsT=w_run[g][:, 2 * at : 2 * (at + P)].bitcast(FP4X4),
+                            lhsT_scale=ws_run[:, V * g + at : V * g + at + P],
+                            rhs=t_codes[g][:, P * i : P * (i + 1)].bitcast(FP8X4),
+                            rhs_scale=t_scales[g][:, P * i : P * (i + 1)],
+                            start=(g == 0),
+                            stop=(g == PASSES - 1),
+                        )
 
-        def quantize_gb(g):
-            quantize(gb_q[g][:], gb_s[g][:], gb_k[g][:])
-
-        def matmul_feat(blk):
-            product("f%d" % blk, lambda f: block_of(hr_q, blk, f).bitcast(FP8X4), lambda f: block_of(hr_s, blk, f),
-                    lambda f: t_q[f][:].bitcast(FP8X4), lambda f: t_s[f][:])
-
-        def copy_feat(blk):
-            nc.scalar.activation(out=feat[blk][:], in_=banks["f%d" % blk][:], func=ACT.Copy, scale=LEARNING_RATE)
-
-        def matmul_logit(blk):
-            product("l%d" % blk, lambda g: ga_q[blk][:, cols(g, P)].bitcast(FP8X4), lambda g: ga_s[blk][:, cols(g, P)],
-                    lambda g: gb_q[g][:].bitcast(FP8X4), lambda g: gb_s[g][:])
-
-        def multiply_grams(blk):
-            nc.vector.tensor_tensor(out=res[blk][:], in0=banks["l%d" % blk][:], in1=feat[blk][:], op=ALU.mult)
-
-        def store_result(blk):
-            nc.sync.dma_start(out=out_0[cols(blk, P), :], in_=res[blk][:])
-
-        def round_result(blk):
-            pairs = res16[blk][:].rearrange("n (u p j) -> n u p j", u=2, j=2)
-            if blk == ROUNDED_FROM_PSUM:
-                nc.vector.tensor_tensor(out=pairs, in0=banks["l%d" % blk][:].rearrange("n (p u j) -> n u p j", u=2, j=2),
-                                        in1=feat[blk][:].rearrange("n (p u j) -> n u p j", u=2, j=2), op=ALU.mult)
+        def sigmoid(kind, i, u):
+            bank = banks["logits", kind, i, u]
+            if kind == "h":
+                out = sig["h"][2 * i + u][:].rearrange("n (j q s) -> n j q s", j=4, q=16)
+                in_ = bank[:].rearrange("n (q j s) -> n j q s", j=4, q=16)
             else:
-                nc.scalar.copy(out=pairs, in_=res[blk][:].rearrange("n (p u j) -> n u p j", u=2, j=2))
+                out = sig["t"][2 * i + u][:].rearrange("p (m j) -> p m j", j=4)
+                in_ = bank[:].rearrange("p (j m) -> p m j", j=4)
+            nc.scalar.activation(out=out, in_=in_, func=ACT.Sigmoid)
 
-        def transpose_result(blk):
-            bank = new_bank("r%d" % blk)
+        def negate_y(i, u):
+            nc.scalar.activation(
+                out=y_neg[i][:, BANK * u : BANK * (u + 1)].rearrange("n (j q s) -> n j q s", j=4, q=16),
+                in_=y_rows[i][:, BANK * u : BANK * (u + 1)].rearrange("n (q j s) -> n j q s", j=4, q=16),
+                func=ACT.Copy, scale=-1.0,
+            )
+
+        def subtract_y(i, u, eng):
+            eng.tensor_tensor(
+                out=diff[2 * i + u][:].rearrange("n (j q s) -> n j q s", j=4, q=16),
+                in0=sig["h"][2 * i + u][:].rearrange("n (j q s) -> n j q s", j=4, q=16),
+                in1=y_rows[i][:, BANK * u : BANK * (u + 1)].rearrange("n (q j s) -> n j q s", j=4, q=16),
+                op=ALU.subtract,
+            )
+
+        def turn_diff(i, u):
+            bank = new_bank()
+            banks["diff", i, u] = bank
+            for j in range(4):
+                cols = slice(P * j, P * (j + 1))
+                nc.tensor.transpose(bank[:, cols], diff[2 * i + u][:, cols], ident[:])
+
+        def turn_and_subtract(i, u):
+            bank = new_bank()
+            banks["diff", i, u] = bank
+            for j in range(4):
+                cols = slice(P * j, P * (j + 1))
+                at = BANK * u + P * j
+                nc.tensor.matmul(bank[:, cols], lhsT=y_neg[i][:, at : at + P], rhs=ident[:], is_transpose=True, start=True, stop=False)
+                nc.tensor.matmul(bank[:, cols], lhsT=sig["h"][2 * i + u][:, cols], rhs=ident[:], is_transpose=True, start=False, stop=True)
+
+        def weigh(kind, i, u):
+            if kind == "h":
+                in0 = banks["diff", i, u][:].rearrange("p (j n) -> p n j", j=4)
+                factor = ce_k[:, u, 0:4]
+            else:
+                in0 = sig["t"][2 * i + u][:].rearrange("p (m j) -> p m j", j=4)
+                factor = ce_k[:, u, 4:8]
+            nc.vector.tensor_tensor(
+                out=grad[kind][2 * i + u][:].rearrange("p (n j) -> p n j", j=4),
+                in0=in0,
+                in1=factor.unsqueeze(1).to_broadcast([P, P, 4]),
+                op=ALU.mult,
+            )
+
+        def quantise_grad(kind, i, u):
+            if kind == "h":
+                cols = slice(P * u, P * (u + 1))
+                quantise(ga_codes[i][:, cols], ga_scales[i][:, cols], grad["h"][2 * i + u][:])
+            else:
+                cols = slice(P * i, P * (i + 1))
+                quantise(gb_codes[u][:, cols], gb_scales[u][:, cols], grad["t"][2 * i + u][:])
+
+        def gram_pass(bank, g, codes, scales, moving_codes, moving_scales):
+            nc.tensor.matmul_mx(
+                out=bank[:],
+                lhsT=codes[:, P * g : P * (g + 1)].bitcast(FP8X4),
+                lhsT_scale=scales[:, P * g : P * (g + 1)],
+                rhs=moving_codes[g][:].bitcast(FP8X4),
+                rhs_scale=moving_scales[g][:],
+                start=(g == 0),
+                stop=(g == PASSES - 1),
+            )
+
+        def feat_gram(i):
+            bank = new_bank()
+            banks["feat", i] = bank
+            for g in range(PASSES):
+                gram_pass(bank, g, hr_codes[i], hr_scales[i], t_codes, t_scales)
+
+        def keep_feat(i):
+            nc.scalar.activation(out=feat[i][:], in_=banks["feat", i][:], func=ACT.Copy, scale=LEARNING_RATE)
+
+        def logit_gram(i):
+            bank = new_bank()
+            banks["logit_gram", i] = bank
+            for g in range(PASSES):
+                gram_pass(bank, g, ga_codes[i], ga_scales[i], gb_codes, gb_scales)
+
+        def influence(i):
+            nc.vector.tensor_tensor(out=infl[i][:], in0=feat[i][:], in1=banks["logit_gram", i][:], op=ALU.mult)
+
+        def store_influence(i):
+            nc.sync.dma_start(out=out_0[P * i : P * (i + 1), :], in_=infl[i][:])
+
+        def round_influence(i, copy):
+            copy(
+                out=infl_bf[i][:].rearrange("n (u p s) -> n u p s", u=2, s=2),
+                in_=infl[i][:].rearrange("n (p u s) -> n u p s", u=2, s=2),
+            )
+
+        def influence_rounded(i):
+            nc.vector.tensor_tensor(
+                out=infl_bf[i][:].rearrange("n (u p s) -> n u p s", u=2, s=2),
+                in0=feat[i][:].rearrange("n (p u s) -> n u p s", u=2, s=2),
+                in1=banks["logit_gram", i][:].rearrange("n (p u s) -> n u p s", u=2, s=2),
+                op=ALU.mult,
+            )
+
+        def turn_influence(i):
+            bank = new_bank()
+            banks["infl", i] = bank
+            words = infl_bf[i][:].bitcast(F32)
             for u in range(2):
-                nc.tensor.transpose(bank[:, cols(u, P)], res16[blk][:].bitcast(F32)[:, cols(u, P)], ident32[:])
+                nc.tensor.transpose(bank[:, P * u : P * (u + 1)], words[:, P * u : P * (u + 1)], ident[:])
 
-        def copy_result(blk):
-            nc.scalar.copy(out=out_k[:, cols(blk, GROUP)].bitcast(F32).rearrange("p (n u) -> p n u", u=2),
-                           in_=banks["r%d" % blk][:, 0 : 2 * P].rearrange("p (u n) -> p n u", u=2))
+        def pack_influence(i, eng=None):
+            out = infl_pack[i][:].bitcast(F32).rearrange("p (n u) -> p n u", u=2)
+            in_ = banks["infl", i][:, 0 : 2 * P].rearrange("p (u n) -> p n u", u=2)
+            if eng is None:
+                nc.scalar.copy(out=out, in_=in_)
+            else:
+                eng.tensor_copy(out=out, in_=in_)
 
-        def quantize_result(blk):
-            quantize(out_q[:, cols(blk, P)], out_s[:, cols(blk, P)], out_k[:, cols(blk, GROUP)])
+        def quantise_influence(i):
+            quantise(out_codes[:, P * i : P * (i + 1)], out_scales[:, P * i : P * (i + 1)], infl_pack[i][:])
 
-        def store_words(blk):
-            nc.sync.dma_start(out=out_1[0].rearrange("p n s -> p (n s)").bitcast(I32)[:, cols(blk, P)],
-                              in_=out_q[:, cols(blk, P)].bitcast(I32))
+        def store_codes(first, last):
+            words = out_1[0].rearrange("p m j -> p (m j)").bitcast(I32)
+            nc.sync.dma_start(out=words[:, P * first : P * last], in_=out_codes[:, P * first : P * last].bitcast(I32))
 
-        def store_scales(quad):
-            queue = nc.sync if quad < 2 else nc.scalar
-            queue.dma_start(out=out_2[0, 4 * quad : 4 * quad + 4, :].bitcast(I32),
-                            in_=out_s[32 * quad : 32 * quad + 4, :].bitcast(I32))
+        def store_scales():
+            for q in range(4):
+                queue = nc.sync if q % 2 == 0 else nc.scalar
+                queue.dma_start(
+                    out=out_2[0, 4 * q : 4 * q + 4, :].bitcast(I32),
+                    in_=out_scales[32 * q : 32 * q + 4, :].bitcast(I32),
+                )
 
-        STEPS = {
-            "wp": permute_w_words, "wsp": permute_w_scales, "tce": transpose_ce, "ece": copy_ce,
-            "th": transpose_h, "eh": copy_h, "qh": quantize_h, "hr": scale_h_by_r, "qr": quantize_hr,
-            "tt": transpose_t, "et": copy_t, "qt": quantize_t,
-            "ma": matmul_a, "sa": sigmoid_a, "d": take_y, "td": transpose_diff, "xc": scale_by_c, "qa": quantize_ga,
-            "mb": matmul_b, "sb": sigmoid_b, "se": scale_by_e, "xe": interleave_gb, "qb": quantize_gb,
-            "fg": matmul_feat, "cf": copy_feat, "lg": matmul_logit, "r": multiply_grams, "so": store_result,
-            "cr": round_result, "tr": transpose_result, "er": copy_result, "qo": quantize_result,
-            "sw": store_words, "ss": store_scales,
-        }
-        for step in ORDER:
-            kind = "".join([ch for ch in step if ch not in "0123456789"])
-            STEPS[kind](*[int(ch) for ch in step if ch in "0123456789"])
+        def setup():
+            nc.gpsimd.memset(ws_nat[:].bitcast(I32), 0)
+            make_identity(nc, ident[:])
+            nc.vector.memset(ce_rows[:], 0.0)
+            nc.vector.tensor_copy(out=ident_bf[:], in_=ident[:])
+
+        warm_in = sb.tile([P, BANK], BF16, align_bytes=64)
+        warm_codes = sb.tile([P, P], U32, align_bytes=64)
+        warm_scales = sb.tile([P, P], U8, align_bytes=64)
+        warm_act = sb.tile([P, 8], F32, align_bytes=64)
+
+        def warm_setup():
+            nc.vector.memset(warm_in[:], 1.0)
+            quantise(warm_codes[:], warm_scales[:], warm_in[:])
+
+        def warm_table():
+            nc.scalar.activation(out=warm_act[:, 0:1], in_=warm_in[:, 0:1], func=ACT.Sigmoid)
+
+        def warm(count):
+            bank = new_bank()
+            for k in range(count):
+                nc.tensor.matmul_mx(
+                    out=bank[:, 0:P], lhsT=warm_codes[:, 0:P].bitcast(FP8X4), lhsT_scale=warm_scales[:, 0:P],
+                    rhs=warm_codes[:].bitcast(FP8X4), rhs_scale=warm_scales[:], start=True, stop=True,
+                )
+
+        warm_setup()
+        setup()
+        load_w_scales()
+        warm_table()
+        load_rows("h", 0)
+        load_rows("t", 0)
+        load_w()
+        load_vectors()
+        load_rows("h", 1)
+        load_rows("t", 1)
+        load_y(0)
+        load_rows("t", 2)
+        load_rows("t", 3)
+        load_y(1)
+        load_y(2)
+        load_rows("h", 2)
+        load_rows("h", 3)
+        load_y(3)
+        warm(14)
+        turn_rows("h", 0)
+        pack_rows("h", 0)
+        turn_rows("t", 0)
+        pack_rows("t", 0)
+        warm(12)
+        quantise_rows("h", 0)
+        sort_w(0)
+        sort_w(1)
+        sort_w_scales()
+        quantise_rows("t", 0)
+        logits("h", 0, 0)
+        sigmoid("h", 0, 0)
+        logits("h", 0, 1)
+        sigmoid("h", 0, 1)
+        scale_rows(0)
+        turn_vectors()
+        turn_rows("h", 1)
+        pack_rows("h", 1)
+        turn_rows("t", 1)
+        pack_rows("t", 1)
+        quantise_scaled(0)
+        subtract_y(0, 0, nc.vector)
+        subtract_y(0, 1, nc.vector)
+        quantise_rows("h", 1)
+        quantise_rows("t", 1)
+        logits("t", 0, 0)
+        sigmoid("t", 0, 0)
+        logits("t", 0, 1)
+        sigmoid("t", 0, 1)
+        turn_diff(0, 0)
+        turn_diff(0, 1)
+        turn_rows("t", 2)
+        pack_rows("t", 2)
+        turn_rows("t", 3)
+        pack_rows("t", 3)
+        scale_rows(1)
+        weigh("t", 0, 0)
+        weigh("t", 0, 1)
+        weigh("h", 0, 0)
+        weigh("h", 0, 1)
+        quantise_grad("t", 0, 0)
+        quantise_grad("t", 0, 1)
+        quantise_rows("t", 2)
+        quantise_grad("h", 0, 0)
+        quantise_grad("h", 0, 1)
+        quantise_rows("t", 3)
+        quantise_scaled(1)
+        logits("h", 1, 0)
+        sigmoid("h", 1, 0)
+        logits("h", 1, 1)
+        sigmoid("h", 1, 1)
+        negate_y(2, 0)
+        turn_rows("h", 2)
+        pack_rows("h", 2)
+        subtract_y(1, 0, nc.vector)
+        subtract_y(1, 1, nc.vector)
+        quantise_rows("h", 2)
+        logits("t", 1, 0)
+        sigmoid("t", 1, 0)
+        logits("t", 1, 1)
+        sigmoid("t", 1, 1)
+        negate_y(2, 1)
+        turn_diff(1, 0)
+        turn_diff(1, 1)
+        turn_rows("h", 3)
+        pack_rows("h", 3)
+        weigh("t", 1, 0)
+        weigh("t", 1, 1)
+        scale_rows(2)
+        quantise_grad("t", 1, 0)
+        quantise_grad("t", 1, 1)
+        weigh("h", 1, 0)
+        weigh("h", 1, 1)
+        quantise_rows("h", 3)
+        quantise_scaled(2)
+        quantise_grad("h", 1, 0)
+        quantise_grad("h", 1, 1)
+        logits("t", 2, 0)
+        sigmoid("t", 2, 0)
+        logits("t", 2, 1)
+        sigmoid("t", 2, 1)
+        negate_y(3, 0)
+        feat_gram(0)
+        keep_feat(0)
+        weigh("t", 2, 0)
+        weigh("t", 2, 1)
+        scale_rows(3)
+        quantise_grad("t", 2, 0)
+        quantise_grad("t", 2, 1)
+        quantise_scaled(3)
+        logits("t", 3, 0)
+        sigmoid("t", 3, 0)
+        logits("t", 3, 1)
+        sigmoid("t", 3, 1)
+        negate_y(3, 1)
+        weigh("t", 3, 0)
+        weigh("t", 3, 1)
+        quantise_grad("t", 3, 0)
+        quantise_grad("t", 3, 1)
+        logits("h", 2, 0)
+        sigmoid("h", 2, 0)
+        logits("h", 2, 1)
+        sigmoid("h", 2, 1)
+        logits("h", 3, 0)
+        sigmoid("h", 3, 0)
+        logits("h", 3, 1)
+        sigmoid("h", 3, 1)
+        feat_gram(1)
+        keep_feat(1)
+        turn_and_subtract(2, 0)
+        turn_and_subtract(2, 1)
+        weigh("h", 2, 0)
+        weigh("h", 2, 1)
+        turn_and_subtract(3, 0)
+        turn_and_subtract(3, 1)
+        logit_gram(0)
+        quantise_grad("h", 2, 0)
+        quantise_grad("h", 2, 1)
+        weigh("h", 3, 0)
+        weigh("h", 3, 1)
+        feat_gram(2)
+        keep_feat(2)
+        influence(0)
+        store_influence(0)
+        feat_gram(3)
+        keep_feat(3)
+        logit_gram(1)
+        quantise_grad("h", 3, 0)
+        quantise_grad("h", 3, 1)
+        round_influence(0, nc.scalar.copy)
+        influence(1)
+        store_influence(1)
+        logit_gram(2)
+        logit_gram(3)
+        round_influence(1, nc.scalar.copy)
+        influence(2)
+        store_influence(2)
+        turn_influence(0)
+        pack_influence(0)
+        influence_rounded(3)
+        turn_influence(1)
+        pack_influence(1)
+        round_influence(2, nc.vector.tensor_copy)
+        influence(3)
+        store_influence(3)
+        turn_influence(3)
+        turn_influence(2)
+        pack_influence(3)
+        pack_influence(2)
+        quantise_influence(0)
+        quantise_influence(1)
+        store_codes(0, 2)
+        quantise_influence(3)
+        quantise_influence(2)
+        store_codes(2, 4)
+        store_scales()

@@ -20,499 +20,434 @@ ALU = mybir.AluOpType
 P = 128
 TILES = 4
 PASSES = 2
-BANK = 512
+PASS = 512
+PLACES = 4
+RUN = 8
+BLOCKS = 16
+BANKS = 8
+ON_VECTOR = (0, 1)
+ON_TENSOR = (2, 3)
+WARM_PASSES = (14, 6, 4)
 
 
 def tile_tracinonevsallheadinfluence_x2_kernel(tc, h, t, w_words, w_scales, y, c, e, r, out_0, out_1, out_2):
     nc = tc.nc
     with ExitStack() as ctx:
         sb = ctx.enter_context(tc.tile_pool(name="sb", bufs=1))
-        ps = ctx.enter_context(tc.psum_pool(name="ps", bufs=8))
+        ps = ctx.enter_context(tc.psum_pool(name="ps", bufs=BANKS))
         ctx.enter_context(tc.manual_schedule())
 
-        def tiles(name, shape, dtype, count=TILES):
-            return [sb.tile(shape, dtype, name=name + str(i), align_bytes=64) for i in range(count)]
+        def tile(name, shape, dtype):
+            return sb.tile(shape, dtype, name=name, align_bytes=64)
 
-        def new_bank():
-            return ps.tile([P, BANK], F32, name="bank")
+        def tiles(name, shape, dtype, keys=range(TILES)):
+            return {key: tile(name + str(n), shape, dtype) for n, key in enumerate(keys)}
 
+        def halves(row_tiles):
+            return [(i, u) for i in row_tiles for u in range(PASSES)]
+
+        source = {"h": h, "t": t}
         rows = {"h": tiles("h", [P, D], BF16), "t": tiles("t", [P, D], BF16)}
-        src = {"h": h, "t": t}
         y_rows = tiles("y", [P, V], BF16)
-        y_neg = tiles("yneg", [P, V], F32)
-        w_all = sb.tile([P, PASSES, 2 * V], U8, align_bytes=64)
-        w_nat = [w_all[:, g, :] for g in range(PASSES)]
-        w_run = tiles("wrun", [P, 2 * V], U8, PASSES)
-        ws_nat = sb.tile([P, PASSES * V], U8, align_bytes=64)
-        ws_run = sb.tile([P, PASSES * V], U8, align_bytes=64)
-        r_k = sb.tile([P, PASSES, 4], BF16, align_bytes=64)
-        ce_rows = sb.tile([P, PASSES * P], BF16, align_bytes=64)
-        ce_k = sb.tile([P, PASSES, 8], BF16, align_bytes=64)
-        ident = sb.tile([P, P], F32, align_bytes=64)
-        ident_bf = sb.tile([P, P], BF16, align_bytes=64)
-        packed = {"h": tiles("hpack", [P, D], BF16), "t": tiles("tpack", [P, D], BF16)}
-        hr_pack = tiles("hrpack", [P, D], BF16)
-        h_codes, h_scales = tiles("hc", [P, PASSES * P], U32), tiles("hs", [P, PASSES * P], U8)
-        hr_codes, hr_scales = tiles("hrc", [P, PASSES * P], U32), tiles("hrs", [P, PASSES * P], U8)
-        t_codes, t_scales = tiles("tc", [P, M], U32, PASSES), tiles("ts", [P, M], U8, PASSES)
-        ga_codes, ga_scales = tiles("gac", [P, PASSES * P], U32), tiles("gas", [P, PASSES * P], U8)
-        gb_codes, gb_scales = tiles("gbc", [P, M], U32, PASSES), tiles("gbs", [P, M], U8, PASSES)
-        sig = {"h": tiles("sa", [P, BANK], F32, 2 * TILES), "t": tiles("sb", [P, BANK], F32, 2 * TILES)}
-        diff = tiles("diff", [P, BANK], F32, 2 * TILES)
-        grad = {"h": tiles("ga", [P, BANK], BF16, 2 * TILES), "t": tiles("gb", [P, BANK], BF16, 2 * TILES)}
+        w_given = tiles("w_given", [P, PASSES, 2 * PASS], U8, range(PASSES))
+        w_sorted = tiles("w_sorted", [P, PASSES, 2 * PASS], U8, range(PASSES))
+        ws_given = tile("ws_given", [P, PASSES * V], U8)
+        ws_sorted = tile("ws_sorted", [P, PASSES * V], U8)
+        r_k = tile("r_k", [P, PASSES, PLACES], BF16)
+        ce_rows = tile("ce_rows", [P, PASSES * P], BF16)
+        ce_k = tile("ce_k", [P, PASSES, 2 * PLACES], BF16)
+        ident = tile("ident", [P, P], F32)
+        ident_bf = tile("ident_bf", [P, P], BF16)
+        packed = {"h": tiles("h_packed", [P, D], BF16), "t": tiles("t_packed", [P, D], BF16)}
+        hr_packed = tiles("hr_packed", [P, D], BF16)
+        h_codes, h_scales = tiles("h_codes", [P, PASSES * P], U32), tiles("h_scales", [P, PASSES * P], U8)
+        hr_codes, hr_scales = tiles("hr_codes", [P, PASSES * P], U32), tiles("hr_scales", [P, PASSES * P], U8)
+        ga_codes, ga_scales = tiles("ga_codes", [P, PASSES * P], U32), tiles("ga_scales", [P, PASSES * P], U8)
+        t_codes, t_scales = tiles("t_codes", [P, M], U32, range(PASSES)), tiles("t_scales", [P, M], U8, range(PASSES))
+        gb_codes, gb_scales = tiles("gb_codes", [P, M], U32, range(PASSES)), tiles("gb_scales", [P, M], U8, range(PASSES))
+        sig = {kind: tiles("sig_" + kind, [P, PASS], F32, halves(range(TILES))) for kind in "ht"}
+        diff = tiles("diff", [P, PASS], F32, halves(ON_VECTOR))
+        y_neg = tiles("y_neg", [P, PASS], F32, halves(ON_TENSOR))
+        grad = {kind: tiles("grad_" + kind, [P, PASS], BF16, halves(range(TILES))) for kind in "ht"}
         feat = tiles("feat", [P, M], F32)
         infl = tiles("infl", [P, M], F32)
-        infl_bf = tiles("inflbf", [P, M], BF16)
-        infl_pack = tiles("inflpack", [P, M], BF16)
-        out_codes = sb.tile([P, N], U32, align_bytes=64)
-        out_scales = sb.tile([P, N], U8, align_bytes=64)
+        infl_pairs = tiles("infl_pairs", [P, M], BF16)
+        infl_packed = tiles("infl_packed", [P, M], BF16)
+        out_codes = tile("out_codes", [P, N], U32)
+        out_scales = tile("out_scales", [P, N], U8)
+        warm_in = tile("warm_in", [P, PASS], BF16)
+        warm_codes, warm_scales = tile("warm_codes", [P, P], U32), tile("warm_scales", [P, P], U8)
+        warm_out = tile("warm_out", [P, 1], F32)
         banks = {}
 
-        def load_rows(kind, i):
-            nc.sync.dma_start(out=rows[kind][i][:], in_=src[kind][P * i : P * (i + 1), :])
+        def new_bank(*key):
+            banks[key] = ps.tile([P, PASS], F32, name="bank")
+            return banks[key]
 
-        def load_y(i):
-            nc.sync.dma_start(out=y_rows[i][:], in_=y[P * i : P * (i + 1), :])
+        def span(n, width):
+            return slice(width * n, width * (n + 1))
 
-        def load_w():
-            nc.sync.dma_start(out=w_all[:].bitcast(I32), in_=w_words.bitcast(I32).rearrange("g p n -> p g n"))
+        def by_place(ap):
+            return ap.rearrange("n (q j s) -> n j q s", j=PLACES, q=BLOCKS)
 
-        def load_w_scales():
-            for q in range(4):
-                nc.scalar.dma_start(
-                    out=ws_nat[32 * q : 32 * q + 4, :].bitcast(I32).rearrange("r (g n) -> r g n", g=PASSES),
-                    in_=w_scales[:, 4 * q : 4 * q + 4, :].bitcast(I32).rearrange("g r n -> r g n"),
-                )
-
-        def load_vectors():
-            nc.sync.dma_start(out=r_k[:], in_=r.rearrange("(g p j) -> p g j", g=PASSES, j=4))
-            for first, vec in ((0, c), (4, e)):
-                nc.sync.dma_start(
-                    out=ce_rows[first : first + 4, :].rearrange("j (q s) -> j q s", s=8),
-                    in_=vec.rearrange("(q j s) -> j q s", j=4, s=8),
-                )
-
-        def turn_vectors():
-            bank = new_bank()
-            view = bank[:].bitcast(BF16)
-            for g in range(PASSES):
-                nc.tensor.transpose(view[:, P * g : P * (g + 1)], ce_rows[:, P * g : P * (g + 1)], ident_bf[:])
-            nc.vector.tensor_copy(out=ce_k[:], in_=view[:, 0 : PASSES * P].rearrange("p (g j) -> p g j", g=PASSES)[:, :, 0:8])
-
-        def sort_w(g):
-            nc.vector.tensor_copy(
-                out=w_run[g][:].bitcast(I32).rearrange("p (u j q s) -> p u j q s", u=2, j=4, q=16),
-                in_=w_nat[g].bitcast(I32).rearrange("p (u q j s) -> p u j q s", u=2, j=4, q=16),
-            )
-
-        def sort_w_scales():
-            nc.vector.tensor_copy(
-                out=ws_run[:].bitcast(I32).rearrange("p (u j q s) -> p u j q s", u=4, j=4, q=16),
-                in_=ws_nat[:].bitcast(I32).rearrange("p (u q j s) -> p u j q s", u=4, j=4, q=16),
-            )
-
-        def turn_rows(kind, i):
-            bank = new_bank()
-            banks["rows", kind, i] = bank
-            words = rows[kind][i][:].bitcast(F32)
-            for g in range(PASSES):
-                for u in range(2):
-                    at = P * (2 * g + u)
-                    nc.tensor.transpose(bank[:, at : at + P], words[:, 256 * g + u : 256 * (g + 1) : 2], ident[:])
-
-        def pack_rows(kind, i):
-            nc.scalar.copy(
-                out=packed[kind][i][:].bitcast(F32).rearrange("p (g n u) -> p g n u", g=PASSES, u=2),
-                in_=banks["rows", kind, i][:].rearrange("p (g u n) -> p g n u", g=PASSES, u=2),
-            )
+        def as_sorted(ap):
+            return ap.rearrange("n (j q s) -> n j q s", j=PLACES, q=BLOCKS)
 
         def quantise(codes, scales, values):
             nc.vector.quantize_mx(out=codes.bitcast(FP8X4), scales=scales, in_=values)
 
-        def quantise_rows(kind, i):
-            if kind == "h":
-                quantise(h_codes[i][:], h_scales[i][:], packed["h"][i][:])
-            else:
-                for g in range(PASSES):
-                    cols = slice(P * i, P * (i + 1))
-                    quantise(t_codes[g][:, cols], t_scales[g][:, cols], packed["t"][i][:, BANK * g : BANK * (g + 1)])
+        def mx(out, g, lhs, lhs_scale, rhs, rhs_scale):
+            nc.tensor.matmul_mx(
+                out=out, lhsT=lhs, lhsT_scale=lhs_scale, rhs=rhs, rhs_scale=rhs_scale, start=(g == 0), stop=(g == PASSES - 1)
+            )
 
-        def scale_rows(i):
+        def load_rows(kind, i, cols=slice(0, D)):
+            nc.sync.dma_start(out=rows[kind][i][:, cols], in_=source[kind][span(i, P), cols])
+
+        def load_y(i):
+            nc.sync.dma_start(out=y_rows[i][:], in_=y[span(i, P), :])
+
+        def load_w(u):
+            words = w_words[:, :, span(u, 2 * PASS)].bitcast(I32)
+            nc.sync.dma_start(out=w_given[u][:].bitcast(I32), in_=words.rearrange("g p n -> p g n"))
+
+        def load_w_scales():
+            for quadrant in range(4):
+                nc.sync.dma_start(
+                    out=ws_given[32 * quadrant : 32 * quadrant + 4, :].bitcast(I32).rearrange("s (g n) -> s g n", g=PASSES),
+                    in_=w_scales[:, span(quadrant, 4), :].bitcast(I32).rearrange("g s n -> s g n"),
+                )
+
+        def load_vectors():
+            nc.sync.dma_start(out=r_k[:], in_=r.rearrange("(g p j) -> p g j", g=PASSES, j=PLACES))
+            for n, vector in enumerate((c, e)):
+                nc.sync.dma_start(
+                    out=ce_rows[span(n, PLACES), :].rearrange("j (b s) -> j b s", s=RUN),
+                    in_=vector.rearrange("(b j s) -> j b s", j=PLACES, s=RUN),
+                )
+
+        def warm(passes):
+            bank = new_bank("warm")
+            for n in range(passes):
+                nc.tensor.matmul_mx(
+                    out=bank[:, 0:P], lhsT=warm_codes[:].bitcast(FP8X4), lhsT_scale=warm_scales[:],
+                    rhs=warm_codes[:].bitcast(FP8X4), rhs_scale=warm_scales[:], start=True, stop=True,
+                )
+
+        def sort_w(u):
+            nc.vector.tensor_copy(
+                out=w_sorted[u][:].bitcast(I32).rearrange("p g (j q s) -> p g j q s", j=PLACES, q=BLOCKS),
+                in_=w_given[u][:].bitcast(I32).rearrange("p g (q j s) -> p g j q s", j=PLACES, q=BLOCKS),
+            )
+
+        def sort_w_scales():
+            nc.vector.tensor_copy(
+                out=ws_sorted[:].bitcast(I32).rearrange("p (x j q s) -> p x j q s", x=4, j=PLACES, q=BLOCKS),
+                in_=ws_given[:].bitcast(I32).rearrange("p (x q j s) -> p x j q s", x=4, j=PLACES, q=BLOCKS),
+            )
+
+        def turn_vectors():
+            turned = new_bank("vectors")[:].bitcast(BF16)
+            for u in range(PASSES):
+                nc.tensor.transpose(turned[:, span(u, P)], ce_rows[:, span(u, P)], ident_bf[:])
+            nc.vector.tensor_copy(
+                out=ce_k[:], in_=turned[:, 0 : PASSES * P].rearrange("p (u x) -> p u x", u=PASSES)[:, :, 0 : 2 * PLACES]
+            )
+
+        def pack_rows(kind, i, passes=range(PASSES)):
+            bank = new_bank("rows", kind, i)
+            words = rows[kind][i][:].bitcast(F32)
+            for n, g in enumerate(passes):
+                for pair in range(2):
+                    nc.tensor.transpose(bank[:, span(2 * n + pair, P)], words[:, 256 * g + pair : 256 * (g + 1) : 2], ident[:])
+            nc.scalar.copy(
+                out=packed[kind][i][:, PASS * passes[0] : PASS * (passes[-1] + 1)].bitcast(F32).rearrange("p (g n x) -> p g n x", n=P, x=2),
+                in_=bank[:, 0 : 2 * P * len(passes)].rearrange("p (g x n) -> p g n x", n=P, x=2),
+            )
+
+        def quantise_h(i):
+            quantise(h_codes[i][:], h_scales[i][:], packed["h"][i][:])
+
+        def quantise_h_pass(i, g):
+            quantise(h_codes[i][:, span(g, P)], h_scales[i][:, span(g, P)], packed["h"][i][:, span(g, PASS)])
+
+        def quantise_t(i):
+            for g in range(PASSES):
+                quantise(t_codes[g][:, span(i, P)], t_scales[g][:, span(i, P)], packed["t"][i][:, span(g, PASS)])
+
+        def scale_h(i):
             nc.vector.tensor_tensor(
-                out=hr_pack[i][:].rearrange("p (g n j) -> p g n j", g=PASSES, j=4),
-                in0=packed["h"][i][:].rearrange("p (g n j) -> p g n j", g=PASSES, j=4),
-                in1=r_k[:].unsqueeze(2).to_broadcast([P, PASSES, P, 4]),
+                out=hr_packed[i][:].rearrange("p (g n j) -> p g n j", g=PASSES, j=PLACES),
+                in0=packed["h"][i][:].rearrange("p (g n j) -> p g n j", g=PASSES, j=PLACES),
+                in1=r_k[:].unsqueeze(2).to_broadcast([P, PASSES, P, PLACES]),
                 op=ALU.mult,
             )
 
-        def quantise_scaled(i):
-            quantise(hr_codes[i][:], hr_scales[i][:], hr_pack[i][:])
+        def quantise_hr(i):
+            quantise(hr_codes[i][:], hr_scales[i][:], hr_packed[i][:])
 
-        def logits(kind, i, u):
-            bank = new_bank()
-            banks["logits", kind, i, u] = bank
-            if kind == "h":
+        def sigmoid_a(i):
+            for u in range(PASSES):
+                bank = new_bank("a", i, u)
                 for g in range(PASSES):
-                    nc.tensor.matmul_mx(
-                        out=bank[:],
-                        lhsT=h_codes[i][:, P * g : P * (g + 1)].bitcast(FP8X4),
-                        lhsT_scale=h_scales[i][:, P * g : P * (g + 1)],
-                        rhs=w_nat[g][:, 2 * BANK * u : 2 * BANK * (u + 1)].bitcast(FP4X4),
-                        rhs_scale=ws_nat[:, V * g + BANK * u : V * g + BANK * (u + 1)],
-                        start=(g == 0),
-                        stop=(g == PASSES - 1),
+                    mx(
+                        bank[:], g, h_codes[i][:, span(g, P)].bitcast(FP8X4), h_scales[i][:, span(g, P)],
+                        w_given[u][:, g, :].bitcast(FP4X4), ws_given[:, span(PASSES * g + u, PASS)],
                     )
-            else:
-                for j in range(4):
-                    at = BANK * u + P * j
+                nc.scalar.activation(out=as_sorted(sig["h"][i, u][:]), in_=by_place(bank[:]), func=ACT.Sigmoid)
+
+        def sigmoid_b(i):
+            for u in range(PASSES):
+                bank = new_bank("b", i, u)
+                for j in range(PLACES):
                     for g in range(PASSES):
-                        nc.tensor.matmul_mx(
-                            out=bank[:, P * j : P * (j + 1)],
-                            lhsT=w_run[g][:, 2 * at : 2 * (at + P)].bitcast(FP4X4),
-                            lhsT_scale=ws_run[:, V * g + at : V * g + at + P],
-                            rhs=t_codes[g][:, P * i : P * (i + 1)].bitcast(FP8X4),
-                            rhs_scale=t_scales[g][:, P * i : P * (i + 1)],
-                            start=(g == 0),
-                            stop=(g == PASSES - 1),
+                        mx(
+                            bank[:, span(j, P)], g, w_sorted[u][:, g, span(j, 2 * P)].bitcast(FP4X4),
+                            ws_sorted[:, span(PLACES * (PASSES * g + u) + j, P)],
+                            t_codes[g][:, span(i, P)].bitcast(FP8X4), t_scales[g][:, span(i, P)],
+                        )
+                nc.scalar.activation(
+                    out=sig["t"][i, u][:].rearrange("p (m j) -> p m j", j=PLACES),
+                    in_=bank[:].rearrange("p (j m) -> p m j", j=PLACES),
+                    func=ACT.Sigmoid,
+                )
+
+        def subtract_y(i):
+            for u in range(PASSES):
+                nc.vector.tensor_tensor(
+                    out=as_sorted(diff[i, u][:]), in0=as_sorted(sig["h"][i, u][:]), in1=by_place(y_rows[i][:, span(u, PASS)]),
+                    op=ALU.subtract,
+                )
+
+        def negate_y(i):
+            for u in range(PASSES):
+                nc.scalar.activation(
+                    out=as_sorted(y_neg[i, u][:]), in_=by_place(y_rows[i][:, span(u, PASS)]), func=ACT.Copy, scale=-1.0
+                )
+
+        def turn_diff(i):
+            for u in range(PASSES):
+                bank = new_bank("diff", i, u)
+                for j in range(PLACES):
+                    nc.tensor.transpose(bank[:, span(j, P)], diff[i, u][:, span(j, P)], ident[:])
+
+        def turn_and_subtract(i):
+            for u in range(PASSES):
+                bank = new_bank("diff", i, u)
+                for j in range(PLACES):
+                    for term, first in ((y_neg[i, u], True), (sig["h"][i, u], False)):
+                        nc.tensor.matmul(
+                            bank[:, span(j, P)], lhsT=term[:, span(j, P)], rhs=ident[:], is_transpose=True, start=first, stop=not first
                         )
 
-        def sigmoid(kind, i, u):
-            bank = banks["logits", kind, i, u]
-            if kind == "h":
-                out = sig["h"][2 * i + u][:].rearrange("n (j q s) -> n j q s", j=4, q=16)
-                in_ = bank[:].rearrange("n (q j s) -> n j q s", j=4, q=16)
-            else:
-                out = sig["t"][2 * i + u][:].rearrange("p (m j) -> p m j", j=4)
-                in_ = bank[:].rearrange("p (j m) -> p m j", j=4)
-            nc.scalar.activation(out=out, in_=in_, func=ACT.Sigmoid)
-
-        def negate_y(i, u):
-            nc.scalar.activation(
-                out=y_neg[i][:, BANK * u : BANK * (u + 1)].rearrange("n (j q s) -> n j q s", j=4, q=16),
-                in_=y_rows[i][:, BANK * u : BANK * (u + 1)].rearrange("n (q j s) -> n j q s", j=4, q=16),
-                func=ACT.Copy, scale=-1.0,
-            )
-
-        def subtract_y(i, u, eng):
-            eng.tensor_tensor(
-                out=diff[2 * i + u][:].rearrange("n (j q s) -> n j q s", j=4, q=16),
-                in0=sig["h"][2 * i + u][:].rearrange("n (j q s) -> n j q s", j=4, q=16),
-                in1=y_rows[i][:, BANK * u : BANK * (u + 1)].rearrange("n (q j s) -> n j q s", j=4, q=16),
-                op=ALU.subtract,
-            )
-
-        def turn_diff(i, u):
-            bank = new_bank()
-            banks["diff", i, u] = bank
-            for j in range(4):
-                cols = slice(P * j, P * (j + 1))
-                nc.tensor.transpose(bank[:, cols], diff[2 * i + u][:, cols], ident[:])
-
-        def turn_and_subtract(i, u):
-            bank = new_bank()
-            banks["diff", i, u] = bank
-            for j in range(4):
-                cols = slice(P * j, P * (j + 1))
-                at = BANK * u + P * j
-                nc.tensor.matmul(bank[:, cols], lhsT=y_neg[i][:, at : at + P], rhs=ident[:], is_transpose=True, start=True, stop=False)
-                nc.tensor.matmul(bank[:, cols], lhsT=sig["h"][2 * i + u][:, cols], rhs=ident[:], is_transpose=True, start=False, stop=True)
-
-        def weigh(kind, i, u):
-            if kind == "h":
-                in0 = banks["diff", i, u][:].rearrange("p (j n) -> p n j", j=4)
-                factor = ce_k[:, u, 0:4]
-            else:
-                in0 = sig["t"][2 * i + u][:].rearrange("p (m j) -> p m j", j=4)
-                factor = ce_k[:, u, 4:8]
+        def times_vector(out, values, factor):
             nc.vector.tensor_tensor(
-                out=grad[kind][2 * i + u][:].rearrange("p (n j) -> p n j", j=4),
-                in0=in0,
-                in1=factor.unsqueeze(1).to_broadcast([P, P, 4]),
+                out=out.rearrange("p (n j) -> p n j", j=PLACES), in0=values, in1=factor.unsqueeze(1).to_broadcast([P, P, PLACES]),
                 op=ALU.mult,
             )
 
-        def quantise_grad(kind, i, u):
-            if kind == "h":
-                cols = slice(P * u, P * (u + 1))
-                quantise(ga_codes[i][:, cols], ga_scales[i][:, cols], grad["h"][2 * i + u][:])
-            else:
-                cols = slice(P * i, P * (i + 1))
-                quantise(gb_codes[u][:, cols], gb_scales[u][:, cols], grad["t"][2 * i + u][:])
+        def make_ga(i):
+            for u in range(PASSES):
+                turned = banks["diff", i, u][:].rearrange("p (j n) -> p n j", j=PLACES)
+                times_vector(grad["h"][i, u][:], turned, ce_k[:, u, span(0, PLACES)])
 
-        def gram_pass(bank, g, codes, scales, moving_codes, moving_scales):
-            nc.tensor.matmul_mx(
-                out=bank[:],
-                lhsT=codes[:, P * g : P * (g + 1)].bitcast(FP8X4),
-                lhsT_scale=scales[:, P * g : P * (g + 1)],
-                rhs=moving_codes[g][:].bitcast(FP8X4),
-                rhs_scale=moving_scales[g][:],
-                start=(g == 0),
-                stop=(g == PASSES - 1),
-            )
+        def make_gb(i):
+            for u in range(PASSES):
+                values = sig["t"][i, u][:].rearrange("p (m j) -> p m j", j=PLACES)
+                times_vector(grad["t"][i, u][:], values, ce_k[:, u, span(1, PLACES)])
+
+        def quantise_ga(i):
+            for u in range(PASSES):
+                quantise(ga_codes[i][:, span(u, P)], ga_scales[i][:, span(u, P)], grad["h"][i, u][:])
+
+        def quantise_gb(i):
+            for u in range(PASSES):
+                quantise(gb_codes[u][:, span(i, P)], gb_scales[u][:, span(i, P)], grad["t"][i, u][:])
+
+        def gram(name, i, codes, scales, moving_codes, moving_scales):
+            bank = new_bank(name, i)
+            for g in range(PASSES):
+                mx(
+                    bank[:], g, codes[i][:, span(g, P)].bitcast(FP8X4), scales[i][:, span(g, P)],
+                    moving_codes[g][:].bitcast(FP8X4), moving_scales[g][:],
+                )
 
         def feat_gram(i):
-            bank = new_bank()
-            banks["feat", i] = bank
-            for g in range(PASSES):
-                gram_pass(bank, g, hr_codes[i], hr_scales[i], t_codes, t_scales)
+            gram("feat", i, hr_codes, hr_scales, t_codes, t_scales)
+
+        def logit_gram(i):
+            gram("logit", i, ga_codes, ga_scales, gb_codes, gb_scales)
 
         def keep_feat(i):
             nc.scalar.activation(out=feat[i][:], in_=banks["feat", i][:], func=ACT.Copy, scale=LEARNING_RATE)
 
-        def logit_gram(i):
-            bank = new_bank()
-            banks["logit_gram", i] = bank
-            for g in range(PASSES):
-                gram_pass(bank, g, ga_codes[i], ga_scales[i], gb_codes, gb_scales)
-
         def influence(i):
-            nc.vector.tensor_tensor(out=infl[i][:], in0=feat[i][:], in1=banks["logit_gram", i][:], op=ALU.mult)
+            nc.vector.tensor_tensor(out=infl[i][:], in0=feat[i][:], in1=banks["logit", i][:], op=ALU.mult)
+            nc.sync.dma_start(out=out_0[span(i, P), :], in_=infl[i][:])
 
-        def store_influence(i):
-            nc.sync.dma_start(out=out_0[P * i : P * (i + 1), :], in_=infl[i][:])
+        def by_pair(ap):
+            return ap.rearrange("n (p x z) -> n x p z", x=2, z=2)
+
+        def pairs(i):
+            return infl_pairs[i][:].rearrange("n (x p z) -> n x p z", x=2, z=2)
 
         def round_influence(i, copy):
-            copy(
-                out=infl_bf[i][:].rearrange("n (u p s) -> n u p s", u=2, s=2),
-                in_=infl[i][:].rearrange("n (p u s) -> n u p s", u=2, s=2),
-            )
+            copy(out=pairs(i), in_=by_pair(infl[i][:]))
 
-        def influence_rounded(i):
-            nc.vector.tensor_tensor(
-                out=infl_bf[i][:].rearrange("n (u p s) -> n u p s", u=2, s=2),
-                in0=feat[i][:].rearrange("n (p u s) -> n u p s", u=2, s=2),
-                in1=banks["logit_gram", i][:].rearrange("n (p u s) -> n u p s", u=2, s=2),
-                op=ALU.mult,
-            )
+        def rounded_influence(i):
+            nc.vector.tensor_tensor(out=pairs(i), in0=by_pair(feat[i][:]), in1=by_pair(banks["logit", i][:]), op=ALU.mult)
 
         def turn_influence(i):
-            bank = new_bank()
-            banks["infl", i] = bank
-            words = infl_bf[i][:].bitcast(F32)
-            for u in range(2):
-                nc.tensor.transpose(bank[:, P * u : P * (u + 1)], words[:, P * u : P * (u + 1)], ident[:])
+            bank = new_bank("infl", i)
+            words = infl_pairs[i][:].bitcast(F32)
+            for pair in range(2):
+                nc.tensor.transpose(bank[:, span(pair, P)], words[:, span(pair, P)], ident[:])
 
-        def pack_influence(i, eng=None):
-            out = infl_pack[i][:].bitcast(F32).rearrange("p (n u) -> p n u", u=2)
-            in_ = banks["infl", i][:, 0 : 2 * P].rearrange("p (u n) -> p n u", u=2)
-            if eng is None:
-                nc.scalar.copy(out=out, in_=in_)
-            else:
-                eng.tensor_copy(out=out, in_=in_)
+        def pack_influence(i):
+            nc.scalar.copy(
+                out=infl_packed[i][:].bitcast(F32).rearrange("p (n x) -> p n x", x=2),
+                in_=banks["infl", i][:, 0 : 2 * P].rearrange("p (x n) -> p n x", x=2),
+            )
 
         def quantise_influence(i):
-            quantise(out_codes[:, P * i : P * (i + 1)], out_scales[:, P * i : P * (i + 1)], infl_pack[i][:])
+            quantise(out_codes[:, span(i, P)], out_scales[:, span(i, P)], infl_packed[i][:])
 
-        def store_codes(first, last):
-            words = out_1[0].rearrange("p m j -> p (m j)").bitcast(I32)
-            nc.sync.dma_start(out=words[:, P * first : P * last], in_=out_codes[:, P * first : P * last].bitcast(I32))
+        def store_codes(half):
+            words = out_1[0].rearrange("p n j -> p (n j)").bitcast(I32)
+            nc.sync.dma_start(out=words[:, span(half, N // 2)], in_=out_codes[:, span(half, N // 2)].bitcast(I32))
 
         def store_scales():
-            for q in range(4):
-                queue = nc.sync if q % 2 == 0 else nc.scalar
+            for quadrant in range(4):
+                queue = (nc.sync, nc.scalar)[quadrant % 2]
                 queue.dma_start(
-                    out=out_2[0, 4 * q : 4 * q + 4, :].bitcast(I32),
-                    in_=out_scales[32 * q : 32 * q + 4, :].bitcast(I32),
+                    out=out_2[0, span(quadrant, 4), :].bitcast(I32),
+                    in_=out_scales[32 * quadrant : 32 * quadrant + 4, :].bitcast(I32),
                 )
 
-        def setup():
-            nc.gpsimd.memset(ws_nat[:].bitcast(I32), 0)
-            make_identity(nc, ident[:])
-            nc.vector.memset(ce_rows[:], 0.0)
-            nc.vector.tensor_copy(out=ident_bf[:], in_=ident[:])
+        nc.vector.memset(warm_in[:], 1.0)
+        quantise(warm_codes[:], warm_scales[:], warm_in[:])
+        nc.gpsimd.memset(ws_given[:].bitcast(I32), 0)
+        make_identity(nc, ident[:])
+        nc.vector.memset(ce_rows[:], 0.0)
+        nc.vector.tensor_copy(out=ident_bf[:], in_=ident[:])
+        nc.scalar.activation(out=warm_out[:], in_=warm_in[:, 0:1], func=ACT.Sigmoid)
 
-        warm_in = sb.tile([P, BANK], BF16, align_bytes=64)
-        warm_codes = sb.tile([P, P], U32, align_bytes=64)
-        warm_scales = sb.tile([P, P], U8, align_bytes=64)
-        warm_act = sb.tile([P, 8], F32, align_bytes=64)
-
-        def warm_setup():
-            nc.vector.memset(warm_in[:], 1.0)
-            quantise(warm_codes[:], warm_scales[:], warm_in[:])
-
-        def warm_table():
-            nc.scalar.activation(out=warm_act[:, 0:1], in_=warm_in[:, 0:1], func=ACT.Sigmoid)
-
-        def warm(count):
-            bank = new_bank()
-            for k in range(count):
-                nc.tensor.matmul_mx(
-                    out=bank[:, 0:P], lhsT=warm_codes[:, 0:P].bitcast(FP8X4), lhsT_scale=warm_scales[:, 0:P],
-                    rhs=warm_codes[:].bitcast(FP8X4), rhs_scale=warm_scales[:], start=True, stop=True,
-                )
-
-        warm_setup()
-        setup()
+        for g in range(PASSES):
+            load_rows("h", 0, span(g, PASS))
         load_w_scales()
-        warm_table()
-        load_rows("h", 0)
         load_rows("t", 0)
-        load_w()
-        load_vectors()
+        for u in range(PASSES):
+            load_w(u)
         load_rows("h", 1)
         load_rows("t", 1)
         load_y(0)
+        load_vectors()
         load_rows("t", 2)
         load_rows("t", 3)
         load_y(1)
-        load_y(2)
-        load_rows("h", 2)
-        load_rows("h", 3)
-        load_y(3)
-        warm(14)
-        turn_rows("h", 0)
-        pack_rows("h", 0)
-        turn_rows("t", 0)
+        for i in ON_TENSOR:
+            load_rows("h", i)
+            load_y(i)
+
+        warm(WARM_PASSES[0])
+        for g in range(PASSES):
+            pack_rows("h", 0, [g])
+        warm(WARM_PASSES[1])
         pack_rows("t", 0)
-        warm(12)
-        quantise_rows("h", 0)
-        sort_w(0)
-        sort_w(1)
+        warm(WARM_PASSES[2])
+        for g in range(PASSES):
+            quantise_h_pass(0, g)
         sort_w_scales()
-        quantise_rows("t", 0)
-        logits("h", 0, 0)
-        sigmoid("h", 0, 0)
-        logits("h", 0, 1)
-        sigmoid("h", 0, 1)
-        scale_rows(0)
-        turn_vectors()
-        turn_rows("h", 1)
+        for u in range(PASSES):
+            sort_w(u)
+        quantise_t(0)
+        sigmoid_a(0)
+
         pack_rows("h", 1)
-        turn_rows("t", 1)
         pack_rows("t", 1)
-        quantise_scaled(0)
-        subtract_y(0, 0, nc.vector)
-        subtract_y(0, 1, nc.vector)
-        quantise_rows("h", 1)
-        quantise_rows("t", 1)
-        logits("t", 0, 0)
-        sigmoid("t", 0, 0)
-        logits("t", 0, 1)
-        sigmoid("t", 0, 1)
-        turn_diff(0, 0)
-        turn_diff(0, 1)
-        turn_rows("t", 2)
+        subtract_y(0)
+        quantise_h(1)
+        scale_h(0)
+        quantise_t(1)
+        quantise_hr(0)
+        sigmoid_b(0)
+        turn_vectors()
+        sigmoid_a(1)
+
+        turn_diff(0)
         pack_rows("t", 2)
-        turn_rows("t", 3)
         pack_rows("t", 3)
-        scale_rows(1)
-        weigh("t", 0, 0)
-        weigh("t", 0, 1)
-        weigh("h", 0, 0)
-        weigh("h", 0, 1)
-        quantise_grad("t", 0, 0)
-        quantise_grad("t", 0, 1)
-        quantise_rows("t", 2)
-        quantise_grad("h", 0, 0)
-        quantise_grad("h", 0, 1)
-        quantise_rows("t", 3)
-        quantise_scaled(1)
-        logits("h", 1, 0)
-        sigmoid("h", 1, 0)
-        logits("h", 1, 1)
-        sigmoid("h", 1, 1)
-        negate_y(2, 0)
-        turn_rows("h", 2)
+        make_gb(0)
+        subtract_y(1)
+        make_ga(0)
+        quantise_t(2)
+        quantise_t(3)
+        quantise_gb(0)
+        quantise_ga(0)
+        sigmoid_b(1)
+        negate_y(2)
+
+        turn_diff(1)
         pack_rows("h", 2)
-        subtract_y(1, 0, nc.vector)
-        subtract_y(1, 1, nc.vector)
-        quantise_rows("h", 2)
-        logits("t", 1, 0)
-        sigmoid("t", 1, 0)
-        logits("t", 1, 1)
-        sigmoid("t", 1, 1)
-        negate_y(2, 1)
-        turn_diff(1, 0)
-        turn_diff(1, 1)
-        turn_rows("h", 3)
         pack_rows("h", 3)
-        weigh("t", 1, 0)
-        weigh("t", 1, 1)
-        scale_rows(2)
-        quantise_grad("t", 1, 0)
-        quantise_grad("t", 1, 1)
-        weigh("h", 1, 0)
-        weigh("h", 1, 1)
-        quantise_rows("h", 3)
-        quantise_scaled(2)
-        quantise_grad("h", 1, 0)
-        quantise_grad("h", 1, 1)
-        logits("t", 2, 0)
-        sigmoid("t", 2, 0)
-        logits("t", 2, 1)
-        sigmoid("t", 2, 1)
-        negate_y(3, 0)
-        feat_gram(0)
-        keep_feat(0)
-        weigh("t", 2, 0)
-        weigh("t", 2, 1)
-        scale_rows(3)
-        quantise_grad("t", 2, 0)
-        quantise_grad("t", 2, 1)
-        quantise_scaled(3)
-        logits("t", 3, 0)
-        sigmoid("t", 3, 0)
-        logits("t", 3, 1)
-        sigmoid("t", 3, 1)
-        negate_y(3, 1)
-        weigh("t", 3, 0)
-        weigh("t", 3, 1)
-        quantise_grad("t", 3, 0)
-        quantise_grad("t", 3, 1)
-        logits("h", 2, 0)
-        sigmoid("h", 2, 0)
-        logits("h", 2, 1)
-        sigmoid("h", 2, 1)
-        logits("h", 3, 0)
-        sigmoid("h", 3, 0)
-        logits("h", 3, 1)
-        sigmoid("h", 3, 1)
-        feat_gram(1)
-        keep_feat(1)
-        turn_and_subtract(2, 0)
-        turn_and_subtract(2, 1)
-        weigh("h", 2, 0)
-        weigh("h", 2, 1)
-        turn_and_subtract(3, 0)
-        turn_and_subtract(3, 1)
+        scale_h(1)
+        make_gb(1)
+        make_ga(1)
+        quantise_h(2)
+        quantise_h(3)
+        quantise_hr(1)
+        quantise_gb(1)
+        quantise_ga(1)
+        sigmoid_b(2)
+        negate_y(3)
+        sigmoid_b(3)
+        scale_h(2)
+        make_gb(2)
+        quantise_hr(2)
+        scale_h(3)
+        quantise_gb(2)
+        make_gb(3)
+        quantise_hr(3)
+        quantise_gb(3)
+        for i in ON_TENSOR:
+            sigmoid_a(i)
+        for i in ON_VECTOR:
+            feat_gram(i)
+            keep_feat(i)
+
+        turn_and_subtract(2)
+        make_ga(2)
+        turn_and_subtract(3)
         logit_gram(0)
-        quantise_grad("h", 2, 0)
-        quantise_grad("h", 2, 1)
-        weigh("h", 3, 0)
-        weigh("h", 3, 1)
         feat_gram(2)
         keep_feat(2)
-        influence(0)
-        store_influence(0)
-        feat_gram(3)
-        keep_feat(3)
         logit_gram(1)
-        quantise_grad("h", 3, 0)
-        quantise_grad("h", 3, 1)
+        feat_gram(3)
+        quantise_ga(2)
+        make_ga(3)
+        influence(0)
         round_influence(0, nc.scalar.copy)
+        keep_feat(3)
+        quantise_ga(3)
         influence(1)
-        store_influence(1)
+        round_influence(1, nc.scalar.copy)
         logit_gram(2)
         logit_gram(3)
-        round_influence(1, nc.scalar.copy)
+
         influence(2)
-        store_influence(2)
         turn_influence(0)
         pack_influence(0)
-        influence_rounded(3)
+        rounded_influence(3)
         turn_influence(1)
         pack_influence(1)
         round_influence(2, nc.vector.tensor_copy)
         influence(3)
-        store_influence(3)
-        turn_influence(3)
-        turn_influence(2)
-        pack_influence(3)
-        pack_influence(2)
-        quantise_influence(0)
-        quantise_influence(1)
-        store_codes(0, 2)
-        quantise_influence(3)
-        quantise_influence(2)
-        store_codes(2, 4)
+        for i in (3, 2):
+            turn_influence(i)
+        for i in (3, 2):
+            pack_influence(i)
+        for half, row_tiles in enumerate(((0, 1), (3, 2))):
+            for i in row_tiles:
+                quantise_influence(i)
+            store_codes(half)
         store_scales()

@@ -27,7 +27,7 @@ BLOCKS = 16
 BANKS = 8
 ON_VECTOR = (0, 1)
 ON_TENSOR = (2, 3)
-WARM_PASSES = (14, 6, 4)
+WARM_PASSES = (12, 4)
 
 
 def tile_tracinonevsallheadinfluence_x2_kernel(tc, h, t, w_words, w_scales, y, c, e, r, out_0, out_1, out_2):
@@ -324,9 +324,9 @@ def tile_tracinonevsallheadinfluence_x2_kernel(tc, h, t, w_words, w_scales, y, c
                     in_=out_scales[32 * quadrant : 32 * quadrant + 4, :].bitcast(I32),
                 )
 
-        nc.vector.memset(warm_in[:], 1.0)
-        quantise(warm_codes[:], warm_scales[:], warm_in[:])
+        nc.gpsimd.memset(warm_in[:].bitcast(I32), 0)
         nc.gpsimd.memset(ws_given[:].bitcast(I32), 0)
+        quantise(warm_codes[:], warm_scales[:], warm_in[:])
         make_identity(nc, ident[:])
         nc.vector.memset(ce_rows[:], 0.0)
         nc.vector.tensor_copy(out=ident_bf[:], in_=ident[:])
@@ -354,7 +354,6 @@ def tile_tracinonevsallheadinfluence_x2_kernel(tc, h, t, w_words, w_scales, y, c
             pack_rows("h", 0, [g])
         warm(WARM_PASSES[1])
         pack_rows("t", 0)
-        warm(WARM_PASSES[2])
         for g in range(PASSES):
             quantise_h_pass(0, g)
         sort_w_scales()

@@ -27,7 +27,6 @@ BLOCKS = 16
 BANKS = 8
 ON_VECTOR = (0, 1)
 ON_TENSOR = (2, 3)
-WARM_PASSES = (12, 4)
 
 
 def tile_tracinonevsallheadinfluence_x2_kernel(tc, h, t, w_words, w_scales, y, c, e, r, out_0, out_1, out_2):
@@ -75,9 +74,6 @@ def tile_tracinonevsallheadinfluence_x2_kernel(tc, h, t, w_words, w_scales, y, c
         infl_packed = tiles("infl_packed", [P, M], BF16)
         out_codes = tile("out_codes", [P, N], U32)
         out_scales = tile("out_scales", [P, N], U8)
-        warm_in = tile("warm_in", [P, PASS], BF16)
-        warm_codes, warm_scales = tile("warm_codes", [P, P], U32), tile("warm_scales", [P, P], U8)
-        warm_out = tile("warm_out", [P, 1], F32)
         banks = {}
 
         def new_bank(*key):
@@ -126,14 +122,6 @@ def tile_tracinonevsallheadinfluence_x2_kernel(tc, h, t, w_words, w_scales, y, c
                     in_=vector.rearrange("(b j s) -> j b s", j=PLACES, s=RUN),
                 )
 
-        def warm(passes):
-            bank = new_bank("warm")
-            for n in range(passes):
-                nc.tensor.matmul_mx(
-                    out=bank[:, 0:P], lhsT=warm_codes[:].bitcast(FP8X4), lhsT_scale=warm_scales[:],
-                    rhs=warm_codes[:].bitcast(FP8X4), rhs_scale=warm_scales[:], start=True, stop=True,
-                )
-
         def sort_w(u):
             nc.vector.tensor_copy(
                 out=w_sorted[u][:].bitcast(I32).rearrange("p g (j q s) -> p g j q s", j=PLACES, q=BLOCKS),
@@ -154,13 +142,13 @@ def tile_tracinonevsallheadinfluence_x2_kernel(tc, h, t, w_words, w_scales, y, c
                 out=ce_k[:], in_=turned[:, 0 : PASSES * P].rearrange("p (u x) -> p u x", u=PASSES)[:, :, 0 : 2 * PLACES]
             )
 
-        def pack_rows(kind, i, passes=range(PASSES)):
+        def pack_rows(kind, i, passes=range(PASSES), copy=nc.scalar.copy):
             bank = new_bank("rows", kind, i)
             words = rows[kind][i][:].bitcast(F32)
             for n, g in enumerate(passes):
                 for pair in range(2):
                     nc.tensor.transpose(bank[:, span(2 * n + pair, P)], words[:, 256 * g + pair : 256 * (g + 1) : 2], ident[:])
-            nc.scalar.copy(
+            copy(
                 out=packed[kind][i][:, PASS * passes[0] : PASS * (passes[-1] + 1)].bitcast(F32).rearrange("p (g n x) -> p g n x", n=P, x=2),
                 in_=bank[:, 0 : 2 * P * len(passes)].rearrange("p (g x n) -> p g n x", n=P, x=2),
             )
@@ -324,13 +312,10 @@ def tile_tracinonevsallheadinfluence_x2_kernel(tc, h, t, w_words, w_scales, y, c
                     in_=out_scales[32 * quadrant : 32 * quadrant + 4, :].bitcast(I32),
                 )
 
-        nc.gpsimd.memset(warm_in[:].bitcast(I32), 0)
         nc.gpsimd.memset(ws_given[:].bitcast(I32), 0)
-        quantise(warm_codes[:], warm_scales[:], warm_in[:])
         make_identity(nc, ident[:])
         nc.vector.memset(ce_rows[:], 0.0)
         nc.vector.tensor_copy(out=ident_bf[:], in_=ident[:])
-        nc.scalar.activation(out=warm_out[:], in_=warm_in[:, 0:1], func=ACT.Sigmoid)
 
         for g in range(PASSES):
             load_rows("h", 0, span(g, PASS))
@@ -349,13 +334,11 @@ def tile_tracinonevsallheadinfluence_x2_kernel(tc, h, t, w_words, w_scales, y, c
             load_rows("h", i)
             load_y(i)
 
-        warm(WARM_PASSES[0])
         for g in range(PASSES):
-            pack_rows("h", 0, [g])
-        warm(WARM_PASSES[1])
-        pack_rows("t", 0)
+            pack_rows("h", 0, [g], nc.vector.tensor_copy)
         for g in range(PASSES):
             quantise_h_pass(0, g)
+        pack_rows("t", 0, copy=nc.vector.tensor_copy)
         sort_w_scales()
         for u in range(PASSES):
             sort_w(u)

from contextlib import ExitStack

import concourse.mybir as mybir
from concourse.masks import make_identity

N, M, D, V = 512, 512, 1024, 1024
LEARNING_RATE = 1.0 / 256.0
FLOPS = 2 * (N + M) * D * V + 2 * N * M * (V + D)

F32 = mybir.dt.float32
BF16 = mybir.dt.bfloat16
I32 = mybir.dt.int32
U32 = mybir.dt.uint32
U8 = mybir.dt.uint8
FP8X4 = mybir.dt.float8_e4m3fn_x4
FP4X4 = mybir.dt.float4_e2m1fn_x4
ACT = mybir.ActivationFunctionType
ALU = mybir.AluOpType

P = 128
TILES = 4
PASSES = 2
PASS = 512
PLACES = 4
RUN = 8
BLOCKS = 16
BANKS = 8
ON_VECTOR = (0, 1)
ON_TENSOR = (2, 3)


def tile_tracinonevsallheadinfluence_x2_kernel(tc, h, t, w_words, w_scales, y, c, e, r, out_0, out_1, out_2):
    nc = tc.nc
    with ExitStack() as ctx:
        sb = ctx.enter_context(tc.tile_pool(name="sb", bufs=1))
        ps = ctx.enter_context(tc.psum_pool(name="ps", bufs=BANKS))
        ctx.enter_context(tc.manual_schedule())

        def tile(name, shape, dtype):
            return sb.tile(shape, dtype, name=name, align_bytes=64)

        def tiles(name, shape, dtype, keys=range(TILES)):
            return {key: tile(name + str(n), shape, dtype) for n, key in enumerate(keys)}

        def halves(row_tiles):
            return [(i, u) for i in row_tiles for u in range(PASSES)]

        source = {"h": h, "t": t}
        rows = {"h": tiles("h", [P, D], BF16), "t": tiles("t", [P, D], BF16)}
        y_rows = tiles("y", [P, V], BF16)
        w_given = tiles("w_given", [P, PASSES, 2 * PASS], U8, range(PASSES))
        w_sorted = tiles("w_sorted", [P, PASSES, 2 * PASS], U8, range(PASSES))
        ws_given = tile("ws_given", [P, PASSES * V], U8)
        ws_sorted = tile("ws_sorted", [P, PASSES * V], U8)
        r_k = tile("r_k", [P, PASSES, PLACES], BF16)
        ce_rows = tile("ce_rows", [P, PASSES * P], BF16)
        ce_k = tile("ce_k", [P, PASSES, 2 * PLACES], BF16)
        ident = tile("ident", [P, P], F32)
        ident_bf = tile("ident_bf", [P, P], BF16)
        packed = {"h": tiles("h_packed", [P, D], BF16), "t": tiles("t_packed", [P, D], BF16)}
        hr_packed = tiles("hr_packed", [P, D], BF16)
        h_codes, h_scales = tiles("h_codes", [P, PASSES * P], U32), tiles("h_scales", [P, PASSES * P], U8)
        hr_codes, hr_scales = tiles("hr_codes", [P, PASSES * P], U32), tiles("hr_scales", [P, PASSES * P], U8)
        ga_codes, ga_scales = tiles("ga_codes", [P, PASSES * P], U32), tiles("ga_scales", [P, PASSES * P], U8)
        t_codes, t_scales = tiles("t_codes", [P, M], U32, range(PASSES)), tiles("t_scales", [P, M], U8, range(PASSES))
        gb_codes, gb_scales = tiles("gb_codes", [P, M], U32, range(PASSES)), tiles("gb_scales", [P, M], U8, range(PASSES))
        sig = {kind: tiles("sig_" + kind, [P, PASS], F32, halves(range(TILES))) for kind in "ht"}
        diff = tiles("diff", [P, PASS], F32, halves(ON_VECTOR))
        y_neg = tiles("y_neg", [P, PASS], F32, halves(ON_TENSOR))
        grad = {kind: tiles("grad_" + kind, [P, PASS], BF16, halves(range(TILES))) for kind in "ht"}
        feat = tiles("feat", [P, M], F32)
        infl = tiles("infl", [P, M], F32)
        infl_pairs = tiles("infl_pairs", [P, M], BF16)
        infl_packed = tiles("infl_packed", [P, M], BF16)
        out_codes = tile("out_codes", [P, N], U32)
        out_scales = tile("out_scales", [P, N], U8)
        banks = {}

        def new_bank(*key):
            banks[key] = ps.tile([P, PASS], F32, name="bank")
            return banks[key]

        def span(n, width):
            return slice(width * n, width * (n + 1))

        def by_place(ap):
            return ap.rearrange("n (q j s) -> n j q s", j=PLACES, q=BLOCKS)

        def as_sorted(ap):
            return ap.rearrange("n (j q s) -> n j q s", j=PLACES, q=BLOCKS)

        def quantise(codes, scales, values):
            nc.vector.quantize_mx(out=codes.bitcast(FP8X4), scales=scales, in_=values)

        def mx(out, g, lhs, lhs_scale, rhs, rhs_scale):
            nc.tensor.matmul_mx(
                out=out, lhsT=lhs, lhsT_scale=lhs_scale, rhs=rhs, rhs_scale=rhs_scale, start=(g == 0), stop=(g == PASSES - 1)
            )

        def load_rows(kind, i, cols=slice(0, D)):
            nc.sync.dma_start(out=rows[kind][i][:, cols], in_=source[kind][span(i, P), cols])

        def load_y(i):
            nc.sync.dma_start(out=y_rows[i][:], in_=y[span(i, P), :])

        def load_w(u):
            words = w_words[:, :, span(u, 2 * PASS)].bitcast(I32)
            nc.sync.dma_start(out=w_given[u][:].bitcast(I32), in_=words.rearrange("g p n -> p g n"))

        def load_w_scales():
            for quadrant in range(4):
                nc.sync.dma_start(
                    out=ws_given[32 * quadrant : 32 * quadrant + 4, :].bitcast(I32).rearrange("s (g n) -> s g n", g=PASSES),
                    in_=w_scales[:, span(quadrant, 4), :].bitcast(I32).rearrange("g s n -> s g n"),
                )

        def load_vectors():
            nc.sync.dma_start(out=r_k[:], in_=r.rearrange("(g p j) -> p g j", g=PASSES, j=PLACES))
            for n, vector in enumerate((c, e)):
                nc.sync.dma_start(
                    out=ce_rows[span(n, PLACES), :].rearrange("j (b s) -> j b s", s=RUN),
                    in_=vector.rearrange("(b j s) -> j b s", j=PLACES, s=RUN),
                )

        def sort_w(u):
            nc.vector.tensor_copy(
                out=w_sorted[u][:].bitcast(I32).rearrange("p g (j q s) -> p g j q s", j=PLACES, q=BLOCKS),
                in_=w_given[u][:].bitcast(I32).rearrange("p g (q j s) -> p g j q s", j=PLACES, q=BLOCKS),
            )

        def sort_w_scales():
            nc.vector.tensor_copy(
                out=ws_sorted[:].bitcast(I32).rearrange("p (x j q s) -> p x j q s", x=4, j=PLACES, q=BLOCKS),
                in_=ws_given[:].bitcast(I32).rearrange("p (x q j s) -> p x j q s", x=4, j=PLACES, q=BLOCKS),
            )

        def turn_vectors():
            turned = new_bank("vectors")[:].bitcast(BF16)
            for u in range(PASSES):
                nc.tensor.transpose(turned[:, span(u, P)], ce_rows[:, span(u, P)], ident_bf[:])
            nc.vector.tensor_copy(
                out=ce_k[:], in_=turned[:, 0 : PASSES * P].rearrange("p (u x) -> p u x", u=PASSES)[:, :, 0 : 2 * PLACES]
            )

        def pack_rows(kind, i, passes=range(PASSES), copy=nc.scalar.copy):
            bank = new_bank("rows", kind, i)
            words = rows[kind][i][:].bitcast(F32)
            for n, g in enumerate(passes):
                for pair in range(2):
                    nc.tensor.transpose(bank[:, span(2 * n + pair, P)], words[:, 256 * g + pair : 256 * (g + 1) : 2], ident[:])
            copy(
                out=packed[kind][i][:, PASS * passes[0] : PASS * (passes[-1] + 1)].bitcast(F32).rearrange("p (g n x) -> p g n x", n=P, x=2),
                in_=bank[:, 0 : 2 * P * len(passes)].rearrange("p (g x n) -> p g n x", n=P, x=2),
            )

        def quantise_h(i):
            quantise(h_codes[i][:], h_scales[i][:], packed["h"][i][:])

        def quantise_h_pass(i, g):
            quantise(h_codes[i][:, span(g, P)], h_scales[i][:, span(g, P)], packed["h"][i][:, span(g, PASS)])

        def quantise_t(i):
            for g in range(PASSES):
                quantise(t_codes[g][:, span(i, P)], t_scales[g][:, span(i, P)], packed["t"][i][:, span(g, PASS)])

        def scale_h(i):
            nc.vector.tensor_tensor(
                out=hr_packed[i][:].rearrange("p (g n j) -> p g n j", g=PASSES, j=PLACES),
                in0=packed["h"][i][:].rearrange("p (g n j) -> p g n j", g=PASSES, j=PLACES),
                in1=r_k[:].unsqueeze(2).to_broadcast([P, PASSES, P, PLACES]),
                op=ALU.mult,
            )

        def quantise_hr(i):
            quantise(hr_codes[i][:], hr_scales[i][:], hr_packed[i][:])

        def sigmoid_a(i):
            for u in range(PASSES):
                bank = new_bank("a", i, u)
                for g in range(PASSES):
                    mx(
                        bank[:], g, h_codes[i][:, span(g, P)].bitcast(FP8X4), h_scales[i][:, span(g, P)],
                        w_given[u][:, g, :].bitcast(FP4X4), ws_given[:, span(PASSES * g + u, PASS)],
                    )
                nc.scalar.activation(out=as_sorted(sig["h"][i, u][:]), in_=by_place(bank[:]), func=ACT.Sigmoid)

        def sigmoid_b(i):
            for u in range(PASSES):
                bank = new_bank("b", i, u)
                for j in range(PLACES):
                    for g in range(PASSES):
                        mx(
                            bank[:, span(j, P)], g, w_sorted[u][:, g, span(j, 2 * P)].bitcast(FP4X4),
                            ws_sorted[:, span(PLACES * (PASSES * g + u) + j, P)],
                            t_codes[g][:, span(i, P)].bitcast(FP8X4), t_scales[g][:, span(i, P)],
                        )
                nc.scalar.activation(
                    out=sig["t"][i, u][:].rearrange("p (m j) -> p m j", j=PLACES),
                    in_=bank[:].rearrange("p (j m) -> p m j", j=PLACES),
                    func=ACT.Sigmoid,
                )

        def subtract_y(i):
            for u in range(PASSES):
                nc.vector.tensor_tensor(
                    out=as_sorted(diff[i, u][:]), in0=as_sorted(sig["h"][i, u][:]), in1=by_place(y_rows[i][:, span(u, PASS)]),
                    op=ALU.subtract,
                )

        def negate_y(i):
            for u in range(PASSES):
                nc.scalar.activation(
                    out=as_sorted(y_neg[i, u][:]), in_=by_place(y_rows[i][:, span(u, PASS)]), func=ACT.Copy, scale=-1.0
                )

        def turn_diff(i):
            for u in range(PASSES):
                bank = new_bank("diff", i, u)
                for j in range(PLACES):
                    nc.tensor.transpose(bank[:, span(j, P)], diff[i, u][:, span(j, P)], ident[:])

        def turn_and_subtract(i):
            for u in range(PASSES):
                bank = new_bank("diff", i, u)
                for j in range(PLACES):
                    for term, first in ((y_neg[i, u], True), (sig["h"][i, u], False)):
                        nc.tensor.matmul(
                            bank[:, span(j, P)], lhsT=term[:, span(j, P)], rhs=ident[:], is_transpose=True, start=first, stop=not first
                        )

        def times_vector(out, values, factor):
            nc.vector.tensor_tensor(
                out=out.rearrange("p (n j) -> p n j", j=PLACES), in0=values, in1=factor.unsqueeze(1).to_broadcast([P, P, PLACES]),
                op=ALU.mult,
            )

        def make_ga(i):
            for u in range(PASSES):
                turned = banks["diff", i, u][:].rearrange("p (j n) -> p n j", j=PLACES)
                times_vector(grad["h"][i, u][:], turned, ce_k[:, u, span(0, PLACES)])

        def make_gb(i):
            for u in range(PASSES):
                values = sig["t"][i, u][:].rearrange("p (m j) -> p m j", j=PLACES)
                times_vector(grad["t"][i, u][:], values, ce_k[:, u, span(1, PLACES)])

        def quantise_ga(i):
            for u in range(PASSES):
                quantise(ga_codes[i][:, span(u, P)], ga_scales[i][:, span(u, P)], grad["h"][i, u][:])

        def quantise_gb(i):
            for u in range(PASSES):
                quantise(gb_codes[u][:, span(i, P)], gb_scales[u][:, span(i, P)], grad["t"][i, u][:])

        def gram(name, i, codes, scales, moving_codes, moving_scales):
            bank = new_bank(name, i)
            for g in range(PASSES):
                mx(
                    bank[:], g, codes[i][:, span(g, P)].bitcast(FP8X4), scales[i][:, span(g, P)],
                    moving_codes[g][:].bitcast(FP8X4), moving_scales[g][:],
                )

        def feat_gram(i):
            gram("feat", i, hr_codes, hr_scales, t_codes, t_scales)

        def logit_gram(i):
            gram("logit", i, ga_codes, ga_scales, gb_codes, gb_scales)

        def keep_feat(i):
            nc.scalar.activation(out=feat[i][:], in_=banks["feat", i][:], func=ACT.Copy, scale=LEARNING_RATE)

        def influence(i):
            nc.vector.tensor_tensor(out=infl[i][:], in0=feat[i][:], in1=banks["logit", i][:], op=ALU.mult)
            nc.sync.dma_start(out=out_0[span(i, P), :], in_=infl[i][:])

        def by_pair(ap):
            return ap.rearrange("n (p x z) -> n x p z", x=2, z=2)

        def pairs(i):
            return infl_pairs[i][:].rearrange("n (x p z) -> n x p z", x=2, z=2)

        def round_influence(i, copy):
            copy(out=pairs(i), in_=by_pair(infl[i][:]))

        def rounded_influence(i):
            nc.vector.tensor_tensor(out=pairs(i), in0=by_pair(feat[i][:]), in1=by_pair(banks["logit", i][:]), op=ALU.mult)

        def turn_influence(i):
            bank = new_bank("infl", i)
            words = infl_pairs[i][:].bitcast(F32)
            for pair in range(2):
                nc.tensor.transpose(bank[:, span(pair, P)], words[:, span(pair, P)], ident[:])

        def pack_influence(i):
            nc.scalar.copy(
                out=infl_packed[i][:].bitcast(F32).rearrange("p (n x) -> p n x", x=2),
                in_=banks["infl", i][:, 0 : 2 * P].rearrange("p (x n) -> p n x", x=2),
            )

        def quantise_influence(i):
            quantise(out_codes[:, span(i, P)], out_scales[:, span(i, P)], infl_packed[i][:])

        def store_codes(half):
            words = out_1[0].rearrange("p n j -> p (n j)").bitcast(I32)
            nc.sync.dma_start(out=words[:, span(half, N // 2)], in_=out_codes[:, span(half, N // 2)].bitcast(I32))

        def store_scales():
            for quadrant in range(4):
                queue = (nc.sync, nc.scalar)[quadrant % 2]
                queue.dma_start(
                    out=out_2[0, span(quadrant, 4), :].bitcast(I32),
                    in_=out_scales[32 * quadrant : 32 * quadrant + 4, :].bitcast(I32),
                )

        nc.gpsimd.memset(ws_given[:].bitcast(I32), 0)
        make_identity(nc, ident[:])
        nc.vector.memset(ce_rows[:], 0.0)
        nc.vector.tensor_copy(out=ident_bf[:], in_=ident[:])

        for g in range(PASSES):
            load_rows("h", 0, span(g, PASS))
        load_w_scales()
        load_rows("t", 0)
        for u in range(PASSES):
            load_w(u)
        load_rows("h", 1)
        load_rows("t", 1)
        load_y(0)
        load_vectors()
        load_rows("t", 2)
        load_rows("t", 3)
        load_y(1)
        for i in ON_TENSOR:
            load_rows("h", i)
            load_y(i)

        for g in range(PASSES):
            pack_rows("h", 0, [g], nc.vector.tensor_copy)
        for g in range(PASSES):
            quantise_h_pass(0, g)
        pack_rows("t", 0, copy=nc.vector.tensor_copy)
        sort_w_scales()
        for u in range(PASSES):
            sort_w(u)
        quantise_t(0)
        sigmoid_a(0)

        pack_rows("h", 1)
        pack_rows("t", 1)
        subtract_y(0)
        quantise_h(1)
        scale_h(0)
        quantise_t(1)
        quantise_hr(0)
        sigmoid_b(0)
        turn_vectors()
        sigmoid_a(1)

        turn_diff(0)
        pack_rows("t", 2)
        pack_rows("t", 3)
        make_gb(0)
        subtract_y(1)
        make_ga(0)
        quantise_t(2)
        quantise_t(3)
        quantise_gb(0)
        quantise_ga(0)
        sigmoid_b(1)
        negate_y(2)

        turn_diff(1)
        pack_rows("h", 2)
        pack_rows("h", 3)
        scale_h(1)
        make_gb(1)
        make_ga(1)
        quantise_h(2)
        quantise_h(3)
        quantise_hr(1)
        quantise_gb(1)
        quantise_ga(1)
        sigmoid_b(2)
        negate_y(3)
        sigmoid_b(3)
        scale_h(2)
        make_gb(2)
        quantise_hr(2)
        scale_h(3)
        quantise_gb(2)
        make_gb(3)
        quantise_hr(3)
        quantise_gb(3)
        for i in ON_TENSOR:
            sigmoid_a(i)
        for i in ON_VECTOR:
            feat_gram(i)
            keep_feat(i)

        turn_and_subtract(2)
        make_ga(2)
        turn_and_subtract(3)
        logit_gram(0)
        feat_gram(2)
        keep_feat(2)
        logit_gram(1)
        feat_gram(3)
        quantise_ga(2)
        make_ga(3)
        influence(0)
        round_influence(0, nc.scalar.copy)
        keep_feat(3)
        quantise_ga(3)
        influence(1)
        round_influence(1, nc.scalar.copy)
        logit_gram(2)
        logit_gram(3)

        influence(2)
        turn_influence(0)
        pack_influence(0)
        rounded_influence(3)
        turn_influence(1)
        pack_influence(1)
        round_influence(2, nc.vector.tensor_copy)
        influence(3)
        for i in (3, 2):
            turn_influence(i)
        for i in (3, 2):
            pack_influence(i)
        for half, row_tiles in enumerate(((0, 1), (3, 2))):
            for i in row_tiles:
                quantise_influence(i)
            store_codes(half)
        store_scales()
